import numpy as np, ml_dtypes
CORES = [51,54,179,182]
N = 4
BF = ml_dtypes.bfloat16
W, M, B, T = 2048, 128, 1024, 5
S = (1, 3, 6)
WQ = (2 * np.arange(16) + 1).reshape(1, 1, 16, 1)
def place(l, a):
    return ((l * a >> 5) + l + 37 * a) & (W - 1)
def spot(u):
    return ((u * u >> 5) + 37 * u) & (B - 1)
def fetch(x, l, a):
    return np.take_along_axis(x, place(l, a).reshape(l.shape[:2] + (1, 16 * M)), 3).reshape(l.shape[:2] + (16, 16, M))
def gaps(rec, s):
    return np.add.reduce(np.abs(rec - np.roll(rec, -s, axis=3)), axis=2, dtype=np.int32)
def parts(rng):
    x = rng.integers(0, 256, (N, 8, 16, W)).astype(np.int16); body = rng.integers(0, 4096, (N, 8, 16, B)); l = rng.integers(0, 4096, (N, 8, 16, M))
    many = rng.choice(np.array([1, 2, 2, 3, 4, 6, 8, 8, 12, 16, 16, 16]), (N, 8, 1, M))
    a = np.take_along_axis(rng.integers(0, 4096, (N, 8, 16, M)), (rng.random((N, 8, 16, M)) * many).astype(np.int64), 2)
    c = rng.integers(0, 256, (N, 8, 16, M)); c = np.where(rng.random((N, 8, 1, M)) < 0.3, c & 7, c)
    return x, body, l, a, c, rng.integers(700, 1300, (N, 8, M))
def apart(rng):
    return rng.integers(0, 256, (16, M)) * 16 + np.argsort(rng.random((16, M)), axis=0)
def named(rng, cols):
    l = np.concatenate([np.array(cols), rng.integers(0, 4096, 2 ** 18)]); a = np.concatenate([np.zeros(len(cols), np.int64), rng.integers(0, 4096, 2 ** 18)])
    ix = np.nonzero(np.isin(place(l, a), np.array(cols)))[0]; l, a = l[ix], a[ix]
    ix = np.unique(a, return_index=True)[1]; ix = rng.permutation(ix)
    return l[ix], a[ix]
def uneven(rng, bits, shape):
    return np.minimum(np.exp2(bits * rng.random(shape)).astype(np.int64), 2 ** bits - 1) * (rng.random(shape) > 0.03)
def always(x, body, l, a, c):
    x = x.copy(); row = np.arange(16).reshape(1, 1, 16, 1); first = 16 * np.arange(M).reshape(1, 1, 1, M); d = []
    for t in range(T):
        full = np.ones(l.shape, bool); rec = fetch(x, l, a)
        for s in S:
            ok = full & np.roll(full, -s, axis=2) & (a != np.roll(a, -s, axis=2))
            key = np.where(ok, gaps(rec, s), 2 ** 20)
            k = np.argmin(key, axis=2)[:, :, None, :]; j = (k + s) & 15
            least = np.take_along_axis(key, k, 2); go = least < 2 ** 20; d.append(least[:, :, 0])
            ak, aj = np.take_along_axis(a, k, 2), np.take_along_axis(a, j, 2)
            low = np.minimum(np.take_along_axis(c, k, 2), np.take_along_axis(c, j, 2))
            c = np.where(go & (row == k), low, c); full = full & ~(go & (row == j))
            a = np.where(go & (a == np.maximum(ak, aj)), np.minimum(ak, aj), a)
            rec = fetch(x, l, a)
        k = np.argmax(np.where(full, c, -1), axis=2)[:, :, None, :]
        z = np.take_along_axis(rec, k[:, :, None], 3)[:, :, :, 0]
        top = np.max(np.where(full[:, :, None], rec, np.int16(0)), axis=3)
        u = np.add.reduce(z.astype(np.int64) * WQ, axis=2, keepdims=True) & 4095
        b = np.take_along_axis(body, spot(u), 3); new = ~full | (row == k)
        ak, ck = np.take_along_axis(a, k, 2), np.take_along_axis(c, k, 2) >> 1
        a = np.where(new, np.where((row & 1) == 1, ak, ((b * u >> 5) + t) & 4095), a)
        l = np.where(new, b, l); c = np.where(new, ck, c)
        np.put_along_axis(x, np.broadcast_to(first + (u & 15), l.shape), (z + top) >> 1, 3)
        l, a, c = np.roll(l, 1, axis=0), np.roll(a, 1, axis=0), np.roll(c, 1, axis=0)
    return np.stack(d)
def pack(x, body, l, a, c, t):
    return {"xs": np.ascontiguousarray(x.reshape(N, 128, W)).astype(np.float32).astype(BF), "rb": np.ascontiguousarray(body.reshape(N, 128, B)).astype(np.int32),
            "lt": np.ascontiguousarray(l.reshape(N, 128, M)).astype(np.int32), "ag": np.ascontiguousarray(a.reshape(N, 128, M)).astype(np.int32),
            "cs": np.ascontiguousarray(c.reshape(N, 128, M)).astype(np.int32), "th": np.ascontiguousarray(t).astype(np.int32)}
def setup_inputs(rng):
    return pack(*parts(rng))
def setup_inputs_spread(rng):
    x = np.minimum(np.exp2(8 * rng.random((N, 8, 1, W))) * rng.random((N, 8, 16, W)), 255).astype(np.int16)
    sh = (N, 8, 16, M)
    return pack(x, uneven(rng, 12, (N, 8, 16, B)), uneven(rng, 12, sh), uneven(rng, 12, sh), uneven(rng, 8, sh), uneven(rng, 12, (N, 8, M)))
def setup_inputs_ends(rng):
    sh = (N, 8, 16, M); half = lambda s: (rng.random(s) < 0.5).astype(np.int64)
    x = (255 * (rng.random((N, 8, 16, W)) < rng.choice(np.array([0.0, 0.5, 1.0]), (N, 8, 1, W)))).astype(np.int16)
    body = 4095 * half((N, 8, 16, B)); c = 255 * half(sh); t = 4095 * half((N, 8, M))
    c = np.where(rng.random((N, 8, 1, M)) < 0.1, 255, c)
    alt = rng.random((N, 8, 1, M)) < 0.3; alt[..., 0] = True; alt[..., M - 1] = True; t[..., 0] = 4095; t[..., M - 1] = 4095
    way = ((np.arange(16) // S[0]) & 1).reshape(1, 1, 16, 1)
    l = 4095 * np.where(alt, way, half(sh)); a = 4095 * np.where(alt, way, half(sh))
    top = np.full(16, 255); top[7] = 0; top[0] = 239
    ub = int(np.argmax(spot(np.arange(4096)))); far = np.zeros(16, np.int64); far[15] = ub // 31; far[0] = ub - 31 * (ub // 31)
    put = rng.random((N, 8)) < 0.6; put[:, 7] = True; put[N - 1] = True
    for q in range(N):
        for g in range(8):
            if put[q, g]:
                x[q, g, :, place(0, 0)] = 0; x[q, g, :, place(4095, 4095)] = 255; x[q, g, :, place(4095, 0)] = top; x[q, g, :, place(0, 4095)] = far
                body[q, g, :, spot(4095)] = 4095; body[q, g, :, spot(ub)] = 4095 * (np.arange(16) & 1)
    return pack(x, body, l, a, c, t)
def setup_inputs_corners(rng):
    x, body, l, a, c, t = parts(rng); k = np.arange(16).reshape(16, 1); i = np.arange(M)
    for q in range(N):
        fl, fa = named(rng, [0, W - 1])
        for g in range(8):
            kind = (g + q) & 7
            if kind == 0: t[q, g] = 0
            if kind == 1: a[q, g] = apart(rng); t[q, g] = 4095
            if kind == 2: a[q, g] = rng.choice(np.array([0, 4095, 77, 2048]), (1, M)); t[q, g] = 4095
            if kind == 3:
                if (q & 1) == 0:
                    m = rng.integers(S[0], 16, M); m[M - 1] = 8; t[q, g] = 4095
                    l[q, g, 15, M - 1] = 4095; c[q, g, :, M - 1] = rng.integers(0, 255, 16); c[q, g, 15, M - 1] = 255
                    l[q, g, m, i] = place(l[q, g, (m - S[0]) & 15, i], 4095)
                else:
                    m = rng.integers(0, 16, M); t[q, g] = np.where(rng.random(M) < 0.8, 4095, t[q, g])
                a[q, g] = np.where(k == m.reshape(1, M), 0, 4095)
            if kind == 4: c[q, g] = rng.choice(np.array([0, 1, 254, 255]), (1, M))
            if kind == 5:
                c[q, g] = np.where(k == rng.choice(np.array([0, 7, 8, 15]), (1, M)), 255, rng.choice(np.array([0, 254, 255]), (1, M))); t[q, g] = rng.choice(np.array([0, 4095]), M)
            if kind == 6:
                x[q, g] = 255 * (rng.random((1, W)) < 0.5); t[q, g] = rng.choice(np.array([0, 1, 4080, 4081]), M)
                x[q, g, :, place(0, 4095)] = 0; x[q, g, :, W - 1] = 255
                lone = rng.random(M) < 0.25; lone[0] = True; lone[M - 1] = True; one = k == rng.integers(0, 16, (1, M))
                l[q, g] = np.where(lone, np.where(one, 0, 4095), l[q, g]); a[q, g] = np.where(lone, np.where(one, 4095, 0), a[q, g])
                t[q, g] = np.where(lone, 4080 + (rng.random(M) < 0.3), t[q, g]); t[q, g, 0] = 4081; t[q, g, M - 1] = 4080
            if kind == 7:
                ix = rng.integers(0, len(fl), (16, M)); l[q, g] = fl[ix]; a[q, g] = fa[ix]
    return pack(x, body, l, a, c, t)
def setup_inputs_crowd(rng):
    x, body, l, a, c, t = parts(rng)
    for q in range(N):
        fl, fa = named(rng, [int(rng.integers(0, W))]); one = (int(rng.integers(0, M)), M - 1)
        for g in range(8):
            kind = (g + q) & 7; i = one[int(rng.integers(0, 2))]
            if g in (3, 4): kind = 8
            if kind in (0, 1, 4):
                ix = (rng.integers(0, len(fl), (1, M)) + np.arange(16).reshape(16, 1)) % len(fl); l[q, g] = fl[ix]; a[q, g] = fa[ix]
            if kind == 1: t[q, g] = 1; t[q, g, i] = 0
            if kind in (2, 3, 8): a[q, g] = apart(rng); t[q, g] = 4095
            if kind == 3: a[q, g, :, i] = a[q, g, 0, i]
            if kind == 4: t[q, g] = rng.integers(0, 3, M); c[q, g] = 200
            if kind == 5: a[q, g] = apart(rng); l[q, g] = l[q, g, 0, 0]; c[q, g] = 255
    d = always(x[:, 3:5], body[:, 3:5], l[:, 3:5], a[:, 3:5], c[:, 3:5])
    edge = d[-1] - ((M * (len(S) * T - 1)) & 31)
    t[:, 3:5] = np.where((d[-1] <= 4080) & (np.max(d[:-1], axis=0) < edge), edge, 4095)
    return pack(x, body, l, a, c, t)
def setup_inputs_ties(rng):
    x, body, l, a, c, t = parts(rng); few = rng.integers(0, 256, (N, 4, 16, 4)).astype(np.int16)
    x[:, ::2] = np.take_along_axis(few, rng.integers(0, 4, (N, 4, 1, W)), 3)
    c[:, 1::2] = rng.integers(5, 7, (N, 4, 16, M))
    key = np.where(a != np.roll(a, -S[0], axis=2), gaps(fetch(x, l, a), S[0]), 5000)
    t = np.where(rng.random((N, 8, M)) < 0.6, np.minimum(np.min(key, axis=2) + rng.integers(0, 2, (N, 8, M)), 4095), t)
    return pack(x, body, l, a, c, t)
def check_inputs(d):
    bad = []
    for k, lo, hi in (("xs", 0, 255), ("rb", 0, 4095), ("lt", 0, 4095), ("ag", 0, 4095), ("cs", 0, 255), ("th", 0, 4095)):
        v = np.asarray(d[k]).astype(np.float64)
        if not (np.min(v) >= lo and np.max(v) <= hi): bad.append("range of " + k)
        elif k == "xs" and np.any(v != np.floor(v)): bad.append("whole numbers of xs")
    return bad
def reference(xs, rb, lt, ag, cs, th):
    x = xs.astype(np.float32).astype(np.int16).reshape(N, 8, 16, W); body = rb.astype(np.int32).reshape(N, 8, 16, B)
    l = lt.astype(np.int32).reshape(N, 8, 16, M); a = ag.astype(np.int32).reshape(N, 8, 16, M); c = cs.astype(np.int32).reshape(N, 8, 16, M)
    limit = th.astype(np.int64); made = np.zeros((N, 8), np.int64)
    row = np.arange(16).reshape(1, 1, 16, 1); first = 16 * np.arange(M).reshape(1, 1, 1, M)
    for t in range(T):
        full = np.ones((N, 8, 16, M), bool); rec = fetch(x, l, a)
        for s in S:
            ok = full & np.roll(full, -s, axis=2) & (a != np.roll(a, -s, axis=2))
            key = np.where(ok, gaps(rec, s), 2 ** 20)
            k = np.argmin(key, axis=2)[:, :, None, :]; j = (k + s) & 15
            go = np.take_along_axis(key, k, 2) < (limit + (made & 31)[:, :, None])[:, :, None, :]
            ak, aj = np.take_along_axis(a, k, 2), np.take_along_axis(a, j, 2)
            low = np.minimum(np.take_along_axis(c, k, 2), np.take_along_axis(c, j, 2))
            c = np.where(go & (row == k), low, c); full = full & ~(go & (row == j))
            a = np.where(go & (a == np.maximum(ak, aj)), np.minimum(ak, aj), a)
            made = made + np.add.reduce(go[:, :, 0].astype(np.int64), axis=2)
            rec = fetch(x, l, a)
        k = np.argmax(np.where(full, c, -1), axis=2)[:, :, None, :]
        z = np.take_along_axis(rec, k[:, :, None], 3)[:, :, :, 0]
        top = np.max(np.where(full[:, :, None], rec, np.int16(0)), axis=3)
        u = (np.add.reduce(z.astype(np.int32) * WQ, axis=2, keepdims=True) & 4095).astype(np.int32)
        b = np.take_along_axis(body, spot(u), 3); new = ~full | (row == k)
        ak, ck = np.take_along_axis(a, k, 2), np.take_along_axis(c, k, 2) >> 1
        a = np.where(new, np.where((row & 1) == 1, ak, ((b * u >> 5) + t) & 4095), a)
        l = np.where(new, b, l); c = np.where(new, ck, c)
        np.put_along_axis(x, np.broadcast_to(first + (u & 15), (N, 8, 16, M)), (z + top) >> 1, 3)
        if t < T - 1: l, a, c = np.roll(l, 1, axis=0), np.roll(a, 1, axis=0), np.roll(c, 1, axis=0)
    return {"yl": l.reshape(N, 128, M).astype(np.float32), "ya": a.reshape(N, 128, M).astype(np.float32), "yc": c.reshape(N, 128, M).astype(np.float32), "yx": x.reshape(N, 128, W).astype(np.float32).astype(BF)}

@@ -1,0 +1,629 @@
+from concourse.mybir import dt, AluOpType as OP, AxisListType, ActivationFunctionType as AF
+
+CW = 64
+NCH = 2
+SH = (1, 3, 6)
+VIS = 5
+H = "float16"
+B = "bfloat16"
+F = "float32"
+I = "int32"
+U = "uint16"
+
+GP = (("a", 0, 32), ("a", 32, 64))
+GF = ((("a", 0, 16), ("a", 16, 32), ("a", 32, 48), ("a", 48, 64)),) * 2
+G0 = ((("a", 0, 32), ("a", 32, 48), ("v", 48, 64)),) * 2
+HALVES = ((0, 32), (32, 64))
+CE = ("v", "a")
+ZE = "a"
+LAT = 110.0
+GAM = 1.56
+PEC = 0.5
+
+
+def _scratch():
+    s = {}
+
+    def sb(n, sh, d):
+        s[n] = ("sbuf", [128] + list(sh), d)
+    sb("X", [2064], B); sb("Xo", [2048], B); sb("rbt", [1024], I)
+    sb("lti", [128], I); sb("agi", [128], I); sb("csi", [128], I); sb("thi", [128], I)
+    sb("Fi", [6, 128], I); sb("Fh", [6, 128], H); sb("pi", [16], I); sb("pf", [16], F)
+    sb("mh", [30, 128], H); sb("mb", [6, 128], B)
+    sb("gF", [3, 128], B); sb("gF2", [16], B); sb("I4", [2, 64], B); sb("gs", [24], B)
+    sb("selo", [144], H); sb("selw", [144], B); sb("keepT", [512], B)
+    sb("thR", [3, 128], H); sb("thx", [128], H); sb("rows", [6, 128], H); sb("rowi", [4, 128], I)
+    sb("t32", [8], F); sb("qc", [16], F); sb("modt", [320], B); sb("a31", [64], B); sb("offa", [4], U)
+    sb("cnt", [8], F); sb("tile0", [2, 192], H); sb("lnd", [8, 192], H); sb("snd", [10, 192], H)
+    sb("fin", [6, 64], F); sb("junk", [64], B); sb("qw", [2, 8], I); sb("ow", [8], U)
+    for c in range(NCH):
+        n = str(c)
+        sb("rec" + n, [1024], B); sb("mn" + n, [1024], B); sb("cl" + n, [128], B)
+        sb("Bk" + n, [2, 128], F); sb("ohT" + n, [128], B); sb("hT" + n, [128], B)
+        sb("pm" + n, [256], H); sb("y" + n, [3, 256], H); sb("eq" + n, [64], B)
+        sb("an" + n, [3, 64], H); sb("f" + n, [5, 64], F); sb("i" + n, [4, 64], I); sb("off" + n, [64], U)
+        sb("yq" + n, [2, 64], H); sb("offq" + n, [8], U); sb("z" + n, [64], B); sb("ui" + n, [2, 72], I)
+        sb("q" + n, [4, 4], I); sb("nw" + n, [2, 64], B); sb("av" + n, [64], I)
+        s["pK" + n] = ("psum", [128, 512], F)
+        s["pO" + n] = ("psum", [128, 512], F)
+        s["pU" + n] = ("psum", [128, 8, 64], F)
+        s["pH" + n] = ("psum", [128, 8, 64], F)
+    return s
+
+
+SCRATCH = _scratch()
+NDMA = 24
+SEMAPHORES = ["sv", "sa", "sp", "sg", "loc"] + ["d%d" % k for k in range(NDMA)] + ["arr%d" % k for k in range(8)]
+
+
+def build_ops(g, core, T, topo, rank):
+    ops = []
+    V, A, PE = g.vector, g.scalar, g.tensor
+
+    def op(e, fn, r, w, d, bank=None, kind="c", ext=None):
+        ops.append({"e": e, "fn": fn, "r": list(r), "w": list(w), "d": float(d), "bank": bank, "kind": kind, "ext": ext})
+
+    def vt(n, rate=1.0):
+        return max(64.0, n * rate)
+
+    def ts(out, in0, s1, s2, o0, o1, r, w, n, rate=1.0, bank=None):
+        if o1 is None:
+            op("v", lambda: V.tensor_scalar(out, in0, s1, None, o0), r, w, vt(n, rate), bank)
+        else:
+            op("v", lambda: V.tensor_scalar(out, in0, s1, s2, o0, o1), r, w, vt(n, rate), bank)
+
+    def tt(out, a, b, o, r, w, n, bank=None, d=None):
+        op("v", lambda: V.tensor_tensor(out, a, b, o), r, w, d or vt(n, 1.0 if bank else 2.0), bank)
+
+    def cp(out, a, r, w, n, rate=1.0, bank=None, d=None):
+        op("v", lambda: V.tensor_copy(out, a), r, w, d or vt(n, rate), bank)
+
+    def ms(out, c, w, n, bank=None):
+        op("v", lambda: V.memset(out, c), [], w, vt(n, 0.5), bank)
+
+    def scan(out, a, b, o0, o1, r, w, n, rate, bank=None):
+        op("v", lambda: V.tensor_tensor_scan(out, a, b, 0.0, o0, o1), r, w, vt(n, rate), bank)
+
+    def iota(out, pat, base, cm, w, n, fl=False):
+        if fl:
+            op("g", lambda: g.iota(out, pat, base, cm, allow_small_or_imprecise_dtypes=True), [], w, 160 + 2 * n)
+        else:
+            op("g", lambda: g.iota(out, pat, base, cm), [], w, 160 + 2 * n)
+
+    def mms(bank, lst):
+        keys = []
+        for x in lst:
+            if x[4] not in keys:
+                keys.append(x[4])
+        for k in keys:
+            sub = [x for x in lst if x[4] == k]
+            for j, (o, l, r_, rd, w, cyc) in enumerate(sub):
+                op("p", (lambda o=o, l=l, r_=r_, a=(j == 0), b=(j == len(sub) - 1): PE.matmul(o, l, r_, a, b)), rd, [w], cyc * PEC, bank, "mm")
+
+    def dma(e, out, in_, r, w, d):
+        q = {"s": g.sync, "a": g.scalar, "g": g}[e]
+        op(e, lambda: q.dma_start(out, in_), r, w, d, None, "dma")
+
+    def gather(e, out, win, off, r, w, n):
+        if e == "a":
+            op("a", lambda: A.activation(out, win.indirect(off), AF.Copy), r, w, 80 + GAM * n)
+        else:
+            op("v", lambda: V.tensor_copy(out, win.indirect(off)), r, w, 60 + GAM * n)
+
+    dma("s", T.lti[:], T.lt[:], [], ["lti"], 2400)
+    dma("a", T.agi[:], T.ag[:], [], ["agi"], 2400)
+    dma("s", T.X[:, 0:1024], T.xs[:, 0:1024], [], ["X0"], 3200)
+    dma("a", T.X[:, 1024:2048], T.xs[:, 1024:2048], [], ["X1"], 3200)
+    dma("s", T.csi[:], T.cs[:], [], ["csi"], 3200)
+    dma("s", T.thi[0:8, :], T.th[:], [], ["thi"], 3200)
+    dma("s", T.rbt[:], T.rb[:], [], ["rbt"], 5000)
+    ms(T.X[:, 2048:2064], 0.0, ["Xz"], 16)
+
+    pats = ([[256, 8], [1, 16]], [[256, 8], [3, 16]], [[256, 8], [3, 2], [6, 8]])
+    iota(T.pi[:, 6:7], [[0, 1]], 0, 1, ["pi6"], 1)
+    iota(T.gF[:, 0, :], [[1, 8], [0, 16]], 0, 0, ["gF0"], 128, True)
+    for o in range(3):
+        iota(T.pi[:, 2 * o:2 * o + 2], [[SH[o], 2]], 0, SH[o], ["pi%d" % o], 2)
+    for o in range(3):
+        for sg in range(2):
+            j = 2 * o + sg
+            iota(T.Fi[:, j, :], pats[o], sg * SH[o], 0, ["Fi%d" % j], 128)
+            ts(T.Fi[:, j, :], T.Fi[:, j, :], 0x70F, None, OP.bitwise_and, None, ["Fi%d" % j], ["Fi%d" % j], 128)
+            cp(T.Fh[:, j, :], T.Fi[:, j, :], ["Fi%d" % j], ["Fh%d" % j], 128)
+    iota(T.gF[:, 1, :], [[1, 8], [0, 8], [-100, 2]], 100, 0, ["gF1"], 128, True)
+    iota(T.gF[:, 2, :], [[1, 8], [0, 8], [100, 2]], 0, 0, ["gF2"], 128, True)
+    iota(T.gF2[:, :], [[1, 8], [0, 2]], 0, 0, ["gF2b"], 16, True)
+    iota(T.modt[:, :], [[0, 5], [2, 32], [0, 2]], 0, 0, ["modt"], 320, True)
+    iota(T.qc[:, 0:8], [[0, 2], [256, 4]], 0, 0, ["qc0"], 8, True)
+    iota(T.t32[:, 0:4], [[32, 4]], 32, 0, ["t32a"], 4, True)
+    P = T.pi
+    ts(P[:, 7:8], P[:, 6:7], 4, None, OP.arith_shift_right, None, ["pi6"], ["pi7"], 1)
+    ts(P[:, 8:9], P[:, 6:7], 3, 1, OP.arith_shift_right, OP.bitwise_and, ["pi6"], ["pi8"], 1)
+    ts(P[:, 9:10], P[:, 6:7], 15, None, OP.bitwise_and, None, ["pi6"], ["pi9"], 1)
+    ts(P[:, 10:11], P[:, 6:7], 1, None, OP.bitwise_and, None, ["pi6"], ["pi10"], 1)
+    pf = T.pf
+    cp(pf[:, 6:11], P[:, 6:11], ["pi6", "pi7", "pi8", "pi9", "pi10"], ["pfa"], 5)
+    ts(pf[:, 11:12], pf[:, 7:8], 256.0, None, OP.mult, None, ["pfa"], ["g256"], 1)
+    ts(pf[:, 12:13], pf[:, 8:9], 3.0, None, OP.mult, None, ["pfa"], ["h3"], 1)
+    ts(P[:, 4:6], P[:, 4:6], pf[:, 12:13], None, OP.add, None, ["pi2", "h3"], ["pi2"], 2)
+    for o in range(3):
+        ts(P[:, 2 * o:2 * o + 2], P[:, 2 * o:2 * o + 2], 15, None, OP.bitwise_and, None, ["pi%d" % o], ["pi%d" % o], 2)
+        ts(pf[:, 2 * o:2 * o + 2], P[:, 2 * o:2 * o + 2], pf[:, 11:12], None, OP.add, None, ["pi%d" % o, "g256"], ["pf%d" % o], 2)
+    ts(pf[:, 13:14], pf[:, 9:10], 2.0, 1.0, OP.mult, OP.add, ["pfa"], ["wcol"], 1)
+    ts(pf[:, 14:15], pf[:, 9:10], 16.0, None, OP.mult, None, ["pfa"], ["k16"], 1)
+    ts(pf[:, 15:16], pf[:, 10:11], -1.0, 1.0, OP.mult, OP.add, ["pfa"], ["evc"], 1)
+    ts(T.qc[:, 8:16], T.qc[:, 0:8], pf[:, 14:15], None, OP.add, None, ["qc0", "k16"], ["qc"], 8)
+    ts(T.t32[:, 4:8], T.t32[:, 0:4], pf[:, 15:16], None, OP.mult, None, ["t32a", "evc"], ["t32"], 4)
+    gcol = pf[:, 7:8]
+
+    slots = {"h": [0], "b": [0]}
+    mats = {}
+
+    def slot(name, kind):
+        j = slots[kind][0]; slots[kind][0] += 1
+        mats[name] = (T.mh if kind == "h" else T.mb)[:, j, :]
+        mats[name + "#"] = (T.mh if kind == "h" else T.mb, j)
+        return mats[name]
+
+    def perm(name, kind, a, sa, b, sb_, scale):
+        ts(slot(name, kind), T.Fh[:, 2 * b + sb_, :], pf[:, 2 * a + sa:2 * a + sa + 1], float(scale), OP.is_equal, OP.mult,
+           ["Fh%d" % (2 * b + sb_), "pf%d" % a], [name], 128, 0.5)
+
+    def grp(out, name, src, skey, s2, n, extra=()):
+        ts(out, src, gcol, s2, OP.is_equal, OP.mult, [skey, "pfa"] + list(extra), [name], n, 0.5)
+
+    for a, b in ((0, 0), (0, 1), (0, 2), (1, 2), (2, 0), (1, 0)):
+        perm("P%d%d" % (a, b), "h", a, 0, b, 0, 1)
+    for a, b in ((0, 1), (1, 2), (2, 0)):
+        perm("nP%d%d" % (a, b), "h", a, 0, b, 0, -1)
+    for b in range(3):
+        perm("W0%d" % b, "h", 0, 0, b, 0, 2080)
+        perm("Nx%d" % b, "h", b, 0, b, 1, 1)
+    for a, b in ((0, 0), (0, 1), (0, 2), (1, 2)):
+        nm = "DC%d%d" % (a, b)
+        perm(nm, "h", a, 0, b, 1, 1)
+        tt(mats[nm], mats[nm], mats["P%d%d" % (a, b)], OP.subtract, [nm, "P%d%d" % (a, b)], [nm], 128)
+    for a in range(3):
+        perm("Sx%d" % a, "h", a, 1, 0, 0, -2048)
+    perm("I4k", "b", 0, 0, 0, 0, 4096)
+    perm("I16", "b", 0, 0, 0, 0, 16)
+    grp(slot("G", "h"), "G", T.gF[:, 0, :], "gF0", 1.0, 128)
+    grp(slot("nG", "h"), "nG", T.gF[:, 0, :], "gF0", -1.0, 128)
+    grp(slot("Godd", "h"), "Godd", T.gF[:, 1, :], "gF1", 1.0, 128)
+    perm("BI", "b", 0, 0, 0, 0, 131072)
+    perm("nI4k", "b", 0, 0, 0, 0, -4096)
+    slot("tmp", "h")
+    for a, b in ((0, 1), (0, 2), (1, 2)):
+        nm = "PN%d%d" % (a, b)
+        perm(nm, "h", a, 1, b, 0, 49152)
+        ts(mats["tmp"], T.Fh[:, 2 * b + 1, :], pf[:, 2 * a + 1:2 * a + 2], 49152.0, OP.is_equal, OP.mult,
+           ["Fh%d" % (2 * b + 1), "pf%d" % a], ["tmp"], 128, 0.5)
+        tt(mats[nm], mats[nm], mats["tmp"], OP.max, [nm, "tmp"], [nm], 128)
+    grp(slot("nGb", "b"), "nGb", T.gF[:, 0, :], "gF0", -0.5, 128)
+    grp(slot("Wev", "b"), "Wev", T.gF[:, 2, :], "gF2", pf[:, 13:14], 128, ["wcol"])
+    grp(T.gs[:, 0:8], "G16", T.gF2[:, 0:16:2], "gF2b", 16.0, 8)
+    grp(T.gs[:, 16:24], "Gm32", T.gF2[:, 0:16:2], "gF2b", -32.0, 8)
+    for j in range(2):
+        ts(T.I4[0:64, j, :], T.Fh[0:64, 0, 0:64], pf[0:64, 0:1], None, OP.is_equal, None, ["Fh0", "pf0"], ["I4_%d" % j], 64, 0.5)
+    ms(T.selw[:], 0.0, ["selw"], 144)
+    cp(T.selo[:], T.selw[:], ["selw"], ["selo"], 144, 0.5)
+    grp(T.selo[:, 15:143:16], "selo", T.gF2[:, 0:16:2], "gF2b", 1.0, 8, ["selo"])
+    grp(T.selw[:, 15:143:16], "selw", T.gF2[:, 0:16:2], "gF2b", pf[:, 13:14], 8, ["selw", "wcol"])
+    ms(T.keepT[:], 1.0, ["keepT1"], 512)
+    op("v", lambda: V.memset(T.keepT[:, 0:512:16], 0.0), ["keepT1"], ["keepT"], 64)
+    ms(T.a31[:], 0.0, ["a31"], 64)
+    for c in range(NCH):
+        ts(T["pm%d" % c][:, 192:256], T.gF[:, 0, 0:64], 0.0, 2.0, OP.mult, OP.add, ["gF0"], ["pm1_%d" % c], 64)
+    ts(T.thx[0:96, :], T.gF[0:96, 0, :], 0.0, 1.0, OP.mult, OP.add, ["gF0"], ["thx"], 128, 0.5)
+    ts(T.thx[0:8, :], T.thi[0:8, :], -2048.0, None, OP.add, None, ["thi", "thx"], ["thx"], 128)
+    for o in range(3):
+        k = "thR%d" % o
+        ts(T.thR[0:96, o, :], T.gF[0:96, 0, :], pf[0:96, 6:7], -16.0, OP.is_equal, OP.mult, ["gF0", "pfa"], [k], 128, 0.5)
+        ts(T.rowi[32:33, o, :], T.Fi[32:33, 2 * o, :], 15, None, OP.bitwise_and, None, ["Fi%d" % (2 * o)], ["rowi%d" % o], 128)
+        ts(T.thR[32:33, o, :], T.rowi[32:33, o, :], 0.5, None, OP.add, None, ["rowi%d" % o, k], [k], 128)
+        ts(T.thR[64:65, o, :], T.gF[64:65, 0, :], 0.0, -32768.0, OP.mult, OP.add, ["gF0", k], [k], 128, 0.5)
+    R = T.rows
+    for j, val in ((0, 1.0), (1, 3232.0), (2, -6160.0), (5, -4096.0)):
+        ts(R[0:1, j, :], T.gF[0:1, 0, :], 0.0, val, OP.mult, OP.add, ["gF0"], ["row%d" % j], 128, 0.5)
+    ts(R[0:1, 3, 0:128:2], T.gF[0:1, 0, 0:64], 0.0, -6144.0, OP.mult, OP.add, ["gF0"], ["row3a"], 64)
+    ts(R[0:1, 3, 1:128:2], T.gF[0:1, 0, 0:64], 0.0, -4096.0, OP.mult, OP.add, ["gF0"], ["row3b"], 64)
+    ts(T.rowi[0:1, 3, :], T.Fi[0:1, 0, :], 15, None, OP.bitwise_and, None, ["Fi0"], ["rowi3"], 128)
+    ts(R[0:1, 4, :], T.rowi[0:1, 3, :], -1.0, 15.0, OP.mult, OP.add, ["rowi3"], ["row4"], 128)
+    ones = R[0:1, 0, 0:CW]
+
+    def m64(name):
+        t_, j = mats[name + "#"]
+        return t_[0:64, j, 0:64]
+
+    nxt = T.cores[(rank + 1) % len(T.cores)]
+    rid, pid = topo.addr(nxt, core)
+    mask = topo.mask(core, nxt)
+    pcore = T.cores[(rank - 1) % len(T.cores)]
+    n_in = len(topo.engines(pcore, core))
+    n_out = len(topo.engines(core, nxt))
+    XW = T.X[:, 0:2064]
+    XK = ["X0", "X1", "Xz"]
+
+    def place(c, a_ap, a_key, last):
+        n = str(c); pU = T["pU" + n]; f = T["f" + n]; ib = T["i" + n]; bk = "U" + n
+        tt(f[:, 2, :], pU[:, 3, :], a_ap, OP.mult, [a_key, "Lp" + n], ["v" + n], CW, bk)
+        tt(ib[:, 0, :], pU[:, 4, :], f[:, 2, :], OP.add, ["v" + n, "Wp" + n], ["v2" + n], CW, bk)
+        ts(ib[:, 1, :], ib[:, 0, :], 5, 2047, OP.arith_shift_right, OP.bitwise_and, ["v2" + n], ["pl" + n], CW)
+        if not last:
+            cp(T["off" + n][:, :], ib[:, 1, :], ["pl" + n], ["off" + n], CW)
+
+    def lw(c, b, l_ap, l_key):
+        n = str(c); pU = T["pU" + n]
+        return [(pU[:, 3, :], mats["P0%d" % b], l_ap, ["P0%d" % b, l_key], "Lp" + n, 64),
+                (pU[:, 3, :], R[0:1, 1, :], ones, ["row0", "row1"], "Lp" + n, 64),
+                (pU[:, 4, :], mats["W0%d" % b], l_ap, ["W0%d" % b, l_key], "Wp" + n, 64)]
+
+    def pairs(c, s, a_ap, a_key, c_ap, c_key):
+        n = str(c); pH = T["pH" + n]; pm = T["pm" + n]; y = T["y" + n]; bk = "H" + n
+        lst = [(pH[:, 0, :], mats["Nx%d" % s], a_ap, ["Nx%d" % s, a_key], "as" + n, 64),
+               (pH[:, 1, :], mats["DC0%d" % s], c_ap, ["DC0%d" % s, c_key], "dc" + n, 64)]
+        for r in range(s):
+            lst.append((pH[:, 1, :], mats["DC%d%d" % (r, s)], y[:, r, 128:192], ["DC%d%d" % (r, s), "y%d" % r + n], "dc" + n, 64))
+        mms(bk, lst)
+        tt(T["eq" + n][:, :], pH[:, 0, :], a_ap, OP.is_equal, ["as" + n, a_key], ["eq" + n], CW, bk)
+        tt(pm[:, 0:64], pH[:, 0, :], a_ap, OP.max, ["as" + n, a_key], ["pmx" + n], CW, bk)
+        tt(pm[:, 64:128], pH[:, 0, :], a_ap, OP.min, ["as" + n, a_key], ["pmn" + n], CW, bk)
+        ts(pm[:, 128:192], pH[:, 1, :], 0.0, None, OP.min, None, ["dc" + n], ["pmc" + n], CW, 1.0, bk)
+
+    def pick(c, pieces):
+        n = str(c)
+        keys = []
+        for j, (e, a, b) in enumerate(pieces):
+            k = units("rec" + n, a, b)
+            gather(e, T["rec" + n][:, 16 * a:16 * b], XW, T["off" + n][:, a:b], XK + ["off" + n], k, 16 * (b - a))
+            keys += k
+        return keys
+
+    def units(name, a, b):
+        return ["%s_%d" % (name, j) for j in range(a // 4, b // 4)]
+
+    def tile_of(t, c):
+        if t == 0:
+            return (lambda a, b: T.tile0[:, c, a:b]), "tile0_%d" % c
+        return (lambda a, b: T.lnd[:, 2 * (t - 1) + c, a:b]), "lnd%d_%d" % (t, c)
+
+    def best(c, o):
+        n = str(c); key = T["pK" + n][0:64, 0:128]; Bk = T["Bk" + n]; kk = "key" + n
+        scan(Bk[0:64, 0, :], T.keepT[0:64, 0:128], key, OP.mult, o, [kk, "keepT"], ["Bp" + n], 128, 1.0, "K" + n)
+        scan(Bk[0:64, 1, ::-1], T.keepT[0:64, 0:128], Bk[0:64, 0, ::-1], OP.mult, o, ["Bp" + n, "keepT"], ["Bk" + n], 128, 1.0)
+        tt(T["ohT" + n][0:64, :], key, Bk[0:64, 1, :], OP.is_equal, [kk, "Bk" + n], ["ohT" + n], 128, "K" + n)
+
+    def step(t, s, c):
+        n = str(c); tl, tk = tile_of(t, c)
+        pK = T["pK" + n]; pO = T["pO" + n]; pU = T["pU" + n]
+        rec = T["rec" + n]; mn = T["mn" + n]; cl = T["cl" + n]; y = T["y" + n]; pm = T["pm" + n]
+        f = T["f" + n]; an = T["an" + n]
+        a_ap, a_key = (tl(0, 64), tk) if s == 0 else (an[:, s - 1, :], "an%d" % (s - 1) + n)
+        pick(c, G0[c] if s == 0 else GP)
+        cyc = 16 if s < 2 else 8
+        w_ = 16 // cyc
+        key = pK[0:64, 0:128]
+        kk = "key" + n
+        lst = [(key, T.thx[0:65, 64 * c:64 * c + 64], T.thR[0:65, s, :], ["thx", "thR%d" % s], kk, 128),
+               (key, T["eq" + n][:, :], mats["BI"], ["eq" + n, "BI"], kk, 128)]
+        for r in range(s):
+            lst.append((key, y[:, r, 192:256], mats["PN%d%d" % (r, s)], ["y%d" % r + n, "PN%d%d" % (r, s)], kk, 128))
+        for a, b in HALVES:
+            rk = units("rec" + n, a, b); mk = units("mn" + n, a, b); ck = units("cl" + n, a, b)
+            tt(cl[:, w_ * a:w_ * b], rec[:, 16 * a + cyc - 1:16 * b:cyc], rec[:, 16 * a:16 * b:cyc], OP.min, rk, ck, w_ * (b - a))
+            scan(mn[:, 16 * a:16 * b - 1], rec[:, 16 * a:16 * b - 1], rec[:, 16 * a + 1:16 * b], OP.max, OP.min, rk, mk, 16 * (b - a), 0.5)
+            for k in range(16):
+                pv = (k - 1) % cyc + (k // cyc) * cyc
+                for j in (k, pv):
+                    lst.append((pK[a:b, j:128:16], rec[:, 16 * a + k:16 * b:16], T.gs[:, 0:8], rk + ["G16"], kk, b - a))
+            for k in range(cyc - 1, 16, cyc):
+                lst.append((pK[a:b, k:128:16], cl[:, w_ * a + k // cyc:w_ * b:w_], T.gs[:, 16:24], ck + ["Gm32"], kk, b - a))
+            for k in range(16):
+                if k % cyc != cyc - 1:
+                    lst.append((pK[a:b, k:128:16], mn[:, 16 * a + k:16 * b:16], T.gs[:, 16:24], mk + ["Gm32"], kk, b - a))
+        lst.append((key, T.a31[:, :], mats["nGb"], ["a31", "nGb"], kk, 128))
+        mms("K" + n, lst)
+        ohT = T["ohT" + n]
+        best(c, OP.min)
+        nb = (s + 1) % 3
+        mms("O" + n, [(pO[:, 0:128], ohT[0:64, :], T.I4[0:64, :, :], ["ohT" + n, "I4_0", "I4_1"], "oN" + n, 128)])
+        yk = "yA%d" % s + n
+        tt(y[:, s, 0:128], pO[:, 0:128], pm[:, 0:128], OP.mult, ["oN" + n, "pmx" + n, "pmn" + n], [yk], 128, "O" + n)
+        tt(y[:, s, 128:256], pO[:, 0:128], pm[:, 128:256], OP.mult, ["oN" + n, "pmc" + n, "pm1_" + n], ["y%d" % s + n], 128, "O" + n)
+        pn = "P%d%d" % (s, nb)
+        lst = lw(c, nb, tl(64, 128), tk) + [
+            (pU[:, 2, :], mats[pn], a_ap, [pn, a_key], "aP" + n, 64),
+            (pU[:, 0, :], mats["n" + pn], a_ap, ["n" + pn, a_key], "E" + n, 64),
+            (pU[:, 0, :], mats["G"], y[:, s, 0:64], ["G", yk], "E" + n, 64),
+            (pU[:, 1, :], mats["G"], y[:, s, 64:128], ["G", yk], "DL" + n, 64),
+            (pU[:, 1, :], mats["nG"], y[:, s, 0:64], ["nG", yk], "DL" + n, 64)]
+        bk = "U" + n
+        mms(bk, lst)
+        ts(f[:, 0, :], pU[:, 0, :], 0.0, None, OP.is_equal, None, ["E" + n], ["e" + n], CW, 1.0, bk)
+        tt(f[:, 1, :], pU[:, 1, :], f[:, 0, :], OP.mult, ["DL" + n, "e" + n], ["t" + n], CW, bk)
+        ak = "an%d" % s + n
+        tt(an[:, s, :], pU[:, 2, :], f[:, 1, :], OP.add, ["aP" + n, "t" + n], [ak], CW, bk)
+        place(c, an[:, s, :], ak, s == 2)
+        if s < 2:
+            pairs(c, s + 1, an[:, s, :], ak, tl(128, 192), tk)
+
+    def act(out, in_, fn, bias, scale, r, w, n, bank=None):
+        op("a", lambda: A.activation(out, in_, fn, bias=bias, scale=scale), r, w, 100 + n, bank)
+
+    def count(s):
+        pO = T["pO%d" % (NCH - 1)]; bk = "O%d" % (NCH - 1)
+        mms(bk, [(pO[:, 256:320], mats["G"], T["y%d" % c][:, s, 192:256], ["G", "y%d%d" % (s, c)], "Ac", 64) for c in range(NCH)])
+        e = CE[s == 2]
+        if e == "a":
+            op("a", lambda: A.activation(T.junk[:, :], pO[:, 256:320], AF.Copy, accum_out=T.cnt[:, 0:1]), ["Ac"], ["cnt", "junk"], 200, bk)
+        else:
+            op("v", lambda: V.tensor_reduce(T.cnt[:, 0:1], pO[:, 256:320], AxisListType.X, OP.add), ["Ac"], ["cnt"], 64, bk)
+        ts(T.offa[:, :], T.a31[:, 0:4], T.cnt[:, 0:1], None, OP.add, None, ["a31", "cnt"], ["offa"], 4)
+        gather(e, T.a31[:, :], T.modt[:, 0:320], T.offa[:, 0:4], ["modt", "offa"], ["a31"], 64)
+
+    def refill(t, c):
+        n = str(c); tl, tk = tile_of(t, c)
+        pK = T["pK" + n]; pO = T["pO" + n]; pU = T["pU" + n]; pH = T["pH" + n]
+        y = T["y" + n]; f = T["f" + n]; an = T["an" + n]; ib = T["i" + n]
+        Bk = T["Bk" + n]; ohT = T["ohT" + n]; hT = T["hT" + n]; yq = T["yq" + n]; oq = T["offq" + n]
+        z = T["z" + n]; ui = T["ui" + n]; q = T["q" + n]; nw = T["nw" + n]; av = T["av" + n]
+        a_ap, ak = an[:, 2, :], "an2" + n
+        terms = [(tl(128, 192), tk, "P00"), (y[:, 0, 128:192], "y0" + n, "P00"), (y[:, 1, 128:192], "y1" + n, "P10"),
+                 (y[:, 2, 128:192], "y2" + n, "P20")]
+        emp = [(y[:, r, 192:256], "y%d" % r + n, "Sx%d" % r) for r in range(3)]
+        key = pK[0:64, 0:128]; kk = "key" + n
+        od = [terms[0], terms[1], terms[2], emp[0], emp[1], terms[3], emp[2]]
+        mms("K" + n, [(key, ones, R[0:1, 4, :], ["row0", "row4"], kk, 128)] + [(key, d, mats[mn_], [dk, mn_], kk, 128) for d, dk, mn_ in od])
+        best(c, OP.max)
+        act(hT[0:64, :], Bk[0:64, 1, :], AF.Identity, 128.515625, 1.0 / 32, ["Bk" + n], ["hT" + n], 128)
+        bo = "O" + n
+        mms(bo, [(pO[:, 0:64], ohT[0:64, :], T.I4[0:64, 0, :], ["ohT" + n, "I4_0"], "oN" + n, 64)])
+        tt(yq[:, 0, :], pO[:, 0:64], ib[:, 1, :], OP.mult, ["oN" + n, "pl" + n], ["yq" + n], CW, bo)
+        tt(yq[:, 1, :], pO[:, 0:64], a_ap, OP.mult, ["oN" + n, ak], ["ya" + n], CW, bo)
+        mms(bo, [(pO[:, 320:324], T.selo[:, 15 - r:143 - r], yq[:, 0, r:64:16], ["selo", "yq" + n], "Qp" + n, 64) for r in range(16)])
+        cp(oq[:, 0:4], pO[:, 320:324], ["Qp" + n], ["oz" + n], 4, 1.0, bo)
+        gather(ZE, z[:, :], XW, oq[:, 0:4], XK + ["oz" + n], ["z" + n], 64)
+        mms(bo, [(pO[:, 448:452], T.selw[:, 15 - r:143 - r], z[:, r:64:16], ["selw", "z" + n], "uQ" + n, 64) for r in range(16)]
+            + [(pO[:, 384:448], mats["Wev"], z[:, :], ["Wev", "z" + n], "uP" + n, 64)])
+        cp(ui[:, 0, 0:68], pO[:, 384:452], ["uP" + n, "uQ" + n], ["u0" + n], 68, 1.0, bo)
+        ts(ui[:, 1, 0:68], ui[:, 0, 0:68], 4095, None, OP.bitwise_and, None, ["u0" + n], ["u" + n], 68)
+        uq = ui[:, 1, 64:68]
+        ts(q[:, 0, :], uq, -2048.0, None, OP.add, None, ["u" + n], ["q0" + n], 4)
+        ts(q[:, 1, :], uq, 3232.0, None, OP.add, None, ["u" + n], ["q1" + n], 4)
+        tt(q[:, 2, :], q[:, 0, :], q[:, 1, :], OP.mult, ["q0" + n, "q1" + n], ["q2" + n], 4)
+        ts(q[:, 3, :], q[:, 2, :], 5, 1023, OP.arith_shift_right, OP.bitwise_and, ["q2" + n], ["q3" + n], 4)
+        cp(oq[:, 4:8], q[:, 3, :], ["q3" + n], ["on" + n], 4)
+        bh = "H" + n
+        mms(bh, [(pH[:, 2, :], mats[mn_], d, [dk, mn_], "emp" + n, 64) for d, dk, mn_ in emp])
+        tt(f[:, 3, :], ib[:, 1, :], pH[:, 2, :], OP.subtract, ["pl" + n, "emp" + n], ["pl2" + n], CW, bh)
+        ts(T["off" + n][:, :], f[:, 3, :], 2048.0, None, OP.min, None, ["pl2" + n], ["off" + n], CW)
+        mms(bh, [(pH[:, 3, :], mats[mn_], d, [dk, mn_], "Cn" + n, 64) for d, dk, mn_ in od]
+            + [(pH[:, 3, :], ohT[0:64, :], m64("nI4k"), ["ohT" + n, "nI4k"], "Cn" + n, 64)])
+        so = 2 * t + c; sk = "snd%d" % so
+        sg = nw[:, 0, :]
+        act(sg, pH[:, 3, :], AF.Sign, 8.0, 1.0, ["Cn" + n], ["nw" + n], CW, bh)
+        act(nw[:, 1, :], pH[:, 3, :], AF.Relu, 0.0, 1.0, ["Cn" + n], ["cr" + n], CW, bh)
+        act(f[:, 1, :], sg, AF.Identity, -6144.0, -4096.0, ["nw" + n], ["t" + n], CW)
+        bu = "U" + n
+        mms(bu, [(pU[:, 5, :], mats["P00"], a_ap, ["P00", ak], "P1" + n, 64),
+                 (pU[:, 5, :], R[0:1, 5, :], ones, ["row0", "row5"], "P1" + n, 64),
+                 (pU[:, 7, :], mats["P00"], tl(64, 128), ["P00", tk], "PL" + n, 64),
+                 (pU[:, 7, :], R[0:1, 5, :], ones, ["row0", "row5"], "PL" + n, 64),
+                 (pU[:, 6, :], R[0:1, 3, :], ones, ["row0", "row3a", "row3b"], "P3" + n, 64),
+                 (pU[:, 0, :], R[0:1, 2, :], ones, ["row0", "row2"], "E" + n, 64),
+                 (pU[:, 6, :], mats["Godd"], yq[:, 1, :], ["Godd", "ya" + n], "P3" + n, 64),
+                 (pU[:, 0, :], hT[0:64, :], m64("I16"), ["hT" + n, "I16"], "E" + n, 64),
+                 (pU[:, 0, :], mats["nI4k"], sg, ["nI4k", "nw" + n], "E" + n, 64),
+                 (pU[:, 6, :], mats["nI4k"], sg, ["nI4k", "nw" + n], "P3" + n, 64),
+                 (pU[:, 5, :], mats["I4k"], sg, ["I4k", "nw" + n], "P1" + n, 64),
+                 (pU[:, 7, :], mats["I4k"], sg, ["I4k", "nw" + n], "PL" + n, 64)])
+        tt(T.snd[:, so, 128:192], pU[:, 0, :], nw[:, 1, :], OP.max, ["E" + n, "cr" + n], [sk + "c"], CW, bu)
+        dg = 60 + GAM * 64
+        op("v", lambda: V.tensor_tensor(ib[:, 2, :], T.rbt[:, 0:1024].indirect(oq[:, 4:8]), ui[:, 1, 0:64], OP.mult),
+           ["rbt", "on" + n, "u" + n], ["w" + n], dg)
+        op("v", lambda: V.tensor_tensor(f[:, 2, :], T.rbt[:, 0:1024].indirect(oq[:, 4:8]), f[:, 1, :], OP.add),
+           ["rbt", "on" + n, "t" + n], ["v" + n], dg)
+        if t > 0:
+            ts(ib[:, 2, :], ib[:, 2, :], T.t32[:, 3 + t:4 + t], None, OP.add, None, ["w" + n, "t32"], ["w" + n], CW)
+        ts(ib[:, 3, :], ib[:, 2, :], 5, 4095, OP.arith_shift_right, OP.bitwise_and, ["w" + n], ["x" + n], CW)
+        tt(T.snd[:, so, 64:128], pU[:, 7, :], f[:, 2, :], OP.max, ["PL" + n, "v" + n], [sk + "l"], CW, bu)
+        tt(f[:, 0, :], pU[:, 6, :], ib[:, 3, :], OP.add, ["P3" + n, "x" + n], ["e" + n], CW, bu)
+        tt(T.snd[:, so, 0:64], pU[:, 5, :], f[:, 0, :], OP.max, ["P1" + n, "e" + n], [sk + "a"], CW, bu)
+        if t < VIS - 1:
+            op("g", lambda: g.remote_dma(T.lnd[:, so, :], T.snd[:, so, :], T.sem["arr%d" % so], T.sem.loc, pid, rid, mask),
+               [sk + "a", sk + "l", sk + "c"], ["lnd%d_%d" % (t + 1, c)], 3500, None, "rem", (so, n_in, n_out))
+        else:
+            for j, (dst, a, mul, add, k) in enumerate(((T.yc, 128, 1.0 / 16, 0.0, "c"), (T.yl, 64, 1.0, 2048.0, "l"), (T.ya, 0, 1.0, 2048.0, "a"))):
+                ts(T.fin[:, 3 * c + j, :], T.snd[:, so, a:a + 64], mul, add, OP.mult, OP.add, [sk + k], ["fin%d" % (3 * c + j)], CW)
+                dma("s", dst[:, 64 * c:64 * c + 64], T.fin[:, 3 * c + j, :], ["fin%d" % (3 * c + j)], [], 2400)
+        pick(c, GF[c])
+        rec = T["rec" + n]; mn = T["mn" + n]
+        mk = []
+        for a, b in ((0, 32), (32, 64)):
+            k = units("mn" + n, a, b)
+            scan(mn[:, 16 * a:16 * b], T.keepT[:, :], rec[:, 16 * a:16 * b], OP.mult, OP.max, units("rec" + n, a, b) + ["keepT"], k, 16 * (b - a), 0.5)
+            mk += k
+        mms(bh, [(pH[:, 5, :], mats["BI"], z[:, :], ["BI", "z" + n], "zt" + n, 64),
+                 (pH[:, 5, :], mats["BI"], mn[:, 15:1024:16], ["BI"] + mk, "zt" + n, 64)])
+        ts(av[:, :], pH[:, 5, :], 0.5 / 131072, -0.25, OP.mult, OP.add, ["zt" + n], ["av" + n], CW, 1.0, bh)
+        ts(T.qw[:, 0, 4 * c:4 * c + 4], uq, 15, None, OP.bitwise_and, None, ["u" + n], ["q4" + n], 4)
+        cc = [c] if t == VIS - 1 else list(range(NCH)) if c == NCH - 1 else []
+        if cc:
+            a, b = 4 * cc[0], 4 * cc[-1] + 4
+            tt(T.qw[:, 1, a:b], T.qw[:, 0, a:b], T.qc[:, 8 + a:8 + b], OP.add, ["q4%d" % x for x in cc] + ["qc"], ["q5%d" % x for x in cc], 8)
+            cp(T.ow[:, a:b], T.qw[:, 1, a:b], ["q5%d" % x for x in cc], ["ow%d" % x for x in cc], 8)
+
+    def write(t, c):
+        n = str(c)
+        tab, k = (T.X, "X" + n) if t < VIS - 1 else (T.Xo, "Xo" + n)
+        op("v", lambda: V.tensor_copy(tab[:, 1024 * c:1024 * c + 1024].indirect(T.ow[:, 4 * c:4 * c + 4]), T["av" + n][:, :]),
+           ["ow" + n, "av" + n, k], [k], 60 + 3.8 * 64)
+        if t == VIS - 1:
+            dma("s" if c == 0 else "a", T.yx[:, 1024 * c:1024 * c + 1024], T.Xo[:, 1024 * c:1024 * c + 1024], [k], [], 3000)
+
+    for t in range(VIS):
+        for c in range(NCH):
+            tl, tk = tile_of(t, c)
+            if t == 0:
+                cs_ = slice(64 * c, 64 * c + 64)
+                ts(tl(0, 64), T.agi[:, cs_], -2048.0, None, OP.add, None, ["agi"], [tk + "a"], CW)
+                ts(tl(64, 128), T.lti[:, cs_], -2048.0, None, OP.add, None, ["lti", tk + "a"], [tk + "l"], CW)
+                mms("U%d" % c, lw(c, 0, tl(64, 128), tk + "l"))
+                place(c, tl(0, 64), tk + "a", False)
+                ts(tl(128, 192), T.csi[:, cs_], 16.0, None, OP.mult, None, ["csi", tk + "l", tk + "a"], [tk], CW)
+            else:
+                mms("U%d" % c, lw(c, 0, tl(64, 128), tk))
+                place(c, tl(0, 64), tk, False)
+            pairs(c, 0, tl(0, 64), tk, tl(128, 192), tk)
+        if t == VIS - 1:
+            for c in range(NCH):
+                dma("s", T.Xo[:, 1024 * c:1024 * c + 1024], T.X[:, 1024 * c:1024 * c + 1024], ["X%d" % c], ["Xo%d" % c], 3000)
+        for s in range(3):
+            for c in range(NCH):
+                step(t, s, c)
+            if not (t == VIS - 1 and s == 2):
+                count(s)
+        for c in range(NCH):
+            refill(t, c)
+        for c in range(NCH):
+            write(t, c)
+    return ops
+
+
+def schedule(ops):
+    n = len(ops)
+    lastw = {}; readers = {}; lastb = {}
+    for i, o in enumerate(ops):
+        dep = {}
+        for k in o["r"]:
+            if k in lastw:
+                dep[lastw[k]] = "raw"
+        for k in o["w"]:
+            if k in lastw:
+                dep.setdefault(lastw[k], "ord")
+            for j in readers.get(k, ()):
+                if j != i:
+                    dep.setdefault(j, "ord")
+        if o["bank"]:
+            for e, j in lastb.get(o["bank"], {}).items():
+                dep.setdefault(j, "ord")
+            lastb.setdefault(o["bank"], {})[o["e"]] = i
+        for k in o["r"]:
+            readers.setdefault(k, []).append(i)
+        for k in o["w"]:
+            lastw[k] = i; readers[k] = []
+        o["dep"] = dep
+
+    def waits(i, j):
+        a, b = ops[j], ops[i]
+        return a["e"] != b["e"] or a["kind"] in ("dma", "rem") or ops[i]["dep"][j] == "raw"
+
+    succ = [[] for _ in range(n)]
+    for i, o in enumerate(ops):
+        for j in o["dep"]:
+            succ[j].append(i)
+    pr = [0.0] * n
+    for i in range(n - 1, -1, -1):
+        pr[i] = ops[i]["d"] + max([pr[k] + (LAT if waits(k, i) else 0.0) for k in succ[i]] + [0.0])
+    left = [len(o["dep"]) for o in ops]
+    rdy = [0.0] * n
+    end = [0.0] * n
+    free = {e: 0.0 for e in "vapgs"}
+    cand = {e: [] for e in "vapgs"}
+    for i in range(n):
+        if left[i] == 0:
+            cand[ops[i]["e"]].append(i)
+    order = []
+    while len(order) < n:
+        best = None
+        for e, lst in cand.items():
+            if not lst:
+                continue
+            t0 = max(free[e], min(rdy[i] for i in lst))
+            i = max((k for k in lst if rdy[k] <= t0 + SLACK), key=lambda k: (pr[k], -k))
+            i = max((k for k in lst if rdy[k] <= t0 + max(SLACK, FRAC * ops[i]["d"])), key=lambda k: (pr[k], -k))
+            st = max(t0, rdy[i])
+            if best is None or t0 < best[0]:
+                best = (t0, i, st)
+        _, i, st = best
+        o = ops[i]; e = o["e"]
+        cand[e].remove(i)
+        occ = {"dma": 80.0, "rem": 600.0}.get(o["kind"], o["d"])
+        free[e] = st + occ
+        end[i] = st + o["d"]
+        o["t0"] = st
+        order.append(i)
+        for k in succ[i]:
+            rdy[k] = max(rdy[k], end[i] + LAT if waits(k, i) else st)
+            left[k] -= 1
+            if left[k] == 0:
+                cand[ops[k]["e"]].append(k)
+    pos = {}; cnt = {e: 0 for e in "vapgs"}
+    know = {e: ({x: -1 for x in "vapg"}, set()) for e in "vapgs"}
+    snap = {}
+    for i in order:
+        o = ops[i]; e = o["e"]
+        kc, kd = know[e]
+        need = []
+        ds = sorted((j for j in o["dep"] if waits(i, j)), key=lambda j: -end[j])
+        for j in ds:
+            a = ops[j]
+            if a["kind"] in ("dma", "rem"):
+                if j in kd:
+                    continue
+                kd.add(j)
+            else:
+                if kc[a["e"]] >= pos[j]:
+                    continue
+                kc[a["e"]] = pos[j]
+            need.append(j)
+            if a["kind"] != "rem":
+                sc, sd = snap[j]
+                for x in sc:
+                    kc[x] = max(kc[x], sc[x])
+                kd.update(sd)
+        o["wait"] = need
+        if o["kind"] not in ("dma", "rem"):
+            pos[i] = cnt[e]; cnt[e] += 1
+        snap[i] = (dict(kc), set(kd))
+    return order, max(end)
+
+
+SLACK = 40.0
+FRAC = 0.5
+
+
+def rank_program(g, core, T, topo):
+    rank = T.rank_of(core)
+    if rank is None:
+        return
+    ops = build_ops(g, core, T, topo, rank)
+    order, _ = schedule(ops)
+    Q = {"v": g.vector, "a": g.scalar, "p": g.tensor, "g": g, "s": g.sync}
+    wanted = set()
+    for o in ops:
+        wanted.update(o["wait"])
+    sig = {}; cnt = {e: 0 for e in "vapg"}; nd = [0]; open_d = []; sent = 0
+    for i in order:
+        o = ops[i]; q = Q[o["e"]]
+        for j in o["wait"]:
+            q.wait_ge(sig[j][0], sig[j][1])
+        ins = o["fn"]()
+        if o["kind"] == "dma":
+            s = T.sem["d%d" % nd[0]]; nd[0] += 1
+            ins.then_inc(s, 16)
+            sig[i] = (s, 16)
+            if i not in wanted:
+                open_d.append((o["e"], s))
+        elif o["kind"] == "rem":
+            so, n_in, n_out = o["ext"]
+            sig[i] = (T.sem["arr%d" % so], n_in)
+            sent += n_out
+        elif i in wanted:
+            cnt[o["e"]] += 1
+            s = T.sem["s" + o["e"]]
+            ins.then_inc(s, 1)
+            sig[i] = (s, cnt[o["e"]])
+    g.wait_ge(T.sem.loc, sent)
+    for e, s in open_d:
+        Q[e].wait_ge(s, 16)

@@ -14,11 +14,12 @@ GP = (("a", 0, 32), ("a", 32, 64))
 GF = ((("a", 0, 16), ("a", 16, 32), ("a", 32, 48), ("a", 48, 64)),) * 2
 G0 = ((("a", 0, 32), ("a", 32, 48), ("v", 48, 64)),) * 2
 HALVES = ((0, 32), (32, 64))
+PH = HALVES
 CE = ("v", "a")
 ZE = "a"
-LAT = 110.0
+LAT = 50.0
 GAM = 1.56
-PEC = 0.5
+PEC = 0.4
 
 
 def _scratch():
@@ -29,7 +30,7 @@ def _scratch():
     sb("X", [2064], B); sb("Xo", [2048], B); sb("rbt", [1024], I)
     sb("lti", [128], I); sb("agi", [128], I); sb("csi", [128], I); sb("thi", [128], I)
     sb("Fi", [6, 128], I); sb("Fh", [6, 128], H); sb("pi", [16], I); sb("pf", [16], F)
-    sb("mh", [30, 128], H); sb("mb", [6, 128], B)
+    sb("mh", [30, 128], H); sb("mb", [7, 128], B)
     sb("gF", [3, 128], B); sb("gF2", [16], B); sb("I4", [2, 64], B); sb("gs", [24], B)
     sb("selo", [144], H); sb("selw", [144], B); sb("keepT", [512], B)
     sb("thR", [3, 128], H); sb("thx", [128], H); sb("rows", [6, 128], H); sb("rowi", [4, 128], I)
@@ -39,7 +40,7 @@ def _scratch():
     for c in range(NCH):
         n = str(c)
         sb("rec" + n, [1024], B); sb("mn" + n, [1024], B); sb("cl" + n, [128], B)
-        sb("Bk" + n, [2, 128], F); sb("ohT" + n, [128], B); sb("hT" + n, [128], B)
+        sb("Bk" + n, [3, 128], F); sb("ohT" + n, [128], B); sb("hT" + n, [128], B)
         sb("pm" + n, [256], H); sb("y" + n, [3, 256], H); sb("eq" + n, [64], B)
         sb("an" + n, [3, 64], H); sb("f" + n, [5, 64], F); sb("i" + n, [4, 64], I); sb("off" + n, [64], U)
         sb("yq" + n, [2, 64], H); sb("offq" + n, [8], U); sb("z" + n, [64], B); sb("ui" + n, [2, 72], I)
@@ -312,6 +313,8 @@ def build_ops(g, core, T, topo, rank):
             rk = units("rec" + n, a, b); mk = units("mn" + n, a, b); ck = units("cl" + n, a, b)
             tt(cl[:, w_ * a:w_ * b], rec[:, 16 * a + cyc - 1:16 * b:cyc], rec[:, 16 * a:16 * b:cyc], OP.min, rk, ck, w_ * (b - a))
             scan(mn[:, 16 * a:16 * b - 1], rec[:, 16 * a:16 * b - 1], rec[:, 16 * a + 1:16 * b], OP.max, OP.min, rk, mk, 16 * (b - a), 0.5)
+        for a, b in PH:
+            rk = units("rec" + n, a, b); mk = units("mn" + n, a, b); ck = units("cl" + n, a, b)
             for k in range(16):
                 pv = (k - 1) % cyc + (k // cyc) * cyc
                 for j in (k, pv):
@@ -500,10 +503,10 @@ def schedule(ops):
                 dep[lastw[k]] = "raw"
         for k in o["w"]:
             if k in lastw:
-                dep.setdefault(lastw[k], "ord")
+                dep.setdefault(lastw[k], "ord" if o["kind"] == "mm" else "raw")
             for j in readers.get(k, ()):
                 if j != i:
-                    dep.setdefault(j, "ord")
+                    dep.setdefault(j, "raw")
         if o["bank"]:
             for e, j in lastb.get(o["bank"], {}).items():
                 dep.setdefault(j, "ord")
@@ -523,8 +526,16 @@ def schedule(ops):
         for j in o["dep"]:
             succ[j].append(i)
     pr = [0.0] * n
+    for o in ops:
+        o["d0"] = o["d"]
+        if o["kind"] in ("c", "mm"):
+            o["d"] = o["d"] * FAC + (FIX if o["kind"] == "c" else PFIX)
+
+    def lat(k, i):
+        return LATS if ops[k]["e"] == ops[i]["e"] else LAT
+
     for i in range(n - 1, -1, -1):
-        pr[i] = ops[i]["d"] + max([pr[k] + (LAT if waits(k, i) else 0.0) for k in succ[i]] + [0.0])
+        pr[i] = ops[i]["d"] + max([pr[k] + (lat(k, i) if waits(k, i) else 0.0) for k in succ[i]] + [0.0])
     left = [len(o["dep"]) for o in ops]
     rdy = [0.0] * n
     end = [0.0] * n
@@ -554,7 +565,7 @@ def schedule(ops):
         o["t0"] = st
         order.append(i)
         for k in succ[i]:
-            rdy[k] = max(rdy[k], end[i] + LAT if waits(k, i) else st)
+            rdy[k] = max(rdy[k], end[i] + lat(k, i) if waits(k, i) else st)
             left[k] -= 1
             if left[k] == 0:
                 cand[ops[k]["e"]].append(k)
@@ -589,8 +600,12 @@ def schedule(ops):
     return order, max(end)
 
 
-SLACK = 40.0
-FRAC = 0.5
+SLACK = 50.0
+FRAC = 0.3
+LATS = 200.0
+FAC = 1.25
+FIX = 20.0
+PFIX = 5.0
 
 
 def rank_program(g, core, T, topo):

@@ -9,17 +9,22 @@ B = "bfloat16"
 F = "float32"
 I = "int32"
 U = "uint16"
+RND = 12582912.0
 
-GP = (("a", 0, 32), ("a", 32, 64))
-GF = ((("a", 0, 16), ("a", 16, 32), ("a", 32, 48), ("a", 48, 64)),) * 2
-G0 = ((("a", 0, 32), ("a", 32, 48), ("v", 48, 64)),) * 2
-HALVES = ((0, 32), (32, 64))
-PH = HALVES
-CE = ("v", "a")
-ZE = "a"
-LAT = 50.0
-GAM = 1.56
-PEC = 0.4
+CFG = {
+    "GP": (("a", 0, 32), ("a", 32, 64)),
+    "G0": (("a", 0, 32), ("a", 32, 64)),
+    "GF": (("a", 0, 32), ("a", 32, 64)),
+    "SP": ((0, 32), (32, 64)),
+    "CP": ((0, 32), (32, 64)),
+    "ZE": "v",
+    "LAT": 250.0, "FAC": 1.1, "GAM": 1.56, "PEC": 0.5, "SLACK": 60.0, "FRAC": 0.3, "REM": 3000.0,
+}
+PH = ((0, 32), (32, 64))
+
+
+def row_of(s, p):
+    return ((6 * (p & 7) + 3 * (p >> 3)) if s == 2 else SH[s] * p) & 15
 
 
 def _scratch():
@@ -29,37 +34,42 @@ def _scratch():
         s[n] = ("sbuf", [128] + list(sh), d)
     sb("X", [2064], B); sb("Xo", [2048], B); sb("rbt", [1024], I)
     sb("lti", [128], I); sb("agi", [128], I); sb("csi", [128], I); sb("thi", [128], I)
-    sb("Fi", [6, 128], I); sb("Fh", [6, 128], H); sb("pi", [16], I); sb("pf", [16], F)
-    sb("mh", [30, 128], H); sb("mb", [7, 128], B)
-    sb("gF", [3, 128], B); sb("gF2", [16], B); sb("I4", [2, 64], B); sb("gs", [24], B)
-    sb("selo", [144], H); sb("selw", [144], B); sb("keepT", [512], B)
-    sb("thR", [3, 128], H); sb("thx", [128], H); sb("rows", [6, 128], H); sb("rowi", [4, 128], I)
-    sb("t32", [8], F); sb("qc", [16], F); sb("modt", [320], B); sb("a31", [64], B); sb("offa", [4], U)
-    sb("cnt", [8], F); sb("tile0", [2, 192], H); sb("lnd", [8, 192], H); sb("snd", [10, 192], H)
-    sb("fin", [6, 64], F); sb("junk", [64], B); sb("qw", [2, 8], I); sb("ow", [8], U)
+    sb("Fi", [2, 128], I); sb("Fh", [2, 128], H); sb("pi", [28], I); sb("pf", [36], F)
+    sb("mh", [30, 128], H); sb("mb", [6, 128], B); sb("IB", [192], B)
+    sb("tab", [5, 128], B); sb("gF2", [16], B); sb("gs", [24], B)
+    sb("selw", [144], B); sb("keepT", [512], B); sb("edge", [2, 128], B); sb("rs2", [128], B)
+    sb("c33", [128], B); sb("cR", [1024], B); sb("cev", [128], B); sb("mk", [64], H)
+    sb("thR", [128], H); sb("thf", [128], F); sb("thx", [128], H)
+    sb("t32", [8], F); sb("qc", [16], F); sb("a31", [8], B); sb("dc", [8], F); sb("du", [32], F)
+    sb("tile0", [2, 192], H); sb("lnd", [8, 192], H); sb("snd", [10, 192], H)
+    sb("lno", [8, 64], U); sb("sno", [8, 64], U)
+    sb("fin", [6, 64], F); sb("qw", [2, 8], I); sb("ow", [8], U)
     for c in range(NCH):
         n = str(c)
         sb("rec" + n, [1024], B); sb("mn" + n, [1024], B); sb("cl" + n, [128], B)
-        sb("Bk" + n, [3, 128], F); sb("ohT" + n, [128], B); sb("hT" + n, [128], B)
-        sb("pm" + n, [256], H); sb("y" + n, [3, 256], H); sb("eq" + n, [64], B)
-        sb("an" + n, [3, 64], H); sb("f" + n, [5, 64], F); sb("i" + n, [4, 64], I); sb("off" + n, [64], U)
-        sb("yq" + n, [2, 64], H); sb("offq" + n, [8], U); sb("z" + n, [64], B); sb("ui" + n, [2, 72], I)
-        sb("q" + n, [4, 4], I); sb("nw" + n, [2, 64], B); sb("av" + n, [64], I)
+        sb("Bk" + n, [2, 128], F); sb("ohT" + n, [128], B); sb("oh2" + n, [128], B); sb("hT" + n, [128], B)
+        sb("hi" + n, [128], H); sb("y" + n, [3, 192], H); sb("eq" + n, [64], B)
+        sb("d3" + n, [576], F); sb("d4" + n, [256], I); sb("so" + n, [256], I); sb("an" + n, [64], H)
+        sb("f" + n, [5, 64], F); sb("i" + n, [4, 64], I); sb("off" + n, [64], U)
+        sb("yq" + n, [2, 64], H); sb("offq" + n, [8], U); sb("z" + n, [64], B)
+        sb("q" + n, [4, 4], I); sb("r5" + n, [32], F); sb("nw" + n, [2, 64], B); sb("av" + n, [64], I)
         s["pK" + n] = ("psum", [128, 512], F)
         s["pO" + n] = ("psum", [128, 512], F)
-        s["pU" + n] = ("psum", [128, 8, 64], F)
-        s["pH" + n] = ("psum", [128, 8, 64], F)
+        s["pU" + n] = ("psum", [128, 512], F)
+        s["pH" + n] = ("psum", [128, 512], F)
     return s
 
 
 SCRATCH = _scratch()
 NDMA = 24
-SEMAPHORES = ["sv", "sa", "sp", "sg", "loc"] + ["d%d" % k for k in range(NDMA)] + ["arr%d" % k for k in range(8)]
+SEMAPHORES = (["sv", "sa", "sp", "sg", "loc"] + ["d%d" % k for k in range(NDMA)]
+              + ["aro%d" % k for k in range(8)] + ["art%d" % k for k in range(8)])
 
 
 def build_ops(g, core, T, topo, rank):
     ops = []
     V, A, PE = g.vector, g.scalar, g.tensor
+    GAM = CFG["GAM"]
 
     def op(e, fn, r, w, d, bank=None, kind="c", ext=None):
         ops.append({"e": e, "fn": fn, "r": list(r), "w": list(w), "d": float(d), "bank": bank, "kind": kind, "ext": ext})
@@ -76,14 +86,23 @@ def build_ops(g, core, T, topo, rank):
     def tt(out, a, b, o, r, w, n, bank=None, d=None):
         op("v", lambda: V.tensor_tensor(out, a, b, o), r, w, d or vt(n, 1.0 if bank else 2.0), bank)
 
-    def cp(out, a, r, w, n, rate=1.0, bank=None, d=None):
-        op("v", lambda: V.tensor_copy(out, a), r, w, d or vt(n, rate), bank)
+    def cp(out, a, r, w, n, rate=1.0, bank=None):
+        op("v", lambda: V.tensor_copy(out, a), r, w, vt(n, rate), bank)
 
-    def ms(out, c, w, n, bank=None):
-        op("v", lambda: V.memset(out, c), [], w, vt(n, 0.5), bank)
+    def ms(out, c, w, n, bank=None, r=()):
+        op("v", lambda: V.memset(out, c), r, w, vt(n, 1.0), bank)
 
-    def scan(out, a, b, o0, o1, r, w, n, rate, bank=None):
+    def scan(out, a, b, o0, o1, r, w, n, rate=1.0, bank=None):
         op("v", lambda: V.tensor_tensor_scan(out, a, b, 0.0, o0, o1), r, w, vt(n, rate), bank)
+
+    def bits(out, in0, sh, mask, r, w, n):
+        if sh:
+            ts(out, in0, sh, mask, OP.arith_shift_right, OP.bitwise_and, r, w, n)
+        else:
+            ts(out, in0, mask, None, OP.bitwise_and, None, r, w, n)
+
+    def act(out, in_, fn, bias, scale, r, w, n, bank=None):
+        op("a", lambda: A.activation(out, in_, fn, bias=bias, scale=scale), r, w, 80 + n, bank)
 
     def iota(out, pat, base, cm, w, n, fl=False):
         if fl:
@@ -91,18 +110,21 @@ def build_ops(g, core, T, topo, rank):
         else:
             op("g", lambda: g.iota(out, pat, base, cm), [], w, 160 + 2 * n)
 
-    def mms(bank, lst):
-        keys = []
-        for x in lst:
-            if x[4] not in keys:
-                keys.append(x[4])
-        for k in keys:
-            sub = [x for x in lst if x[4] == k]
-            for j, (o, l, r_, rd, w, cyc) in enumerate(sub):
-                op("p", (lambda o=o, l=l, r_=r_, a=(j == 0), b=(j == len(sub) - 1): PE.matmul(o, l, r_, a, b)), rd, [w], cyc * PEC, bank, "mm")
+    def group(bank, key, runs):
+        runs = [x for x in runs if x]
+        for j, run in enumerate(runs):
+            def fn(run=run, a=(j == 0), b=(j == len(runs) - 1)):
+                ins = None
+                for k, (o, l, r_, rd, cyc) in enumerate(run):
+                    ins = PE.matmul(o, l, r_, a and k == 0, b and k == len(run) - 1)
+                return ins
+            rd = []
+            for x in run:
+                rd += [k for k in x[3] if k not in rd]
+            op("p", fn, rd, [key], sum(x[4] for x in run) * CFG["PEC"], bank, "mm")
 
     def dma(e, out, in_, r, w, d):
-        q = {"s": g.sync, "a": g.scalar, "g": g}[e]
+        q = {"s": g.sync, "a": g.scalar}[e]
         op(e, lambda: q.dma_start(out, in_), r, w, d, None, "dma")
 
     def gather(e, out, win, off, r, w, n):
@@ -120,42 +142,42 @@ def build_ops(g, core, T, topo, rank):
     dma("s", T.rbt[:], T.rb[:], [], ["rbt"], 5000)
     ms(T.X[:, 2048:2064], 0.0, ["Xz"], 16)
 
-    pats = ([[256, 8], [1, 16]], [[256, 8], [3, 16]], [[256, 8], [3, 2], [6, 8]])
-    iota(T.pi[:, 6:7], [[0, 1]], 0, 1, ["pi6"], 1)
-    iota(T.gF[:, 0, :], [[1, 8], [0, 16]], 0, 0, ["gF0"], 128, True)
-    for o in range(3):
-        iota(T.pi[:, 2 * o:2 * o + 2], [[SH[o], 2]], 0, SH[o], ["pi%d" % o], 2)
-    for o in range(3):
-        for sg in range(2):
-            j = 2 * o + sg
-            iota(T.Fi[:, j, :], pats[o], sg * SH[o], 0, ["Fi%d" % j], 128)
-            ts(T.Fi[:, j, :], T.Fi[:, j, :], 0x70F, None, OP.bitwise_and, None, ["Fi%d" % j], ["Fi%d" % j], 128)
-            cp(T.Fh[:, j, :], T.Fi[:, j, :], ["Fi%d" % j], ["Fh%d" % j], 128)
-    iota(T.gF[:, 1, :], [[1, 8], [0, 8], [-100, 2]], 100, 0, ["gF1"], 128, True)
-    iota(T.gF[:, 2, :], [[1, 8], [0, 8], [100, 2]], 0, 0, ["gF2"], 128, True)
+    P = T.pi; pf = T.pf; tab = T.tab
+    iota(P[:, 0:16], [[1, 16]], 0, 1, ["pa"], 16)
+    iota(tab[:, 0, :], [[1, 128]], 0, 0, ["h0"], 128, True)
+    iota(tab[:, 1, :], [[1, 8], [0, 16]], 0, 0, ["gF0"], 128, True)
     iota(T.gF2[:, :], [[1, 8], [0, 2]], 0, 0, ["gF2b"], 16, True)
-    iota(T.modt[:, :], [[0, 5], [2, 32], [0, 2]], 0, 0, ["modt"], 320, True)
+    iota(tab[:, 2, :], [[0, 8], [1, 16]], 0, 0, ["kk"], 128, True)
+    iota(P[:, 16:18], [[-3, 2]], 48, 3, ["pb"], 2)
+    iota(P[:, 18:20], [[-6, 2]], 48, 6, ["pc"], 2)
+    for o, pat in ((1, [[256, 8], [3, 16]]), (2, [[256, 8], [3, 2], [6, 8]])):
+        iota(T.Fi[:, o - 1, :], pat, 0, 0, ["Fi%d" % o], 128)
+        bits(T.Fi[:, o - 1, :], T.Fi[:, o - 1, :], 0, 0x70F, ["Fi%d" % o], ["Fi%d" % o], 128)
+        cp(T.Fh[:, o - 1, :], T.Fi[:, o - 1, :], ["Fi%d" % o], ["Fh%d" % o], 128)
+    iota(tab[:, 3, :], [[1, 8], [0, 8], [-100, 2]], 100, 0, ["gF1"], 128, True)
+    iota(tab[:, 4, :], [[1, 8], [0, 8], [100, 2]], 0, 0, ["gF2"], 128, True)
     iota(T.qc[:, 0:8], [[0, 2], [256, 4]], 0, 0, ["qc0"], 8, True)
     iota(T.t32[:, 0:4], [[32, 4]], 32, 0, ["t32a"], 4, True)
-    P = T.pi
-    ts(P[:, 7:8], P[:, 6:7], 4, None, OP.arith_shift_right, None, ["pi6"], ["pi7"], 1)
-    ts(P[:, 8:9], P[:, 6:7], 3, 1, OP.arith_shift_right, OP.bitwise_and, ["pi6"], ["pi8"], 1)
-    ts(P[:, 9:10], P[:, 6:7], 15, None, OP.bitwise_and, None, ["pi6"], ["pi9"], 1)
-    ts(P[:, 10:11], P[:, 6:7], 1, None, OP.bitwise_and, None, ["pi6"], ["pi10"], 1)
-    pf = T.pf
-    cp(pf[:, 6:11], P[:, 6:11], ["pi6", "pi7", "pi8", "pi9", "pi10"], ["pfa"], 5)
-    ts(pf[:, 11:12], pf[:, 7:8], 256.0, None, OP.mult, None, ["pfa"], ["g256"], 1)
-    ts(pf[:, 12:13], pf[:, 8:9], 3.0, None, OP.mult, None, ["pfa"], ["h3"], 1)
-    ts(P[:, 4:6], P[:, 4:6], pf[:, 12:13], None, OP.add, None, ["pi2", "h3"], ["pi2"], 2)
-    for o in range(3):
-        ts(P[:, 2 * o:2 * o + 2], P[:, 2 * o:2 * o + 2], 15, None, OP.bitwise_and, None, ["pi%d" % o], ["pi%d" % o], 2)
-        ts(pf[:, 2 * o:2 * o + 2], P[:, 2 * o:2 * o + 2], pf[:, 11:12], None, OP.add, None, ["pi%d" % o, "g256"], ["pf%d" % o], 2)
-    ts(pf[:, 13:14], pf[:, 9:10], 2.0, 1.0, OP.mult, OP.add, ["pfa"], ["wcol"], 1)
-    ts(pf[:, 14:15], pf[:, 9:10], 16.0, None, OP.mult, None, ["pfa"], ["k16"], 1)
-    ts(pf[:, 15:16], pf[:, 10:11], -1.0, 1.0, OP.mult, OP.add, ["pfa"], ["evc"], 1)
-    ts(T.qc[:, 8:16], T.qc[:, 0:8], pf[:, 14:15], None, OP.add, None, ["qc0", "k16"], ["qc"], 8)
-    ts(T.t32[:, 4:8], T.t32[:, 0:4], pf[:, 15:16], None, OP.mult, None, ["t32a", "evc"], ["t32"], 4)
-    gcol = pf[:, 7:8]
+    cp(pf[:, 20:21], P[:, 0:1], ["pa"], ["pcol"], 1)
+    bits(P[:, 21:22], P[:, 0:1], 4, 7, ["pa"], ["p21"], 1)
+    bits(P[:, 22:23], P[:, 0:1], 3, 1, ["pa"], ["p22"], 1)
+    bits(P[:, 23:24], P[:, 0:1], 0, 1, ["pa"], ["p23"], 1)
+    bits(P[:, 24:25], P[:, 0:1], 0, 0x70, ["pa"], ["p24"], 1)
+    bits(P[:, 25:26], P[:, 0:1], 0, 15, ["pa"], ["p25"], 1)
+    cp(pf[:, 21:26], P[:, 21:26], ["p21", "p22", "p23", "p24", "p25"], ["pfa"], 5)
+    pcol, gcol, g16, kcol = pf[:, 20:21], pf[:, 21:22], pf[:, 24:25], pf[:, 25:26]
+    bits(P[:, 0:16], P[:, 0:16], 0, 15, ["pa"], ["pa", "pa2"], 16)
+    ts(pf[:, 0:16], P[:, 0:16], g16, None, OP.add, None, ["pa2", "pfa"], ["shf"], 16)
+    ts(pf[:, 26:27], pf[:, 22:23], 3.0, None, OP.mult, None, ["pfa"], ["h3"], 1)
+    ts(P[:, 18:20], P[:, 18:20], pf[:, 26:27], None, OP.add, None, ["pc", "h3"], ["pc"], 2)
+    bits(P[:, 16:20], P[:, 16:20], 0, 15, ["pb", "pc"], ["pb2"], 4)
+    ts(pf[:, 16:20], P[:, 16:20], g16, None, OP.add, None, ["pb2", "pfa"], ["shr"], 4)
+    ts(pf[:, 27:28], gcol, 256.0, kcol, OP.mult, OP.add, ["pfa"], ["p256"], 1)
+    ts(pf[:, 28:29], kcol, 2.0, 1.0, OP.mult, OP.add, ["pfa"], ["wcol"], 1)
+    ts(pf[:, 29:30], kcol, 16.0, None, OP.mult, None, ["pfa"], ["k16"], 1)
+    ts(pf[:, 30:31], pf[:, 23:24], -1.0, 1.0, OP.mult, OP.add, ["pfa"], ["evc"], 1)
+    ts(T.qc[:, 8:16], T.qc[:, 0:8], pf[:, 29:30], None, OP.add, None, ["qc0", "k16"], ["qc"], 8)
+    ts(T.t32[:, 4:8], T.t32[:, 0:4], pf[:, 30:31], None, OP.mult, None, ["t32a", "evc"], ["t32"], 4)
 
     slots = {"h": [0], "b": [0]}
     mats = {}
@@ -163,78 +185,102 @@ def build_ops(g, core, T, topo, rank):
     def slot(name, kind):
         j = slots[kind][0]; slots[kind][0] += 1
         mats[name] = (T.mh if kind == "h" else T.mb)[:, j, :]
-        mats[name + "#"] = (T.mh if kind == "h" else T.mb, j)
+        mats[name + "64"] = (T.mh if kind == "h" else T.mb)[0:64, j, 0:64]
+        mats[name + "8"] = (T.mh if kind == "h" else T.mb)[0:8, j, 0:8]
         return mats[name]
 
-    def perm(name, kind, a, sa, b, sb_, scale):
-        ts(slot(name, kind), T.Fh[:, 2 * b + sb_, :], pf[:, 2 * a + sa:2 * a + sa + 1], float(scale), OP.is_equal, OP.mult,
-           ["Fh%d" % (2 * b + sb_), "pf%d" % a], [name], 128, 0.5)
+    def pick1(name, kind, table, tkey, col, ckey, scale):
+        ts(slot(name, kind), table, col, scale, OP.is_equal, OP.mult, [tkey, ckey], [name], 128, 0.5)
 
-    def grp(out, name, src, skey, s2, n, extra=()):
-        ts(out, src, gcol, s2, OP.is_equal, OP.mult, [skey, "pfa"] + list(extra), [name], n, 0.5)
+    def shift(name, j, scale):
+        pick1(name, "h", tab[:, 0, :], "h0", pf[:, j & 15:(j & 15) + 1], "shf", scale)
 
-    for a, b in ((0, 0), (0, 1), (0, 2), (1, 2), (2, 0), (1, 0)):
-        perm("P%d%d" % (a, b), "h", a, 0, b, 0, 1)
-    for a, b in ((0, 1), (1, 2), (2, 0)):
-        perm("nP%d%d" % (a, b), "h", a, 0, b, 0, -1)
-    for b in range(3):
-        perm("W0%d" % b, "h", 0, 0, b, 0, 2080)
-        perm("Nx%d" % b, "h", b, 0, b, 1, 1)
-    for a, b in ((0, 0), (0, 1), (0, 2), (1, 2)):
-        nm = "DC%d%d" % (a, b)
-        perm(nm, "h", a, 0, b, 1, 1)
-        tt(mats[nm], mats[nm], mats["P%d%d" % (a, b)], OP.subtract, [nm, "P%d%d" % (a, b)], [nm], 128)
-    for a in range(3):
-        perm("Sx%d" % a, "h", a, 1, 0, 0, -2048)
-    perm("I4k", "b", 0, 0, 0, 0, 4096)
-    perm("I16", "b", 0, 0, 0, 0, 16)
-    grp(slot("G", "h"), "G", T.gF[:, 0, :], "gF0", 1.0, 128)
-    grp(slot("nG", "h"), "nG", T.gF[:, 0, :], "gF0", -1.0, 128)
-    grp(slot("Godd", "h"), "Godd", T.gF[:, 1, :], "gF1", 1.0, 128)
-    perm("BI", "b", 0, 0, 0, 0, 131072)
-    perm("nI4k", "b", 0, 0, 0, 0, -4096)
-    slot("tmp", "h")
-    for a, b in ((0, 1), (0, 2), (1, 2)):
-        nm = "PN%d%d" % (a, b)
-        perm(nm, "h", a, 1, b, 0, 49152)
-        ts(mats["tmp"], T.Fh[:, 2 * b + 1, :], pf[:, 2 * a + 1:2 * a + 2], 49152.0, OP.is_equal, OP.mult,
-           ["Fh%d" % (2 * b + 1), "pf%d" % a], ["tmp"], 128, 0.5)
-        tt(mats[nm], mats[nm], mats["tmp"], OP.max, [nm, "tmp"], [nm], 128)
-    grp(slot("nGb", "b"), "nGb", T.gF[:, 0, :], "gF0", -0.5, 128)
-    grp(slot("Wev", "b"), "Wev", T.gF[:, 2, :], "gF2", pf[:, 13:14], 128, ["wcol"])
-    grp(T.gs[:, 0:8], "G16", T.gF2[:, 0:16:2], "gF2b", 16.0, 8)
-    grp(T.gs[:, 16:24], "Gm32", T.gF2[:, 0:16:2], "gF2b", -32.0, 8)
-    for j in range(2):
-        ts(T.I4[0:64, j, :], T.Fh[0:64, 0, 0:64], pf[0:64, 0:1], None, OP.is_equal, None, ["Fh0", "pf0"], ["I4_%d" % j], 64, 0.5)
-    ms(T.selw[:], 0.0, ["selw"], 144)
-    cp(T.selo[:], T.selw[:], ["selw"], ["selo"], 144, 0.5)
-    grp(T.selo[:, 15:143:16], "selo", T.gF2[:, 0:16:2], "gF2b", 1.0, 8, ["selo"])
-    grp(T.selw[:, 15:143:16], "selw", T.gF2[:, 0:16:2], "gF2b", pf[:, 13:14], 8, ["selw", "wcol"])
-    ms(T.keepT[:], 1.0, ["keepT1"], 512)
-    op("v", lambda: V.memset(T.keepT[:, 0:512:16], 0.0), ["keepT1"], ["keepT"], 64)
-    ms(T.a31[:], 0.0, ["a31"], 64)
+    pick1("I", "h", tab[:, 0, :], "h0", pcol, "pcol", 1.0)
+    pick1("nI", "h", tab[:, 0, :], "h0", pcol, "pcol", -1.0)
+    pick1("W0", "h", tab[:, 0, :], "h0", pcol, "pcol", 2080.0)
+    mats["P0"] = mats["I"]
+    for o in (1, 2):
+        pick1("P%d" % o, "h", T.Fh[:, o - 1, :], "Fh%d" % o, pf[:, 27:28], "p256", 1.0)
+        pick1("W%d" % o, "h", T.Fh[:, o - 1, :], "Fh%d" % o, pf[:, 27:28], "p256", 2080.0)
+        pick1("PT%d" % o, "h", tab[:, 0, :], "h0", pf[:, 14 + 2 * o:15 + 2 * o], "shr", 1.0)
+        pick1("PS%d" % o, "h", tab[:, 0, :], "h0", pf[:, 15 + 2 * o:16 + 2 * o], "shr", 1.0)
+    for s in range(3):
+        shift("Sh%d" % s, -SH[s], 1.0)
+        tt(slot("nIS%d" % s, "h"), mats["nI"], mats["Sh%d" % s], OP.subtract, ["nI", "Sh%d" % s], ["nIS%d" % s], 128)
+        tt(slot("D%d" % s, "h"), mats["nI"], mats["Sh%d" % s], OP.add, ["nI", "Sh%d" % s], ["D%d" % s], 128)
+        shift("nSx%d" % s, SH[s], -1.0)
+    tmp = slot("tmp", "h")
+    for r, s in ((0, 1), (0, 2), (1, 2)):
+        nm = "PN%d%d" % (r, s)
+        shift(nm, SH[r], 64.0)
+        j = (SH[r] - SH[s]) & 15
+        ts(tmp, tab[:, 0, :], pf[:, j:j + 1], 64.0, OP.is_equal, OP.mult, ["h0", "shf"], ["tmp"], 128, 0.5)
+        tt(mats[nm], mats[nm], tmp, OP.add, [nm, "tmp"], [nm], 128)
+    pick1("G", "h", tab[:, 1, :], "gF0", gcol, "pfa", 1.0)
+    pick1("nG", "h", tab[:, 1, :], "gF0", gcol, "pfa", -1.0)
+    pick1("Godd", "h", tab[:, 3, :], "gF1", gcol, "pfa", 1.0)
+    for nm, v in (("Ib", 1.0), ("BI", 262144.0), ("I4k", 4096.0), ("nI4k", -4096.0), ("I16", 16.0)):
+        pick1(nm, "b", tab[:, 0, :], "h0", pcol, "pcol", v)
+    ts(slot("Wev", "b"), tab[:, 4, :], gcol, pf[:, 28:29], OP.is_equal, OP.mult, ["gF2", "pfa", "wcol"], ["Wev"], 128, 0.5)
+    for j, v in enumerate((4096.0, 4096.0, -8192.0)):
+        ts(T.IB[0:64, 64 * j:64 * j + 64], tab[0:64, 0, 0:64], pf[0:64, 20:21], v, OP.is_equal, OP.mult, ["h0", "pcol"], ["IB%d" % j], 64)
+    ts(T.gs[:, 0:8], T.gF2[:, 0:16:2], gcol, 32.0, OP.is_equal, OP.mult, ["gF2b", "pfa"], ["G32"], 16)
+    ts(T.gs[:, 16:24], T.gF2[:, 0:16:2], gcol, -64.0, OP.is_equal, OP.mult, ["gF2b", "pfa"], ["Gm64"], 8)
+    ms(T.selw[:], 0.0, ["selw"], 72)
+    ts(T.selw[:, 15:143:16], T.gF2[:, 0:16:2], gcol, pf[:, 28:29], OP.is_equal, OP.mult, ["gF2b", "pfa", "wcol", "selw"], ["selw"], 8)
+    ts(T.mk[:, :], tab[:, 2, 0:64], kcol, -4096.0, OP.not_equal, OP.mult, ["kk", "pfa"], ["mk"], 64)
+    ts(T.thR[0:8, :], tab[0:8, 1, :], pf[0:8, 20:21], -32.0, OP.is_equal, OP.mult, ["gF0", "pcol"], ["thR"], 128, 0.5)
+    ms(T.keepT[:], 1.0, ["keepT"], 256)
+    ms(T.keepT[:, 0:512:16], 0.0, ["keepT"], 32)
+    for j, v in enumerate((1.0e9, -1.0e9)):
+        ms(T.edge[:, j, :], -v, ["edge%d" % j], 64)
+        ms(T.edge[:, j, 0:128:16], v, ["edge%d" % j], 8)
+    ms(T.rs2[:], 0.0, ["rs2"], 64)
+    ms(T.rs2[:, 0:128:2], -1.0e6, ["rs2"], 64)
+    ms(T.c33[0:33, :], 1.0, ["c33"], 64)
+    ms(T.c33[32:33, :], 1024.0, ["c33"], 64)
+    cR = T.cR
+    ms(cR[0:33, :], 0.0, ["cR"], 512)
+    for s in range(3):
+        ts(cR[0:1, 128 * s:128 * s + 128], tab[0:1, 2, :], 2.0, 1.0, OP.mult, OP.add, ["kk", "cR"], ["cK%d" % s], 64)
+        ms(cR[32:33, 128 * s:128 * s + 128], -64.0 + 512.0 * s, ["cK%db" % s], 64, None, ["cR"])
+    ts(cR[0:1, 384:512], tab[0:1, 2, :], -1.0, 15.0, OP.mult, OP.add, ["kk", "cR"], ["cC"], 64)
+    for row, a, b, v, k in ((32, 384, 576, -12.0, "c12"), (0, 576, 640, 1.0, "cOa"), (0, 640, 704, -1.0, "cOb"),
+                            (32, 576, 704, -4.0, "cOc"), (32, 704, 768, 8.0, "cOd"), (32, 768, 832, -60.0, "c60"),
+                            (32, 832, 896, -4.0, "c4"), (0, 896, 960, -16.0, "cEa"), (32, 896, 960, -6.0, "cEb"),
+                            (0, 960, 1024, 1.0, "c1")):
+        ms(cR[row:row + 1, a:b], v, [k], 64, None, ["cR"])
+    ms(T.cev[0:1, :], 0.0, ["cev"], 64)
+    ms(T.cev[0:1, 0:128:2], -2048.0, ["cev"], 64)
+
+    def const(out, m, a, b, keys):
+        return (out, T.c33[0:33, 0:m], cR[0:33, a:b], ["c33", "cR"] + keys, max(64, b - a))
+
+    ms(T.dc[0:8, 0:5], 1.0, ["dc"], 8)
+    for j, v in ((0, 0.0), (1, 1.0 / 32), (3, -32.0)):
+        ms(T.dc[0:8, j:j + 1], v, ["dc"], 1)
+    ms(T.du[:], 1.0, ["du"], 32)
+    for j, v in ((0, 0.0), (2, 1.0 / 4096), (4, -4096.0)):
+        ms(T.du[:, j:32:8], v, ["du"], 4)
     for c in range(NCH):
-        ts(T["pm%d" % c][:, 192:256], T.gF[:, 0, 0:64], 0.0, 2.0, OP.mult, OP.add, ["gF0"], ["pm1_%d" % c], 64)
-    ts(T.thx[0:96, :], T.gF[0:96, 0, :], 0.0, 1.0, OP.mult, OP.add, ["gF0"], ["thx"], 128, 0.5)
-    ts(T.thx[0:8, :], T.thi[0:8, :], -2048.0, None, OP.add, None, ["thi", "thx"], ["thx"], 128)
-    for o in range(3):
-        k = "thR%d" % o
-        ts(T.thR[0:96, o, :], T.gF[0:96, 0, :], pf[0:96, 6:7], -16.0, OP.is_equal, OP.mult, ["gF0", "pfa"], [k], 128, 0.5)
-        ts(T.rowi[32:33, o, :], T.Fi[32:33, 2 * o, :], 15, None, OP.bitwise_and, None, ["Fi%d" % (2 * o)], ["rowi%d" % o], 128)
-        ts(T.thR[32:33, o, :], T.rowi[32:33, o, :], 0.5, None, OP.add, None, ["rowi%d" % o, k], [k], 128)
-        ts(T.thR[64:65, o, :], T.gF[64:65, 0, :], 0.0, -32768.0, OP.mult, OP.add, ["gF0", k], [k], 128, 0.5)
-    R = T.rows
-    for j, val in ((0, 1.0), (1, 3232.0), (2, -6160.0), (5, -4096.0)):
-        ts(R[0:1, j, :], T.gF[0:1, 0, :], 0.0, val, OP.mult, OP.add, ["gF0"], ["row%d" % j], 128, 0.5)
-    ts(R[0:1, 3, 0:128:2], T.gF[0:1, 0, 0:64], 0.0, -6144.0, OP.mult, OP.add, ["gF0"], ["row3a"], 64)
-    ts(R[0:1, 3, 1:128:2], T.gF[0:1, 0, 0:64], 0.0, -4096.0, OP.mult, OP.add, ["gF0"], ["row3b"], 64)
-    ts(T.rowi[0:1, 3, :], T.Fi[0:1, 0, :], 15, None, OP.bitwise_and, None, ["Fi0"], ["rowi3"], 128)
-    ts(R[0:1, 4, :], T.rowi[0:1, 3, :], -1.0, 15.0, OP.mult, OP.add, ["rowi3"], ["row4"], 128)
-    ones = R[0:1, 0, 0:CW]
+        n = str(c)
+        ms(T["d3" + n][:, 0:576:3], 0.0, ["d3z" + n], 192)
+        ms(T["d4" + n][:], 0, ["d4z" + n, "d4x" + n, "d4n" + n, "d4l" + n], 256)
+    pA = T.pK1
+    for j, v in ((1, RND), (2, -RND), (4, 0.0)):
+        ms(pA[0:8, 288 + j:289 + j], v, ["cA"], 1, "K1")
+    ms(T.a31[0:8, :], -15.5, ["a31"], 8)
+    ts(T.thf[0:8, :], T.thi[0:8, :], -2048.0 + 15.5, None, OP.add, None, ["thi"], ["thf"], 128)
 
-    def m64(name):
-        t_, j = mats[name + "#"]
-        return t_[0:64, j, 0:64]
+    def late_constants():
+        for c in range(NCH):
+            n = str(c); pK = T["pK" + n]
+            ms(pK[:, 256:288], 0.0, ["cu" + n], 32, "K" + n)
+            for j, v in ((1, -2047.5), (2, RND), (3, -RND), (4, -2048.0), (5, 5280.0)):
+                ms(pK[:, 256 + j:288:8], v, ["cu" + n], 4, "K" + n)
+
+    def limit():
+        ts(T.thx[0:8, :], T.thf[0:8, :], T.a31[0:8, 3:4], 2047.0, OP.add, OP.min, ["thf", "a31"], ["thx"], 128)
 
     nxt = T.cores[(rank + 1) % len(T.cores)]
     rid, pid = topo.addr(nxt, core)
@@ -245,239 +291,241 @@ def build_ops(g, core, T, topo, rank):
     XW = T.X[:, 0:2064]
     XK = ["X0", "X1", "Xz"]
 
-    def place(c, a_ap, a_key, last):
-        n = str(c); pU = T["pU" + n]; f = T["f" + n]; ib = T["i" + n]; bk = "U" + n
-        tt(f[:, 2, :], pU[:, 3, :], a_ap, OP.mult, [a_key, "Lp" + n], ["v" + n], CW, bk)
-        tt(ib[:, 0, :], pU[:, 4, :], f[:, 2, :], OP.add, ["v" + n, "Wp" + n], ["v2" + n], CW, bk)
-        ts(ib[:, 1, :], ib[:, 0, :], 5, 2047, OP.arith_shift_right, OP.bitwise_and, ["v2" + n], ["pl" + n], CW)
-        if not last:
-            cp(T["off" + n][:, :], ib[:, 1, :], ["pl" + n], ["off" + n], CW)
-
-    def lw(c, b, l_ap, l_key):
-        n = str(c); pU = T["pU" + n]
-        return [(pU[:, 3, :], mats["P0%d" % b], l_ap, ["P0%d" % b, l_key], "Lp" + n, 64),
-                (pU[:, 3, :], R[0:1, 1, :], ones, ["row0", "row1"], "Lp" + n, 64),
-                (pU[:, 4, :], mats["W0%d" % b], l_ap, ["W0%d" % b, l_key], "Wp" + n, 64)]
-
-    def pairs(c, s, a_ap, a_key, c_ap, c_key):
-        n = str(c); pH = T["pH" + n]; pm = T["pm" + n]; y = T["y" + n]; bk = "H" + n
-        lst = [(pH[:, 0, :], mats["Nx%d" % s], a_ap, ["Nx%d" % s, a_key], "as" + n, 64),
-               (pH[:, 1, :], mats["DC0%d" % s], c_ap, ["DC0%d" % s, c_key], "dc" + n, 64)]
-        for r in range(s):
-            lst.append((pH[:, 1, :], mats["DC%d%d" % (r, s)], y[:, r, 128:192], ["DC%d%d" % (r, s), "y%d" % r + n], "dc" + n, 64))
-        mms(bk, lst)
-        tt(T["eq" + n][:, :], pH[:, 0, :], a_ap, OP.is_equal, ["as" + n, a_key], ["eq" + n], CW, bk)
-        tt(pm[:, 0:64], pH[:, 0, :], a_ap, OP.max, ["as" + n, a_key], ["pmx" + n], CW, bk)
-        tt(pm[:, 64:128], pH[:, 0, :], a_ap, OP.min, ["as" + n, a_key], ["pmn" + n], CW, bk)
-        ts(pm[:, 128:192], pH[:, 1, :], 0.0, None, OP.min, None, ["dc" + n], ["pmc" + n], CW, 1.0, bk)
-
-    def pick(c, pieces):
-        n = str(c)
-        keys = []
-        for j, (e, a, b) in enumerate(pieces):
-            k = units("rec" + n, a, b)
-            gather(e, T["rec" + n][:, 16 * a:16 * b], XW, T["off" + n][:, a:b], XK + ["off" + n], k, 16 * (b - a))
-            keys += k
-        return keys
-
     def units(name, a, b):
-        return ["%s_%d" % (name, j) for j in range(a // 4, b // 4)]
+        return ["%s_%d" % (name, j) for j in range(a // 8, b // 8)]
+
+    def pick(c, pieces, off, okey):
+        n = str(c)
+        for e, a, b in pieces:
+            gather(e, T["rec" + n][:, 16 * a:16 * b], XW, off(a, b), XK + [okey], units("rec" + n, a, b) + (["turnA"] if e == "a" else []), 16 * (b - a))
 
     def tile_of(t, c):
         if t == 0:
             return (lambda a, b: T.tile0[:, c, a:b]), "tile0_%d" % c
         return (lambda a, b: T.lnd[:, 2 * (t - 1) + c, a:b]), "lnd%d_%d" % (t, c)
 
-    def best(c, o):
-        n = str(c); key = T["pK" + n][0:64, 0:128]; Bk = T["Bk" + n]; kk = "key" + n
-        scan(Bk[0:64, 0, :], T.keepT[0:64, 0:128], key, OP.mult, o, [kk, "keepT"], ["Bp" + n], 128, 1.0, "K" + n)
-        scan(Bk[0:64, 1, ::-1], T.keepT[0:64, 0:128], Bk[0:64, 0, ::-1], OP.mult, o, ["Bp" + n, "keepT"], ["Bk" + n], 128, 1.0)
-        tt(T["ohT" + n][0:64, :], key, Bk[0:64, 1, :], OP.is_equal, [kk, "Bk" + n], ["ohT" + n], 128, "K" + n)
+    def best(c, o, oh, okey):
+        n = str(c); pK = T["pK" + n]; Bk = T["Bk" + n]; kk = "key" + n
+        j, other = (0, OP.max) if o == OP.min else (1, OP.min)
+        scan(Bk[0:64, 0, :], T.keepT[0:64, 0:128], pK[0:64, 0:128], OP.mult, o, [kk, "keepT"], ["Bk" + n], 128, 1.0, "K" + n)
+        scan(pK[0:64, 255:127:-1], T.edge[0:64, j, :], pK[0:64, 127::-1], other, o, [kk, "edge%d" % j], ["Bs" + n], 128, 1.0, "K" + n)
+        tt(oh[0:64, :], pK[0:64, 128:256], Bk[0:64, 0, :], OP.is_equal, ["Bs" + n, "Bk" + n], [okey], 128, "K" + n)
+
+    def begin(t, c):
+        n = str(c); tl, tk = tile_of(t, c); pU = T["pU" + n]
+        for s in range(3):
+            nb = "P%d" % ((s + 1) % 3)
+            group("U" + n, "Lp%d" % s + n, [[(pU[:, 256 + 64 * s:320 + 64 * s], mats[nb], tl(64, 128), [nb if nb != "P0" else "I", tk], 64)]])
+        act(T["d3" + n][:, 2:576:3], pU[:, 256:448], AF.Identity, 3232.0, 1.0, ["Lp%d" % s + n for s in range(3)], ["d3l" + n], 192, "U" + n)
 
     def step(t, s, c):
         n = str(c); tl, tk = tile_of(t, c)
-        pK = T["pK" + n]; pO = T["pO" + n]; pU = T["pU" + n]
-        rec = T["rec" + n]; mn = T["mn" + n]; cl = T["cl" + n]; y = T["y" + n]; pm = T["pm" + n]
-        f = T["f" + n]; an = T["an" + n]
-        a_ap, a_key = (tl(0, 64), tk) if s == 0 else (an[:, s - 1, :], "an%d" % (s - 1) + n)
-        pick(c, G0[c] if s == 0 else GP)
+        pK = T["pK" + n]; pO = T["pO" + n]; pU = T["pU" + n]; pH = T["pH" + n]
+        rec = T["rec" + n]; mn = T["mn" + n]; cl = T["cl" + n]; y = T["y" + n]; hi2 = T["hi" + n]
+        an = T["an" + n]; eq = T["eq" + n]; so = T["so" + n]; d3 = T["d3" + n]; ib = T["i" + n]; ohT = T["ohT" + n]
+        bh, bo, bu = "H" + n, "O" + n, "U" + n
+        if s == 0 and t > 0:
+            pick(c, CFG["G0"], lambda a, b: T.lno[:, 2 * (t - 1) + c, a:b], "lno%d_%d" % (t, c))
+        else:
+            pick(c, CFG["G0"] if s == 0 else CFG["GP"], lambda a, b: T["off" + n][:, a:b], "off" + n)
+        hi = hi2[:, 1:128:2]
+        if s == 0:
+            a_ap, ak = tl(0, 64), tk
+            group(bh, "aj" + n, [[(pH[:, 1:128:2], mats["Sh0"], a_ap, ["Sh0", ak], 64)]])
+            tt(hi, pH[:, 1:128:2], a_ap, OP.max, ["aj" + n, ak], ["hi" + n], CW, bh)
+        else:
+            a_ap, ak = hi2[:, 0:128:2], "hi" + n
+            group(bh, "ak" + n, [[(pH[:, 0:128:2], mats["PT%d" % s], an[:, :], ["PT%d" % s, "an" + n], 64)]])
+            group(bh, "aj" + n, [[(pH[:, 1:128:2], mats["PS%d" % s], an[:, :], ["PS%d" % s, "an" + n], 64)]])
+            scan(hi2[:, :], T.rs2[:, :], pH[:, 0:128], OP.add, OP.max, ["ak" + n, "aj" + n, "rs2"], ["hi" + n], 128, 1.0, bh)
+        tt(eq[:, :], pH[:, 1:128:2], a_ap, OP.is_equal, ["aj" + n, ak], ["eq" + n], CW, bh)
         cyc = 16 if s < 2 else 8
         w_ = 16 // cyc
+        for a, b in CFG["CP"]:
+            tt(cl[:, w_ * a:w_ * b], rec[:, 16 * a + cyc - 1:16 * b:cyc], rec[:, 16 * a:16 * b:cyc], OP.min, units("rec" + n, a, b), units("cl" + n, a, b), w_ * (b - a))
+        for a, b in CFG["SP"]:
+            rk = units("rec" + n, a, b)
+            scan(mn[:, 16 * a:16 * b - 1], rec[:, 16 * a:16 * b - 1], rec[:, 16 * a + 1:16 * b], OP.max, OP.min, rk, units("mn" + n, a, b), 16 * (b - a), 0.5)
         key = pK[0:64, 0:128]
-        kk = "key" + n
-        lst = [(key, T.thx[0:65, 64 * c:64 * c + 64], T.thR[0:65, s, :], ["thx", "thR%d" % s], kk, 128),
-               (key, T["eq" + n][:, :], mats["BI"], ["eq" + n, "BI"], kk, 128)]
+        runs = [[const(key, 64, 128 * s, 128 * s + 128, ["cK%d" % s, "cK%db" % s])]]
         for r in range(s):
-            lst.append((key, y[:, r, 192:256], mats["PN%d%d" % (r, s)], ["y%d" % r + n, "PN%d%d" % (r, s)], kk, 128))
-        for a, b in HALVES:
-            rk = units("rec" + n, a, b); mk = units("mn" + n, a, b); ck = units("cl" + n, a, b)
-            tt(cl[:, w_ * a:w_ * b], rec[:, 16 * a + cyc - 1:16 * b:cyc], rec[:, 16 * a:16 * b:cyc], OP.min, rk, ck, w_ * (b - a))
-            scan(mn[:, 16 * a:16 * b - 1], rec[:, 16 * a:16 * b - 1], rec[:, 16 * a + 1:16 * b], OP.max, OP.min, rk, mk, 16 * (b - a), 0.5)
+            nm = "PN%d%d" % (r, s)
+            runs.append([(key, y[:, r, 64 * h:64 * h + 64], mats[nm], ["y%d" % r + n, nm], 128) for h in range(2)])
+        sums = []
         for a, b in PH:
             rk = units("rec" + n, a, b); mk = units("mn" + n, a, b); ck = units("cl" + n, a, b)
-            for k in range(16):
-                pv = (k - 1) % cyc + (k // cyc) * cyc
-                for j in (k, pv):
-                    lst.append((pK[a:b, j:128:16], rec[:, 16 * a + k:16 * b:16], T.gs[:, 0:8], rk + ["G16"], kk, b - a))
-            for k in range(cyc - 1, 16, cyc):
-                lst.append((pK[a:b, k:128:16], cl[:, w_ * a + k // cyc:w_ * b:w_], T.gs[:, 16:24], ck + ["Gm32"], kk, b - a))
-            for k in range(16):
-                if k % cyc != cyc - 1:
-                    lst.append((pK[a:b, k:128:16], mn[:, 16 * a + k:16 * b:16], T.gs[:, 16:24], mk + ["Gm32"], kk, b - a))
-        lst.append((key, T.a31[:, :], mats["nGb"], ["a31", "nGb"], kk, 128))
-        mms("K" + n, lst)
-        ohT = T["ohT" + n]
-        best(c, OP.min)
+            one = []; two = []
+            for p in range(16):
+                k = row_of(s, p)
+                for j in (k, (k - SH[s]) & 15):
+                    one.append((pK[a:b, j:128:16], rec[:, 16 * a + p:16 * b:16], T.gs[:, 0:8], rk + ["G32"], b - a))
+                if p % cyc == cyc - 1:
+                    two.append((pK[a:b, k:128:16], cl[:, w_ * a + p // cyc:w_ * b:w_], T.gs[:, 16:24], ck + ["Gm64"], b - a))
+                else:
+                    two.append((pK[a:b, k:128:16], mn[:, 16 * a + p:16 * b:16], T.gs[:, 16:24], mk + ["Gm64"], b - a))
+            sums.append((one, two))
+        runs += [sums[0][0], sums[0][1], [(key, eq[:, :], mats["BI"], ["eq" + n, "BI"], 128)], sums[1][0], sums[1][1],
+                 [(key, T.thx[0:8, 64 * c:64 * c + 64], T.thR[0:8, :], ["thx", "thR"], 128)]]
+        group("K" + n, "key" + n, runs)
+        best(c, OP.min, ohT, "ohT" + n)
+        cs_ = [(tl(128, 192), tk)] + [(y[:, r, 128:192], "yC%d" % r + n) for r in range(s)]
+        group(bo, "yP" + n, [
+            [const(pO[:, 0:192], 128, 576, 768, ["cOa", "cOb", "cOc", "cOd"])],
+            [(pO[:, 128:192], mats["D%d" % s], d, ["D%d" % s, dk], 64) for d, dk in cs_],
+            [(pO[:, 0:64], mats["I"], hi, ["I", "hi" + n], 64), (pO[:, 64:128], mats["I"], hi, ["I", "hi" + n], 64),
+             (pO[:, 64:128], mats["nIS%d" % s], a_ap, ["nIS%d" % s, ak], 64)],
+            [(pO[:, 0:192], ohT[0:64, :], T.IB[0:64, :], ["ohT" + n, "IB0", "IB1", "IB2"], 192)]])
+        yk = "y%d" % s + n
+        late = [lambda: ts(y[:, s, 0:128], pO[:, 0:128], -2048.0, None, OP.max, None, ["yP" + n], [yk], 128, 1.0, bo),
+                lambda: ts(y[:, s, 128:192], pO[:, 128:192], 0.0, None, OP.min, None, ["yP" + n], ["yC%d" % s + n], 64, 1.0, bo)]
+        for fn in late:
+            fn()
         nb = (s + 1) % 3
-        mms("O" + n, [(pO[:, 0:128], ohT[0:64, :], T.I4[0:64, :, :], ["ohT" + n, "I4_0", "I4_1"], "oN" + n, 128)])
-        yk = "yA%d" % s + n
-        tt(y[:, s, 0:128], pO[:, 0:128], pm[:, 0:128], OP.mult, ["oN" + n, "pmx" + n, "pmn" + n], [yk], 128, "O" + n)
-        tt(y[:, s, 128:256], pO[:, 0:128], pm[:, 128:256], OP.mult, ["oN" + n, "pmc" + n, "pm1_" + n], ["y%d" % s + n], 128, "O" + n)
-        pn = "P%d%d" % (s, nb)
-        lst = lw(c, nb, tl(64, 128), tk) + [
-            (pU[:, 2, :], mats[pn], a_ap, [pn, a_key], "aP" + n, 64),
-            (pU[:, 0, :], mats["n" + pn], a_ap, ["n" + pn, a_key], "E" + n, 64),
-            (pU[:, 0, :], mats["G"], y[:, s, 0:64], ["G", yk], "E" + n, 64),
-            (pU[:, 1, :], mats["G"], y[:, s, 64:128], ["G", yk], "DL" + n, 64),
-            (pU[:, 1, :], mats["nG"], y[:, s, 0:64], ["nG", yk], "DL" + n, 64)]
-        bk = "U" + n
-        mms(bk, lst)
-        ts(f[:, 0, :], pU[:, 0, :], 0.0, None, OP.is_equal, None, ["E" + n], ["e" + n], CW, 1.0, bk)
-        tt(f[:, 1, :], pU[:, 1, :], f[:, 0, :], OP.mult, ["DL" + n, "e" + n], ["t" + n], CW, bk)
-        ak = "an%d" % s + n
-        tt(an[:, s, :], pU[:, 2, :], f[:, 1, :], OP.add, ["aP" + n, "t" + n], [ak], CW, bk)
-        place(c, an[:, s, :], ak, s == 2)
+        pn = "P%d" % nb; pk = pn if nb else "I"
+        group(bu, "ua" + n, [[(pU[:, 1:192:3], mats[pn], a_ap, [pk, ak], 64)]])
+        group(bu, "uw" + n, [[(pU[:, 2:192:3], mats["W%d" % nb], tl(64, 128), ["W%d" % nb, tk], 64)]])
+        group(bh, "E" + n, [[(pH[:, 128:192], mats[pn], a_ap, [pk, ak], 64)],
+                            [(pH[:, 128:192], mats["nG"], y[:, s, 0:64], ["nG", yk], 64)]])
+        group(bu, "ud" + n, [[const(pU[:, 0:192:3], 128, 768, 832, ["c60"])],
+                             [(pU[:, 0:192:3], mats["nG"], y[:, s, 64 * h:64 * h + 64], ["nG", yk], 64) for h in range(2)]])
+        ts(d3[:, 192 * s + 1:192 * s + 192:3], pH[:, 128:192], 30719.0, None, OP.is_equal, None, ["E" + n], ["e%d" % s + n], CW, 1.0, bh)
+        scan(so[:, 0:192], d3[:, 192 * s:192 * s + 192], pU[:, 0:192], OP.mult, OP.add,
+             ["e%d" % s + n, "d3z" + n, "d3l" + n, "ua" + n, "uw" + n, "ud" + n], ["so" + n], 192, 1.0, bu)
+        bits(ib[:, 1, :], so[:, 2:192:3], 5, 2047, ["so" + n], ["pl" + n], CW)
         if s < 2:
-            pairs(c, s + 1, an[:, s, :], ak, tl(128, 192), tk)
+            cp(T["off" + n][:, :], ib[:, 1, :], ["pl" + n], ["off" + n], CW)
+        cp(an[:, :], so[:, 1:192:3], ["so" + n], ["an" + n], CW)
 
-    def act(out, in_, fn, bias, scale, r, w, n, bank=None):
-        op("a", lambda: A.activation(out, in_, fn, bias=bias, scale=scale), r, w, 100 + n, bank)
-
-    def count(s):
-        pO = T["pO%d" % (NCH - 1)]; bk = "O%d" % (NCH - 1)
-        mms(bk, [(pO[:, 256:320], mats["G"], T["y%d" % c][:, s, 192:256], ["G", "y%d%d" % (s, c)], "Ac", 64) for c in range(NCH)])
-        e = CE[s == 2]
-        if e == "a":
-            op("a", lambda: A.activation(T.junk[:, :], pO[:, 256:320], AF.Copy, accum_out=T.cnt[:, 0:1]), ["Ac"], ["cnt", "junk"], 200, bk)
-        else:
-            op("v", lambda: V.tensor_reduce(T.cnt[:, 0:1], pO[:, 256:320], AxisListType.X, OP.add), ["Ac"], ["cnt"], 64, bk)
-        ts(T.offa[:, :], T.a31[:, 0:4], T.cnt[:, 0:1], None, OP.add, None, ["a31", "cnt"], ["offa"], 4)
-        gather(e, T.a31[:, :], T.modt[:, 0:320], T.offa[:, 0:4], ["modt", "offa"], ["a31"], 64)
+    def count():
+        out = pA[0:8, 288:292:3]
+        runs = [[(out, mats["Ib8"], T.a31[0:8, 3:5], ["Ib", "a31"], 8)]
+                + [(out, T["ohT%d" % c][0:64, k:128:16], T.keepT[0:64, 1:3], ["ohT%d" % c, "keepT"], 8) for c in range(NCH) for k in range(16)]]
+        group("K1", "Ac", runs)
+        scan(T.a31[0:8, 0:5], T.dc[0:8, 0:5], pA[0:8, 288:293], OP.mult, OP.add, ["Ac", "cA", "dc"], ["a31"], 5, 1.0, "K1")
+        limit()
 
     def refill(t, c):
         n = str(c); tl, tk = tile_of(t, c)
         pK = T["pK" + n]; pO = T["pO" + n]; pU = T["pU" + n]; pH = T["pH" + n]
-        y = T["y" + n]; f = T["f" + n]; an = T["an" + n]; ib = T["i" + n]
-        Bk = T["Bk" + n]; ohT = T["ohT" + n]; hT = T["hT" + n]; yq = T["yq" + n]; oq = T["offq" + n]
-        z = T["z" + n]; ui = T["ui" + n]; q = T["q" + n]; nw = T["nw" + n]; av = T["av" + n]
-        a_ap, ak = an[:, 2, :], "an2" + n
-        terms = [(tl(128, 192), tk, "P00"), (y[:, 0, 128:192], "y0" + n, "P00"), (y[:, 1, 128:192], "y1" + n, "P10"),
-                 (y[:, 2, 128:192], "y2" + n, "P20")]
-        emp = [(y[:, r, 192:256], "y%d" % r + n, "Sx%d" % r) for r in range(3)]
-        key = pK[0:64, 0:128]; kk = "key" + n
-        od = [terms[0], terms[1], terms[2], emp[0], emp[1], terms[3], emp[2]]
-        mms("K" + n, [(key, ones, R[0:1, 4, :], ["row0", "row4"], kk, 128)] + [(key, d, mats[mn_], [dk, mn_], kk, 128) for d, dk, mn_ in od])
-        best(c, OP.max)
-        act(hT[0:64, :], Bk[0:64, 1, :], AF.Identity, 128.515625, 1.0 / 32, ["Bk" + n], ["hT" + n], 128)
-        bo = "O" + n
-        mms(bo, [(pO[:, 0:64], ohT[0:64, :], T.I4[0:64, 0, :], ["ohT" + n, "I4_0"], "oN" + n, 64)])
+        y = T["y" + n]; f = T["f" + n]; an = T["an" + n]; ib = T["i" + n]; so = T["so" + n]; d4 = T["d4" + n]
+        Bk = T["Bk" + n]; oh2 = T["oh2" + n]; hT = T["hT" + n]; yq = T["yq" + n]; oq = T["offq" + n]
+        z = T["z" + n]; q = T["q" + n]; nw = T["nw" + n]; av = T["av" + n]; r5 = T["r5" + n]
+        bk, bh, bo, bu = "K" + n, "H" + n, "O" + n, "U" + n
+        a_ap, ak = an[:, :], "an" + n
+        cost = [(tl(128, 192), tk, "I")] + [(y[:, r, 128:192], "yC%d" % r + n, "I") for r in range(3)]
+        emp = [(y[:, r, 64 * h:64 * h + 64], "y%d" % r + n, "nSx%d" % r) for r in range(3) for h in range(2)]
+        early = cost[0:3] + emp[0:4]; late = emp[4:6] + cost[3:4]
+        key = pK[0:64, 0:128]
+        group(bk, "key" + n, [[const(key, 64, 384, 512, ["cC", "c12"])] + [(key, d, mats[m], [dk, m], 128) for d, dk, m in early],
+                              [(key, d, mats[m], [dk, m], 128) for d, dk, m in late]])
+        best(c, OP.max, oh2, "oh2" + n)
+        tt(Bk[0:64, 1, :], pK[0:64, 128:256], Bk[0:64, 0, :], OP.max, ["Bs" + n, "Bk" + n], ["Bb" + n], 128, bk)
+        act(hT[0:64, :], Bk[0:64, 1, :], AF.Identity, 128.515625, 1.0 / 32, ["Bb" + n], ["hT" + n], 128)
+        group(bh, "emp" + n, [[const(pH[:, 256:320], 128, 512, 576, ["c12"])] + [(pH[:, 256:320], mats[m], d, [dk, m], 64) for d, dk, m in emp[0:4]],
+                              [(pH[:, 256:320], mats[m], d, [dk, m], 64) for d, dk, m in emp[4:6]]])
+        tt(f[:, 3, :], ib[:, 1, :], pH[:, 256:320], OP.subtract, ["pl" + n, "emp" + n], ["pl2" + n], CW, bh)
+        ts(T["off" + n][:, :], f[:, 3, :], 2048.0, None, OP.min, None, ["pl2" + n], ["off" + n], CW)
+        group(bo, "oN" + n, [[(pO[:, 0:64], oh2[0:64, :], mats["Ib64"], ["oh2" + n, "Ib"], 64)]])
         tt(yq[:, 0, :], pO[:, 0:64], ib[:, 1, :], OP.mult, ["oN" + n, "pl" + n], ["yq" + n], CW, bo)
         tt(yq[:, 1, :], pO[:, 0:64], a_ap, OP.mult, ["oN" + n, ak], ["ya" + n], CW, bo)
-        mms(bo, [(pO[:, 320:324], T.selo[:, 15 - r:143 - r], yq[:, 0, r:64:16], ["selo", "yq" + n], "Qp" + n, 64) for r in range(16)])
-        cp(oq[:, 0:4], pO[:, 320:324], ["Qp" + n], ["oz" + n], 4, 1.0, bo)
-        gather(ZE, z[:, :], XW, oq[:, 0:4], XK + ["oz" + n], ["z" + n], 64)
-        mms(bo, [(pO[:, 448:452], T.selw[:, 15 - r:143 - r], z[:, r:64:16], ["selw", "z" + n], "uQ" + n, 64) for r in range(16)]
-            + [(pO[:, 384:448], mats["Wev"], z[:, :], ["Wev", "z" + n], "uP" + n, 64)])
-        cp(ui[:, 0, 0:68], pO[:, 384:452], ["uP" + n, "uQ" + n], ["u0" + n], 68, 1.0, bo)
-        ts(ui[:, 1, 0:68], ui[:, 0, 0:68], 4095, None, OP.bitwise_and, None, ["u0" + n], ["u" + n], 68)
-        uq = ui[:, 1, 64:68]
-        ts(q[:, 0, :], uq, -2048.0, None, OP.add, None, ["u" + n], ["q0" + n], 4)
-        ts(q[:, 1, :], uq, 3232.0, None, OP.add, None, ["u" + n], ["q1" + n], 4)
+        group(bu, "Qp" + n, [[(pU[:, 448:512], mats["I"], T.mk[:, :], ["I", "mk"], 64)],
+                             [(pU[:, 448:512], mats["G"], yq[:, 0, :], ["G", "yq" + n], 64)]])
+        scan(f[:, 4, :], T.keepT[:, 0:64], pU[:, 448:512], OP.mult, OP.max, ["Qp" + n, "keepT"], ["Qs" + n], CW, 1.0, bu)
+        cp(oq[:, 0:4], f[:, 4, 15:64:16], ["Qs" + n], ["oz" + n], 4)
+        gather(CFG["ZE"], z[:, :], XW, oq[:, 0:4], XK + ["oz" + n], ["z" + n], 64)
+        S = pK[:, 256:288:8]
+        group(bk, "uQ" + n, [[(S, T.selw[:, 15 - r:143 - r], z[:, r:64:16], ["selw", "z" + n], 64) for r in range(16)]])
+        group(bo, "uP" + n, [[(pO[:, 128:192], mats["Wev"], z[:, :], ["Wev", "z" + n], 64)]])
+        scan(r5[:, :], T.du[:, :], pK[:, 256:288], OP.mult, OP.add, ["uQ" + n, "cu" + n, "du"], ["r5" + n], 32, 1.0, bk)
+        tt(q[:, 0, :], S, r5[:, 4:32:8], OP.add, ["uQ" + n, "r5" + n], ["q0" + n], 4, bk)
+        tt(q[:, 1, :], S, r5[:, 5:32:8], OP.add, ["uQ" + n, "r5" + n], ["q1" + n], 4, bk)
         tt(q[:, 2, :], q[:, 0, :], q[:, 1, :], OP.mult, ["q0" + n, "q1" + n], ["q2" + n], 4)
-        ts(q[:, 3, :], q[:, 2, :], 5, 1023, OP.arith_shift_right, OP.bitwise_and, ["q2" + n], ["q3" + n], 4)
+        bits(q[:, 3, :], q[:, 2, :], 5, 1023, ["q2" + n], ["q3" + n], 4)
         cp(oq[:, 4:8], q[:, 3, :], ["q3" + n], ["on" + n], 4)
-        bh = "H" + n
-        mms(bh, [(pH[:, 2, :], mats[mn_], d, [dk, mn_], "emp" + n, 64) for d, dk, mn_ in emp])
-        tt(f[:, 3, :], ib[:, 1, :], pH[:, 2, :], OP.subtract, ["pl" + n, "emp" + n], ["pl2" + n], CW, bh)
-        ts(T["off" + n][:, :], f[:, 3, :], 2048.0, None, OP.min, None, ["pl2" + n], ["off" + n], CW)
-        mms(bh, [(pH[:, 3, :], mats[mn_], d, [dk, mn_], "Cn" + n, 64) for d, dk, mn_ in od]
-            + [(pH[:, 3, :], ohT[0:64, :], m64("nI4k"), ["ohT" + n, "nI4k"], "Cn" + n, 64)])
-        so = 2 * t + c; sk = "snd%d" % so
+        cp(ib[:, 0, :], pO[:, 128:192], ["uP" + n], ["u0" + n], CW, 1.0, bo)
+        bits(ib[:, 3, :], ib[:, 0, :], 0, 4095, ["u0" + n], ["u" + n], CW)
+        Cn = pH[:, 320:384]
+        group(bh, "Cn" + n, [[const(Cn, 128, 512, 576, ["c12"])] + [(Cn, mats[m], d, [dk, m], 64) for d, dk, m in early + late],
+                             [(Cn, oh2[0:64, :], mats["nI4k64"], ["oh2" + n, "nI4k"], 64)]])
+        sx = 2 * t + c; sk = "snd%d" % sx
         sg = nw[:, 0, :]
-        act(sg, pH[:, 3, :], AF.Sign, 8.0, 1.0, ["Cn" + n], ["nw" + n], CW, bh)
-        act(nw[:, 1, :], pH[:, 3, :], AF.Relu, 0.0, 1.0, ["Cn" + n], ["cr" + n], CW, bh)
-        act(f[:, 1, :], sg, AF.Identity, -6144.0, -4096.0, ["nw" + n], ["t" + n], CW)
-        bu = "U" + n
-        mms(bu, [(pU[:, 5, :], mats["P00"], a_ap, ["P00", ak], "P1" + n, 64),
-                 (pU[:, 5, :], R[0:1, 5, :], ones, ["row0", "row5"], "P1" + n, 64),
-                 (pU[:, 7, :], mats["P00"], tl(64, 128), ["P00", tk], "PL" + n, 64),
-                 (pU[:, 7, :], R[0:1, 5, :], ones, ["row0", "row5"], "PL" + n, 64),
-                 (pU[:, 6, :], R[0:1, 3, :], ones, ["row0", "row3a", "row3b"], "P3" + n, 64),
-                 (pU[:, 0, :], R[0:1, 2, :], ones, ["row0", "row2"], "E" + n, 64),
-                 (pU[:, 6, :], mats["Godd"], yq[:, 1, :], ["Godd", "ya" + n], "P3" + n, 64),
-                 (pU[:, 0, :], hT[0:64, :], m64("I16"), ["hT" + n, "I16"], "E" + n, 64),
-                 (pU[:, 0, :], mats["nI4k"], sg, ["nI4k", "nw" + n], "E" + n, 64),
-                 (pU[:, 6, :], mats["nI4k"], sg, ["nI4k", "nw" + n], "P3" + n, 64),
-                 (pU[:, 5, :], mats["I4k"], sg, ["I4k", "nw" + n], "P1" + n, 64),
-                 (pU[:, 7, :], mats["I4k"], sg, ["I4k", "nw" + n], "PL" + n, 64)])
-        tt(T.snd[:, so, 128:192], pU[:, 0, :], nw[:, 1, :], OP.max, ["E" + n, "cr" + n], [sk + "c"], CW, bu)
+        act(sg, Cn, AF.Sign, 8.0, 1.0, ["Cn" + n], ["nw" + n], CW, bh)
+        act(nw[:, 1, :], Cn, AF.Relu, 0.0, 1.0, ["Cn" + n], ["cr" + n], CW, bh)
+        ts(d4[:, 2:256:4], Cn, 0.0, None, OP.is_lt, None, ["Cn" + n], ["d4n" + n], CW, 1.0, bh)
+        act(f[:, 1, :], sg, AF.Identity, -6144.0, -4096.0, ["nw" + n], ["mL" + n], CW)
+        group(bu, "ud" + n, [[const(pU[:, 0:256:4], 128, 960, 1024, ["c1"])]])
+        group(bu, "ua" + n, [[(pU[:, 2:256:4], mats["I"], a_ap, ["I", ak], 64)]])
+        group(bu, "uw" + n, [[(pU[:, 1:256:4], T.cev[0:1, :], cR[0:1, 960:1024], ["cev", "c1"], 64),
+                              (pU[:, 1:256:4], mats["nI"], a_ap, ["nI", ak], 64),
+                              (pU[:, 1:256:4], mats["Godd"], yq[:, 1, :], ["Godd", "ya" + n], 64)]])
+        group(bu, "Lp0" + n, [[const(pU[:, 256:320], 128, 832, 896, ["c4"]), (pU[:, 256:320], mats["I"], tl(64, 128), ["I", tk], 64),
+                               (pU[:, 256:320], mats["I4k"], sg, ["I4k", "nw" + n], 64)]])
+        group(bu, "Lp1" + n, [[const(pU[:, 320:384], 128, 896, 960, ["cEa", "cEb"]),
+                               (pU[:, 320:384], mats["nI4k"], sg, ["nI4k", "nw" + n], 64),
+                               (pU[:, 320:384], hT[0:64, :], mats["I1664"], ["hT" + n, "I16"], 64)]])
+        tt(T.snd[:, sx, 128:192], pU[:, 320:384], nw[:, 1, :], OP.max, ["Lp1" + n, "cr" + n], [sk + "c"], CW, bu)
         dg = 60 + GAM * 64
-        op("v", lambda: V.tensor_tensor(ib[:, 2, :], T.rbt[:, 0:1024].indirect(oq[:, 4:8]), ui[:, 1, 0:64], OP.mult),
-           ["rbt", "on" + n, "u" + n], ["w" + n], dg)
-        op("v", lambda: V.tensor_tensor(f[:, 2, :], T.rbt[:, 0:1024].indirect(oq[:, 4:8]), f[:, 1, :], OP.add),
-           ["rbt", "on" + n, "t" + n], ["v" + n], dg)
+        body = T.rbt[:, 0:1024]
+        op("v", lambda: V.tensor_tensor(f[:, 2, :], body.indirect(oq[:, 4:8]), f[:, 1, :], OP.add), ["rbt", "on" + n, "mL" + n], ["vb" + n], dg)
+        op("v", lambda: V.tensor_tensor(ib[:, 2, :], body.indirect(oq[:, 4:8]), ib[:, 3, :], OP.mult), ["rbt", "on" + n, "u" + n], ["w" + n], dg)
+        Ln = T.snd[:, sx, 64:128]
+        tt(Ln, pU[:, 256:320], f[:, 2, :], OP.max, ["Lp0" + n, "vb" + n], [sk + "l"], CW, bu)
         if t > 0:
             ts(ib[:, 2, :], ib[:, 2, :], T.t32[:, 3 + t:4 + t], None, OP.add, None, ["w" + n, "t32"], ["w" + n], CW)
-        ts(ib[:, 3, :], ib[:, 2, :], 5, 4095, OP.arith_shift_right, OP.bitwise_and, ["w" + n], ["x" + n], CW)
-        tt(T.snd[:, so, 64:128], pU[:, 7, :], f[:, 2, :], OP.max, ["PL" + n, "v" + n], [sk + "l"], CW, bu)
-        tt(f[:, 0, :], pU[:, 6, :], ib[:, 3, :], OP.add, ["P3" + n, "x" + n], ["e" + n], CW, bu)
-        tt(T.snd[:, so, 0:64], pU[:, 5, :], f[:, 0, :], OP.max, ["P1" + n, "e" + n], [sk + "a"], CW, bu)
+        bits(d4[:, 1:256:4], ib[:, 2, :], 5, 4095, ["w" + n], ["d4x" + n], CW)
         if t < VIS - 1:
-            op("g", lambda: g.remote_dma(T.lnd[:, so, :], T.snd[:, so, :], T.sem["arr%d" % so], T.sem.loc, pid, rid, mask),
-               [sk + "a", sk + "l", sk + "c"], ["lnd%d_%d" % (t + 1, c)], 3500, None, "rem", (so, n_in, n_out))
+            ts(d4[:, 3:256:4], Ln, 3232.0, None, OP.add, None, [sk + "l"], ["d4l" + n], CW)
+            group(bu, "u4" + n, [[(pU[:, 3:256:4], mats["W0"], Ln, ["W0", sk + "l"], 64)]])
+        scan(so[:, :], d4[:, :], pU[:, 0:256], OP.mult, OP.add,
+             ["d4z" + n, "d4x" + n, "d4n" + n, "d4l" + n, "ua" + n, "uw" + n, "ud" + n, "u4" + n], ["so" + n], 256, 1.0, bu)
+        if t < VIS - 1:
+            bits(ib[:, 2, :], so[:, 3:256:4], 5, 2047, ["so" + n], ["w" + n], CW)
+            cp(T.sno[:, sx, :], ib[:, 2, :], ["w" + n], ["sno%d" % sx], CW)
+            cp(T.snd[:, sx, 0:64], so[:, 2:256:4], ["so" + n], [sk + "a"], CW)
+            op("g", lambda: g.remote_dma(T.lno[:, sx, :], T.sno[:, sx, :], T.sem["aro%d" % sx], T.sem.loc, pid, rid, mask),
+               ["sno%d" % sx], ["lno%d_%d" % (t + 1, c), "turn"], CFG["REM"], None, "rem", ("aro%d" % sx, n_in, n_out))
+            op("g", lambda: g.remote_dma(T.lnd[:, sx, :], T.snd[:, sx, :], T.sem["art%d" % sx], T.sem.loc, pid, rid, mask),
+               [sk + "a", sk + "l", sk + "c"], ["lnd%d_%d" % (t + 1, c), "turn"], CFG["REM"], None, "rem", ("art%d" % sx, n_in, n_out))
         else:
-            for j, (dst, a, mul, add, k) in enumerate(((T.yc, 128, 1.0 / 16, 0.0, "c"), (T.yl, 64, 1.0, 2048.0, "l"), (T.ya, 0, 1.0, 2048.0, "a"))):
-                ts(T.fin[:, 3 * c + j, :], T.snd[:, so, a:a + 64], mul, add, OP.mult, OP.add, [sk + k], ["fin%d" % (3 * c + j)], CW)
+            for j, (dst, src, mul, add, k) in enumerate(((T.yc, T.snd[:, sx, 128:192], 1.0 / 16, 0.0, sk + "c"), (T.yl, Ln, 1.0, 2048.0, sk + "l"),
+                                                         (T.ya, so[:, 2:256:4], 1.0, 2048.0, "so" + n))):
+                ts(T.fin[:, 3 * c + j, :], src, mul, add, OP.mult, OP.add, [k], ["fin%d" % (3 * c + j)], CW)
                 dma("s", dst[:, 64 * c:64 * c + 64], T.fin[:, 3 * c + j, :], ["fin%d" % (3 * c + j)], [], 2400)
-        pick(c, GF[c])
+        pick(c, CFG["GF"], lambda a, b: T["off" + n][:, a:b], "off" + n)
         rec = T["rec" + n]; mn = T["mn" + n]
-        mk = []
-        for a, b in ((0, 32), (32, 64)):
-            k = units("mn" + n, a, b)
-            scan(mn[:, 16 * a:16 * b], T.keepT[:, :], rec[:, 16 * a:16 * b], OP.mult, OP.max, units("rec" + n, a, b) + ["keepT"], k, 16 * (b - a), 0.5)
-            mk += k
-        mms(bh, [(pH[:, 5, :], mats["BI"], z[:, :], ["BI", "z" + n], "zt" + n, 64),
-                 (pH[:, 5, :], mats["BI"], mn[:, 15:1024:16], ["BI"] + mk, "zt" + n, 64)])
-        ts(av[:, :], pH[:, 5, :], 0.5 / 131072, -0.25, OP.mult, OP.add, ["zt" + n], ["av" + n], CW, 1.0, bh)
-        ts(T.qw[:, 0, 4 * c:4 * c + 4], uq, 15, None, OP.bitwise_and, None, ["u" + n], ["q4" + n], 4)
-        cc = [c] if t == VIS - 1 else list(range(NCH)) if c == NCH - 1 else []
-        if cc:
-            a, b = 4 * cc[0], 4 * cc[-1] + 4
-            tt(T.qw[:, 1, a:b], T.qw[:, 0, a:b], T.qc[:, 8 + a:8 + b], OP.add, ["q4%d" % x for x in cc] + ["qc"], ["q5%d" % x for x in cc], 8)
-            cp(T.ow[:, a:b], T.qw[:, 1, a:b], ["q5%d" % x for x in cc], ["ow%d" % x for x in cc], 8)
+        for a, b in PH:
+            scan(mn[:, 16 * a:16 * b], T.keepT[:, :], rec[:, 16 * a:16 * b], OP.mult, OP.max, units("rec" + n, a, b) + ["keepT"], units("mn" + n, a, b), 16 * (b - a), 0.5)
+        group(bh, "zt" + n, [[(pH[:, 192:256], mats["Ib"], z[:, :], ["Ib", "z" + n], 64),
+                              (pH[:, 192:256], mats["Ib"], mn[:, 15:1024:16], ["Ib"] + units("mn" + n, 0, 64), 64)]])
+        ts(av[:, :], pH[:, 192:256], 0.5, -0.25, OP.mult, OP.add, ["zt" + n], ["av" + n], CW, 1.0, bh)
+        a, b = 4 * c, 4 * c + 4
+        bits(T.qw[:, 0, a:b], q[:, 0, :], 0, 15, ["q0" + n], ["q4" + n], 4)
+        tt(T.qw[:, 1, a:b], T.qw[:, 0, a:b], T.qc[:, 8 + a:8 + b], OP.add, ["q4" + n, "qc"], ["q5" + n], 4)
+        cp(T.ow[:, a:b], T.qw[:, 1, a:b], ["q5" + n], ["ow" + n], 4)
 
     def write(t, c):
         n = str(c)
-        tab, k = (T.X, "X" + n) if t < VIS - 1 else (T.Xo, "Xo" + n)
-        op("v", lambda: V.tensor_copy(tab[:, 1024 * c:1024 * c + 1024].indirect(T.ow[:, 4 * c:4 * c + 4]), T["av" + n][:, :]),
+        tab_, k = (T.X, "X" + n) if t < VIS - 1 else (T.Xo, "Xo" + n)
+        op("v", lambda: V.tensor_copy(tab_[:, 1024 * c:1024 * c + 1024].indirect(T.ow[:, 4 * c:4 * c + 4]), T["av" + n][:, :]),
            ["ow" + n, "av" + n, k], [k], 60 + 3.8 * 64)
         if t == VIS - 1:
             dma("s" if c == 0 else "a", T.yx[:, 1024 * c:1024 * c + 1024], T.Xo[:, 1024 * c:1024 * c + 1024], [k], [], 3000)
 
+    limit()
+    for c in range(NCH):
+        n = str(c); tl, tk = tile_of(0, c); f = T["f" + n]; ib = T["i" + n]; cs_ = slice(64 * c, 64 * c + 64)
+        ts(tl(0, 64), T.agi[:, cs_], -2048.0, None, OP.add, None, ["agi"], [tk + "a"], CW)
+        ts(f[:, 0, :], T.lti[:, cs_], 1184.0, None, OP.add, None, ["lti"], ["f0" + n], CW)
+        ts(f[:, 1, :], T.lti[:, cs_], -2048.0, 2080.0, OP.add, OP.mult, ["lti"], ["mL" + n], CW)
+        tt(f[:, 2, :], f[:, 0, :], tl(0, 64), OP.mult, ["f0" + n, tk + "a"], ["vb" + n], CW)
+        tt(ib[:, 0, :], f[:, 2, :], f[:, 1, :], OP.add, ["vb" + n, "mL" + n], ["u0" + n], CW)
+        bits(ib[:, 1, :], ib[:, 0, :], 5, 2047, ["u0" + n], ["pl" + n], CW)
+        cp(T["off" + n][:, :], ib[:, 1, :], ["pl" + n], ["off" + n], CW)
+        ts(tl(64, 128), T.lti[:, cs_], -2048.0, None, OP.add, None, ["lti"], [tk + "l"], CW)
+        ts(tl(128, 192), T.csi[:, cs_], 16.0, None, OP.mult, None, ["csi", tk + "l", tk + "a"], [tk], CW)
     for t in range(VIS):
         for c in range(NCH):
-            tl, tk = tile_of(t, c)
-            if t == 0:
-                cs_ = slice(64 * c, 64 * c + 64)
-                ts(tl(0, 64), T.agi[:, cs_], -2048.0, None, OP.add, None, ["agi"], [tk + "a"], CW)
-                ts(tl(64, 128), T.lti[:, cs_], -2048.0, None, OP.add, None, ["lti", tk + "a"], [tk + "l"], CW)
-                mms("U%d" % c, lw(c, 0, tl(64, 128), tk + "l"))
-                place(c, tl(0, 64), tk + "a", False)
-                ts(tl(128, 192), T.csi[:, cs_], 16.0, None, OP.mult, None, ["csi", tk + "l", tk + "a"], [tk], CW)
-            else:
-                mms("U%d" % c, lw(c, 0, tl(64, 128), tk))
-                place(c, tl(0, 64), tk, False)
-            pairs(c, 0, tl(0, 64), tk, tl(128, 192), tk)
+            begin(t, c)
         if t == VIS - 1:
             for c in range(NCH):
                 dma("s", T.Xo[:, 1024 * c:1024 * c + 1024], T.X[:, 1024 * c:1024 * c + 1024], ["X%d" % c], ["Xo%d" % c], 3000)
@@ -485,7 +533,9 @@ def build_ops(g, core, T, topo, rank):
             for c in range(NCH):
                 step(t, s, c)
             if not (t == VIS - 1 and s == 2):
-                count(s)
+                count()
+            if t == 0 and s == 0:
+                late_constants()
         for c in range(NCH):
             refill(t, c)
         for c in range(NCH):
@@ -495,7 +545,9 @@ def build_ops(g, core, T, topo, rank):
 
 def schedule(ops):
     n = len(ops)
+    LAT, FAC, SLACK, FRAC = CFG["LAT"], CFG["FAC"], CFG["SLACK"], CFG["FRAC"]
     lastw = {}; readers = {}; lastb = {}
+    deps = []
     for i, o in enumerate(ops):
         dep = {}
         for k in o["r"]:
@@ -503,7 +555,7 @@ def schedule(ops):
                 dep[lastw[k]] = "raw"
         for k in o["w"]:
             if k in lastw:
-                dep.setdefault(lastw[k], "ord" if o["kind"] == "mm" else "raw")
+                dep.setdefault(lastw[k], "ord" if o["kind"] == "mm" or k.startswith("turn") else "raw")
             for j in readers.get(k, ()):
                 if j != i:
                     dep.setdefault(j, "raw")
@@ -515,28 +567,21 @@ def schedule(ops):
             readers.setdefault(k, []).append(i)
         for k in o["w"]:
             lastw[k] = i; readers[k] = []
-        o["dep"] = dep
+        deps.append(dep)
 
     def waits(i, j):
-        a, b = ops[j], ops[i]
-        return a["e"] != b["e"] or a["kind"] in ("dma", "rem") or ops[i]["dep"][j] == "raw"
+        return ops[j]["e"] != ops[i]["e"] or deps[i][j] == "raw"
 
     succ = [[] for _ in range(n)]
-    for i, o in enumerate(ops):
-        for j in o["dep"]:
+    for i in range(n):
+        for j in deps[i]:
             succ[j].append(i)
+    dur = [o["d"] * (FAC if o["kind"] in ("c", "mm") else 1.0) for o in ops]
+    occ = [{"dma": 80.0, "rem": 500.0}.get(o["kind"], dur[i]) for i, o in enumerate(ops)]
     pr = [0.0] * n
-    for o in ops:
-        o["d0"] = o["d"]
-        if o["kind"] in ("c", "mm"):
-            o["d"] = o["d"] * FAC + (FIX if o["kind"] == "c" else PFIX)
-
-    def lat(k, i):
-        return LATS if ops[k]["e"] == ops[i]["e"] else LAT
-
     for i in range(n - 1, -1, -1):
-        pr[i] = ops[i]["d"] + max([pr[k] + (lat(k, i) if waits(k, i) else 0.0) for k in succ[i]] + [0.0])
-    left = [len(o["dep"]) for o in ops]
+        pr[i] = max([dur[i]] + [pr[k] + (dur[i] + LAT if waits(k, i) else occ[i]) for k in succ[i]])
+    left = [len(d) for d in deps]
     rdy = [0.0] * n
     end = [0.0] * n
     free = {e: 0.0 for e in "vapgs"}
@@ -551,33 +596,30 @@ def schedule(ops):
             if not lst:
                 continue
             t0 = max(free[e], min(rdy[i] for i in lst))
-            i = max((k for k in lst if rdy[k] <= t0 + SLACK), key=lambda k: (pr[k], -k))
-            i = max((k for k in lst if rdy[k] <= t0 + max(SLACK, FRAC * ops[i]["d"])), key=lambda k: (pr[k], -k))
-            st = max(t0, rdy[i])
             if best is None or t0 < best[0]:
-                best = (t0, i, st)
-        _, i, st = best
-        o = ops[i]; e = o["e"]
-        cand[e].remove(i)
-        occ = {"dma": 80.0, "rem": 600.0}.get(o["kind"], o["d"])
-        free[e] = st + occ
-        end[i] = st + o["d"]
-        o["t0"] = st
+                best = (t0, e)
+        t0, e = best
+        lst = cand[e]
+        i = max((k for k in lst if rdy[k] <= t0 + SLACK), key=lambda k: (pr[k], -k))
+        i = max((k for k in lst if rdy[k] <= t0 + max(SLACK, FRAC * occ[i])), key=lambda k: (pr[k], -k))
+        st = max(t0, rdy[i])
+        lst.remove(i)
+        free[e] = st + occ[i]
+        end[i] = st + dur[i]
         order.append(i)
         for k in succ[i]:
-            rdy[k] = max(rdy[k], end[i] + lat(k, i) if waits(k, i) else st)
+            rdy[k] = max(rdy[k], end[i] + LAT if waits(k, i) else st)
             left[k] -= 1
             if left[k] == 0:
                 cand[ops[k]["e"]].append(k)
     pos = {}; cnt = {e: 0 for e in "vapgs"}
     know = {e: ({x: -1 for x in "vapg"}, set()) for e in "vapgs"}
-    snap = {}
+    snap = {}; wait = {}
     for i in order:
         o = ops[i]; e = o["e"]
         kc, kd = know[e]
         need = []
-        ds = sorted((j for j in o["dep"] if waits(i, j)), key=lambda j: -end[j])
-        for j in ds:
+        for j in sorted((j for j in deps[i] if waits(i, j)), key=lambda j: -end[j]):
             a = ops[j]
             if a["kind"] in ("dma", "rem"):
                 if j in kd:
@@ -593,19 +635,14 @@ def schedule(ops):
                 for x in sc:
                     kc[x] = max(kc[x], sc[x])
                 kd.update(sd)
-        o["wait"] = need
+        wait[i] = need
         if o["kind"] not in ("dma", "rem"):
             pos[i] = cnt[e]; cnt[e] += 1
         snap[i] = (dict(kc), set(kd))
-    return order, max(end)
+    return order, wait, max(end)
 
 
-SLACK = 50.0
-FRAC = 0.3
-LATS = 200.0
-FAC = 1.25
-FIX = 20.0
-PFIX = 5.0
+PLAN = {}
 
 
 def rank_program(g, core, T, topo):
@@ -613,15 +650,17 @@ def rank_program(g, core, T, topo):
     if rank is None:
         return
     ops = build_ops(g, core, T, topo, rank)
-    order, _ = schedule(ops)
+    if "plan" not in PLAN:
+        PLAN["plan"] = schedule(ops)
+    order, wait, _ = PLAN["plan"]
     Q = {"v": g.vector, "a": g.scalar, "p": g.tensor, "g": g, "s": g.sync}
     wanted = set()
-    for o in ops:
-        wanted.update(o["wait"])
+    for i in order:
+        wanted.update(wait[i])
     sig = {}; cnt = {e: 0 for e in "vapg"}; nd = [0]; open_d = []; sent = 0
     for i in order:
         o = ops[i]; q = Q[o["e"]]
-        for j in o["wait"]:
+        for j in wait[i]:
             q.wait_ge(sig[j][0], sig[j][1])
         ins = o["fn"]()
         if o["kind"] == "dma":
@@ -631,8 +670,8 @@ def rank_program(g, core, T, topo):
             if i not in wanted:
                 open_d.append((o["e"], s))
         elif o["kind"] == "rem":
-            so, n_in, n_out = o["ext"]
-            sig[i] = (T.sem["arr%d" % so], n_in)
+            name, n_in, n_out = o["ext"]
+            sig[i] = (T.sem[name], n_in)
             sent += n_out
         elif i in wanted:
             cnt[o["e"]] += 1

@@ -12,13 +12,16 @@ U = "uint16"
 RND = 12582912.0
 
 CFG = {
-    "GP": (("a", 0, 32), ("a", 32, 64)),
-    "G0": (("a", 0, 32), ("a", 32, 64)),
-    "GF": (("a", 0, 32), ("a", 32, 64)),
+    "GP": (("a", 0, 32), ("v", 32, 40), ("a", 40, 64)),
+    "G0": (("a", 0, 32), ("v", 32, 48), ("a", 48, 64)),
+    "GF": ((("a", 0, 32), ("a", 32, 64)),) * 2,
+    "TS": (((0, 32), (32, 64)),) * 2,
     "SP": ((0, 32), (32, 64)),
     "CP": ((0, 32), (32, 64)),
-    "ZE": "v",
-    "LAT": 250.0, "FAC": 1.1, "GAM": 1.56, "PEC": 0.5, "SLACK": 60.0, "FRAC": 0.3, "REM": 3000.0,
+    "ZE": "a", "UE": "v", "U16": False,
+    "GA": 0, "SM": False, "PX2": 1.5, "TAB": True, "AFX": 100, "TP": 16, "RS": 0, "RUN": 4, "LAT": 280.0, "LATS": 320.0, "FAC": 1.0, "GAM": 1.4, "PEC": 0.35,
+    "PASSES": 10, "JIT": 100.0, "LAG": 2000.0, "MOVES": 800, "MK": 1, "BY": 1.5,
+    "FAC2": 1.35, "GX2": 1.1, "W2": 0.6, "REM": 2400.0,
 }
 PH = ((0, 32), (32, 64))
 
@@ -32,27 +35,29 @@ def _scratch():
 
     def sb(n, sh, d):
         s[n] = ("sbuf", [128] + list(sh), d)
-    sb("X", [2064], B); sb("Xo", [2048], B); sb("rbt", [1024], I)
+    sb("X", [2064], B); sb("Xo", [2048], B); sb("rbt", [1024], I); sb("rbf", [1024], F)
+    sb("IU", [4096], F); sb("TU", [2048], F); sb("TB", [2048], F); sb("tw", [3, 128], I); sb("to", [2, 128], U)
     sb("lti", [128], I); sb("agi", [128], I); sb("csi", [128], I); sb("thi", [128], I)
     sb("Fi", [2, 128], I); sb("Fh", [2, 128], H); sb("pi", [28], I); sb("pf", [36], F)
-    sb("mh", [30, 128], H); sb("mb", [6, 128], B); sb("IB", [192], B)
+    sb("mh", [30, 128], H); sb("mb", [7, 128], B); sb("IB", [192], B)
     sb("tab", [5, 128], B); sb("gF2", [16], B); sb("gs", [24], B)
     sb("selw", [144], B); sb("keepT", [512], B); sb("edge", [2, 128], B); sb("rs2", [128], B)
-    sb("c33", [128], B); sb("cR", [1024], B); sb("cev", [128], B); sb("mk", [64], H)
-    sb("thR", [128], H); sb("thf", [128], F); sb("thx", [128], H)
-    sb("t32", [8], F); sb("qc", [16], F); sb("a31", [8], B); sb("dc", [8], F); sb("du", [32], F)
+    sb("c33", [2, 128], B); sb("cR", [320], B); sb("c2", [704], B); sb("w2", [128], B); sb("cn", [4], B); sb("cev", [128], B); sb("mk", [64], H); sb("G16", [128], B)
+    sb("thR", [128], H); sb("thf", [128], H); sb("thx", [128], H)
+    sb("t32", [8], F); sb("cu", [192], F); sb("a31", [8], B); sb("dc", [8], F); sb("du", [128], F)
+    sb("z", [128], B); sb("av", [128], B); sb("avi", [128], I); sb("rw", [64], F); sb("qn", [4, 8], I); sb("on", [16], U); sb("nv", [2, 128], F)
     sb("tile0", [2, 192], H); sb("lnd", [8, 192], H); sb("snd", [10, 192], H)
     sb("lno", [8, 64], U); sb("sno", [8, 64], U)
-    sb("fin", [6, 64], F); sb("qw", [2, 8], I); sb("ow", [8], U)
+    sb("fin", [6, 64], F); sb("qw", [8], F); sb("ow", [8], U)
     for c in range(NCH):
         n = str(c)
         sb("rec" + n, [1024], B); sb("mn" + n, [1024], B); sb("cl" + n, [128], B)
-        sb("Bk" + n, [2, 128], F); sb("ohT" + n, [128], B); sb("oh2" + n, [128], B); sb("hT" + n, [128], B)
+        sb("Bk" + n, [128], F); sb("Cs" + n, [128], B); sb("ohT" + n, [128], B); sb("oh2" + n, [128], B); sb("hT" + n, [128], B)
         sb("hi" + n, [128], H); sb("y" + n, [3, 192], H); sb("eq" + n, [64], B)
         sb("d3" + n, [576], F); sb("d4" + n, [256], I); sb("so" + n, [256], I); sb("an" + n, [64], H)
         sb("f" + n, [5, 64], F); sb("i" + n, [4, 64], I); sb("off" + n, [64], U)
-        sb("yq" + n, [2, 64], H); sb("offq" + n, [8], U); sb("z" + n, [64], B)
-        sb("q" + n, [4, 4], I); sb("r5" + n, [32], F); sb("nw" + n, [2, 64], B); sb("av" + n, [64], I)
+        sb("yq" + n, [2, 64], H); sb("offq" + n, [8], U)
+        sb("q" + n, [4, 4], I); sb("r5" + n, [32], F); sb("nw" + n, [2, 64], B)
         s["pK" + n] = ("psum", [128, 512], F)
         s["pO" + n] = ("psum", [128, 512], F)
         s["pU" + n] = ("psum", [128, 512], F)
@@ -70,9 +75,15 @@ def build_ops(g, core, T, topo, rank):
     ops = []
     V, A, PE = g.vector, g.scalar, g.tensor
     GAM = CFG["GAM"]
+    at = ["start", 0]
 
     def op(e, fn, r, w, d, bank=None, kind="c", ext=None):
-        ops.append({"e": e, "fn": fn, "r": list(r), "w": list(w), "d": float(d), "bank": bank, "kind": kind, "ext": ext})
+        at[1] += 1
+        ops.append({"e": e, "fn": fn, "r": list(r), "w": list(w), "d": float(d), "bank": bank, "kind": kind, "ext": ext, "cls": tuple(at)})
+
+    def phase(fn, name, *args):
+        at[0], at[1] = name, 0
+        fn(*args)
 
     def vt(n, rate=1.0):
         return max(64.0, n * rate)
@@ -102,7 +113,7 @@ def build_ops(g, core, T, topo, rank):
             ts(out, in0, mask, None, OP.bitwise_and, None, r, w, n)
 
     def act(out, in_, fn, bias, scale, r, w, n, bank=None):
-        op("a", lambda: A.activation(out, in_, fn, bias=bias, scale=scale), r, w, 80 + n, bank)
+        op("a", lambda: A.activation(out, in_, fn, bias=bias, scale=scale), r, w, CFG["AFX"] + n, bank)
 
     def iota(out, pat, base, cm, w, n, fl=False):
         if fl:
@@ -110,8 +121,11 @@ def build_ops(g, core, T, topo, rank):
         else:
             op("g", lambda: g.iota(out, pat, base, cm), [], w, 160 + 2 * n)
 
+    def gcopy(out, in_, r, w, n):
+        op("g", lambda: g.affine_select(out, in_, [[0, n]], OP.is_ge, 0.0, 0, 0), r, w, 205 + 2 * n)
+
     def group(bank, key, runs):
-        runs = [x for x in runs if x]
+        runs = [x[k:k + CFG["RUN"]] for x in runs for k in range(0, len(x), CFG["RUN"])]
         for j, run in enumerate(runs):
             def fn(run=run, a=(j == 0), b=(j == len(runs) - 1)):
                 ins = None
@@ -129,9 +143,9 @@ def build_ops(g, core, T, topo, rank):
 
     def gather(e, out, win, off, r, w, n):
         if e == "a":
-            op("a", lambda: A.activation(out, win.indirect(off), AF.Copy), r, w, 80 + GAM * n)
+            op("a", lambda: A.activation(out, win.indirect(off), AF.Copy), r, w, 80 + GAM * n, None, "c", "pick")
         else:
-            op("v", lambda: V.tensor_copy(out, win.indirect(off)), r, w, 60 + GAM * n)
+            op("v", lambda: V.tensor_copy(out, win.indirect(off)), r, w, 60 + GAM * n, None, "c", "pick")
 
     dma("s", T.lti[:], T.lt[:], [], ["lti"], 2400)
     dma("a", T.agi[:], T.ag[:], [], ["agi"], 2400)
@@ -156,7 +170,6 @@ def build_ops(g, core, T, topo, rank):
         cp(T.Fh[:, o - 1, :], T.Fi[:, o - 1, :], ["Fi%d" % o], ["Fh%d" % o], 128)
     iota(tab[:, 3, :], [[1, 8], [0, 8], [-100, 2]], 100, 0, ["gF1"], 128, True)
     iota(tab[:, 4, :], [[1, 8], [0, 8], [100, 2]], 0, 0, ["gF2"], 128, True)
-    iota(T.qc[:, 0:8], [[0, 2], [256, 4]], 0, 0, ["qc0"], 8, True)
     iota(T.t32[:, 0:4], [[32, 4]], 32, 0, ["t32a"], 4, True)
     cp(pf[:, 20:21], P[:, 0:1], ["pa"], ["pcol"], 1)
     bits(P[:, 21:22], P[:, 0:1], 4, 7, ["pa"], ["p21"], 1)
@@ -176,7 +189,6 @@ def build_ops(g, core, T, topo, rank):
     ts(pf[:, 28:29], kcol, 2.0, 1.0, OP.mult, OP.add, ["pfa"], ["wcol"], 1)
     ts(pf[:, 29:30], kcol, 16.0, None, OP.mult, None, ["pfa"], ["k16"], 1)
     ts(pf[:, 30:31], pf[:, 23:24], -1.0, 1.0, OP.mult, OP.add, ["pfa"], ["evc"], 1)
-    ts(T.qc[:, 8:16], T.qc[:, 0:8], pf[:, 29:30], None, OP.add, None, ["qc0", "k16"], ["qc"], 8)
     ts(T.t32[:, 4:8], T.t32[:, 0:4], pf[:, 30:31], None, OP.mult, None, ["t32a", "evc"], ["t32"], 4)
 
     slots = {"h": [0], "b": [0]}
@@ -192,6 +204,9 @@ def build_ops(g, core, T, topo, rank):
     def pick1(name, kind, table, tkey, col, ckey, scale):
         ts(slot(name, kind), table, col, scale, OP.is_equal, OP.mult, [tkey, ckey], [name], 128, 0.5)
 
+    def diagonal(name, src, skey, v):
+        op("g", lambda: g.affine_select(mats[name], src, [[-1, 128]], OP.not_equal, v, 0, 1), [skey], [name], 461)
+
     def shift(name, j, scale):
         pick1(name, "h", tab[:, 0, :], "h0", pf[:, j & 15:(j & 15) + 1], "shf", scale)
 
@@ -206,20 +221,21 @@ def build_ops(g, core, T, topo, rank):
         pick1("PS%d" % o, "h", tab[:, 0, :], "h0", pf[:, 15 + 2 * o:16 + 2 * o], "shr", 1.0)
     for s in range(3):
         shift("Sh%d" % s, -SH[s], 1.0)
-        tt(slot("nIS%d" % s, "h"), mats["nI"], mats["Sh%d" % s], OP.subtract, ["nI", "Sh%d" % s], ["nIS%d" % s], 128)
-        tt(slot("D%d" % s, "h"), mats["nI"], mats["Sh%d" % s], OP.add, ["nI", "Sh%d" % s], ["D%d" % s], 128)
+        shift("nIS%d" % s, -SH[s], -1.0)
+        diagonal("nIS%d" % s, mats["nIS%d" % s], "nIS%d" % s, -1.0)
+        slot("D%d" % s, "h")
+        diagonal("D%d" % s, mats["Sh%d" % s], "Sh%d" % s, -1.0)
         shift("nSx%d" % s, SH[s], -1.0)
-    tmp = slot("tmp", "h")
-    for r, s in ((0, 1), (0, 2), (1, 2)):
-        nm = "PN%d%d" % (r, s)
-        shift(nm, SH[r], 64.0)
-        j = (SH[r] - SH[s]) & 15
-        ts(tmp, tab[:, 0, :], pf[:, j:j + 1], 64.0, OP.is_equal, OP.mult, ["h0", "shf"], ["tmp"], 128, 0.5)
-        tt(mats[nm], mats[nm], tmp, OP.add, [nm, "tmp"], [nm], 128)
+    shift("PN", SH[0], 64.0)
+    shift("PNb", SH[0] - SH[1], 64.0)
+    tt(mats["PN"], mats["PN"], mats["PNb"], OP.add, ["PN", "PNb"], ["PN"], 128)
+    j = -SH[2] & 15
+    pick1("PE", "b", tab[:, 0, :], "h0", pf[:, j:j + 1], "shf", 8192.0)
+    diagonal("PE", mats["PE"], "PE", 8192.0)
     pick1("G", "h", tab[:, 1, :], "gF0", gcol, "pfa", 1.0)
     pick1("nG", "h", tab[:, 1, :], "gF0", gcol, "pfa", -1.0)
     pick1("Godd", "h", tab[:, 3, :], "gF1", gcol, "pfa", 1.0)
-    for nm, v in (("Ib", 1.0), ("BI", 262144.0), ("I4k", 4096.0), ("nI4k", -4096.0), ("I16", 16.0)):
+    for nm, v in (("Ib", 1.0), ("BI", 262144.0), ("I4k", 4096.0), ("nI4k", -4096.0)):
         pick1(nm, "b", tab[:, 0, :], "h0", pcol, "pcol", v)
     ts(slot("Wev", "b"), tab[:, 4, :], gcol, pf[:, 28:29], OP.is_equal, OP.mult, ["gF2", "pfa", "wcol"], ["Wev"], 128, 0.5)
     for j, v in enumerate((4096.0, 4096.0, -8192.0)):
@@ -230,57 +246,75 @@ def build_ops(g, core, T, topo, rank):
     ts(T.selw[:, 15:143:16], T.gF2[:, 0:16:2], gcol, pf[:, 28:29], OP.is_equal, OP.mult, ["gF2b", "pfa", "wcol", "selw"], ["selw"], 8)
     ts(T.mk[:, :], tab[:, 2, 0:64], kcol, -4096.0, OP.not_equal, OP.mult, ["kk", "pfa"], ["mk"], 64)
     ts(T.thR[0:8, :], tab[0:8, 1, :], pf[0:8, 20:21], -32.0, OP.is_equal, OP.mult, ["gF0", "pcol"], ["thR"], 128, 0.5)
-    ms(T.keepT[:], 1.0, ["keepT"], 256)
-    ms(T.keepT[:, 0:512:16], 0.0, ["keepT"], 32)
+    ts(T.G16[0:8, :], tab[0:8, 1, :], pf[0:8, 20:21], 16.0, OP.is_equal, OP.mult, ["gF0", "pcol"], ["G16"], 128, 0.5)
+    ms(T.keepT[:, 0:128], 1.0, ["keepT"], 64)
+    ms(T.keepT[:, 0:128:16], 0.0, ["keepT"], 8)
+    iota(T.keepT[:, 128:512], [[0, 384]], 1, 0, ["keepW"], 384, True)
+    iota(T.keepT[:, 128:512:16], [[0, 24]], 0, 0, ["keepW"], 24, True)
     for j, v in enumerate((1.0e9, -1.0e9)):
         ms(T.edge[:, j, :], -v, ["edge%d" % j], 64)
         ms(T.edge[:, j, 0:128:16], v, ["edge%d" % j], 8)
-    ms(T.rs2[:], 0.0, ["rs2"], 64)
-    ms(T.rs2[:, 0:128:2], -1.0e6, ["rs2"], 64)
-    ms(T.c33[0:33, :], 1.0, ["c33"], 64)
-    ms(T.c33[32:33, :], 1024.0, ["c33"], 64)
-    cR = T.cR
-    ms(cR[0:33, :], 0.0, ["cR"], 512)
-    for s in range(3):
-        ts(cR[0:1, 128 * s:128 * s + 128], tab[0:1, 2, :], 2.0, 1.0, OP.mult, OP.add, ["kk", "cR"], ["cK%d" % s], 64)
-        ms(cR[32:33, 128 * s:128 * s + 128], -64.0 + 512.0 * s, ["cK%db" % s], 64, None, ["cR"])
-    ts(cR[0:1, 384:512], tab[0:1, 2, :], -1.0, 15.0, OP.mult, OP.add, ["kk", "cR"], ["cC"], 64)
-    for row, a, b, v, k in ((32, 384, 576, -12.0, "c12"), (0, 576, 640, 1.0, "cOa"), (0, 640, 704, -1.0, "cOb"),
-                            (32, 576, 704, -4.0, "cOc"), (32, 704, 768, 8.0, "cOd"), (32, 768, 832, -60.0, "c60"),
-                            (32, 832, 896, -4.0, "c4"), (0, 896, 960, -16.0, "cEa"), (32, 896, 960, -6.0, "cEb"),
-                            (0, 960, 1024, 1.0, "c1")):
-        ms(cR[row:row + 1, a:b], v, [k], 64, None, ["cR"])
-    ms(T.cev[0:1, :], 0.0, ["cev"], 64)
-    ms(T.cev[0:1, 0:128:2], -2048.0, ["cev"], 64)
+    iota(T.rs2[:, :], [[0, 64], [30000, 2]], -30000, 0, ["rs2"], 128, True)
+    iota(T.cev[0:1, :], [[0, 64], [2048, 2]], -2048, 0, ["cev"], 128, True)
+    cR = T.cR; rows = {}
+    ms(T.c33[0:1, 0, :], 1.0, ["c1"], 64)
+    ms(T.c33[0:1, 1, :], 1024.0, ["c1k"], 64)
+    for j, v in enumerate((-60, -4, -12, -8, -6)):
+        rows[v] = 64 * j
+        iota(cR[0:1, 64 * j:64 * j + 64], [[0, 64]], v, 0, ["row%d" % v], 64, True)
 
-    def const(out, m, a, b, keys):
-        return (out, T.c33[0:33, 0:m], cR[0:33, a:b], ["c33", "cR"] + keys, max(64, b - a))
+    def const(out, m, v, n_):
+        return (out, T.c33[0:1, 1, 0:m], cR[0:1, rows[v]:rows[v] + n_], ["c1k", "row%d" % v], 64)
 
-    ms(T.dc[0:8, 0:5], 1.0, ["dc"], 8)
+    c2 = T.c2
+    ms(T.w2[0:33, :], 1.0, ["w2"], 64)
+    ms(T.w2[32:33, :], 1024.0, ["w2"], 64)
+    ms(c2[0:33, :], 0.0, ["c2"], 352)
+    for a, b, pat, base, k in ((0, 128, [[0, 8], [2, 16]], 1, "a"), (512, 640, [[-2, 2], [0, 64]], 1, "c"),
+                               (128, 256, [[0, 8], [2, 16]], 1, "f"), (384, 512, [[0, 8], [-1, 16]], 15, "h")):
+        op("g", lambda a=a, b=b, pat=pat, base=base: g.iota(c2[0:1, a:b], pat, base, 0, allow_small_or_imprecise_dtypes=True),
+           ["c2"], ["c2" + k], 160 + 2 * (b - a))
+    for a, b, v, k in ((0, 128, -64.0, ["c2b"]), (384, 640, -4.0, ["c2d", "c2i"]), (640, 704, 8.0, ["c2e"]), (128, 256, 448.0, ["c2g"])):
+        ms(c2[32:33, a:b], v, k, (b - a) // 2, None, ["c2"])
+
+    def const2(out, m, a, b, keys):
+        return (out, T.w2[0:33, 0:m], c2[0:33, a:b], ["w2"] + ["c2" + k for k in keys], b - a)
+
+    ms(T.dc[0:8, 0:6], 1.0, ["dc"], 8)
     for j, v in ((0, 0.0), (1, 1.0 / 32), (3, -32.0)):
         ms(T.dc[0:8, j:j + 1], v, ["dc"], 1)
-    ms(T.du[:], 1.0, ["du"], 32)
-    for j, v in ((0, 0.0), (2, 1.0 / 4096), (4, -4096.0)):
-        ms(T.du[:, j:32:8], v, ["du"], 4)
     for c in range(NCH):
         n = str(c)
-        ms(T["d3" + n][:, 0:576:3], 0.0, ["d3z" + n], 192)
-        ms(T["d4" + n][:], 0, ["d4z" + n, "d4x" + n, "d4n" + n, "d4l" + n], 256)
-    pA = T.pK1
-    for j, v in ((1, RND), (2, -RND), (4, 0.0)):
-        ms(pA[0:8, 288 + j:289 + j], v, ["cA"], 1, "K1")
-    ms(T.a31[0:8, :], -15.5, ["a31"], 8)
-    ts(T.thf[0:8, :], T.thi[0:8, :], -2048.0 + 15.5, None, OP.add, None, ["thi"], ["thf"], 128)
+        iota(T["d3" + n][:, 0:576:3], [[0, 192]], 0, 0, ["d3z" + n], 192, True)
+        ms(T["d4" + n][:, 0:256:2], 0, ["d4z" + n, "d4n" + n], 128)
+    pA = T.pO1
+    for j, v in ((1, RND), (2, -RND), (4, 0.0), (5, 15.5)):
+        ms(pA[0:8, 288 + j:289 + j], v, ["cA"], 1, "O1")
+    ms(T.a31[0:8, 0:5], -15.5, ["a31"], 8)
+    ms(T.a31[0:8, 5:6], 0.0, ["a31"], 1)
+    ts(T.thf[0:8, :], T.thi[0:8, :], -2048.0, None, OP.add, None, ["thi"], ["thf"], 128)
 
     def late_constants():
-        for c in range(NCH):
-            n = str(c); pK = T["pK" + n]
-            ms(pK[:, 256:288], 0.0, ["cu" + n], 32, "K" + n)
-            for j, v in ((1, -2047.5), (2, RND), (3, -RND), (4, -2048.0), (5, 5280.0)):
-                ms(pK[:, 256 + j:288:8], v, ["cu" + n], 4, "K" + n)
+        for a, b, st_, pat, base in ((0, 128, 1, [[0, 128]], 1), (0, 128, 8, [[0, 16]], 0), (1, 128, 8, [[0, 16]], 2), (4, 128, 8, [[4080, 2], [0, 8]], -4096)):
+            iota(T.du[:, a:b:st_], pat, base, 0, ["du"], (b - a) // st_, True)
+        for a, m in ((0, 4096.0), (64, 16.0)):
+            ms(T.du[:, a + 2:a + 64:8], 0.5 / m, ["du"], 8)
+        for a, b, st_, pat, base in ((0, 192, 1, [[0, 192]], 0), (1, 64, 8, [[4080, 2], [0, 4]], -4095), (65, 192, 8, [[4080, 2], [0, 8]], -4095),
+                                     (2, 192, 8, [[0, 24]], int(RND)), (3, 192, 8, [[0, 24]], -int(RND)), (4, 32, 8, [[0, 4]], -2048),
+                                     (68, 128, 8, [[0, 8]], -2048), (5, 32, 8, [[0, 4]], 5280), (69, 128, 8, [[0, 8]], 5280),
+                                     (36, 64, 8, [[256, 4]], 0), (132, 192, 8, [[256, 8]], 0)):
+            iota(T.cu[:, a:b:st_], pat, base, 0, ["cu"], (b - a) // st_, True)
+        for a, b in ((36, 64), (132, 192)):
+            ts(T.cu[:, a:b:8], T.cu[:, a:b:8], pf[:, 29:30], None, OP.add, None, ["cu", "k16"], ["cu"], 8)
+        cp(T.pK0[:, 256:320], T.cu[:, 0:64], ["cu"], ["cu0"], 64, 1.0, "K0")
+        cp(T.pK1[:, 256:448], T.cu[:, :], ["cu"], ["cu1"], 192, 1.0, "K1")
+        for j in range(4):
+            gcopy(T.rbf[:, 256 * j:256 * j + 256], T.rbt[:, 256 * j:256 * j + 256], ["rbt"], ["rbf"], 256)
+        for j in range(4):
+            iota(T.IU[:, 1024 * j:1024 * j + 1024], [[1, 1024]], 1024 * j, 0, ["IU%d" % j], 1024, True)
 
     def limit():
-        ts(T.thx[0:8, :], T.thf[0:8, :], T.a31[0:8, 3:4], 2047.0, OP.add, OP.min, ["thf", "a31"], ["thx"], 128)
+        ts(T.thx[0:8, :], T.thf[0:8, :], T.a31[0:8, 5:6], 2047.0, OP.add, OP.min, ["thf", "a31"], ["thx"], 128, 0.5)
 
     nxt = T.cores[(rank + 1) % len(T.cores)]
     rid, pid = topo.addr(nxt, core)
@@ -307,9 +341,9 @@ def build_ops(g, core, T, topo, rank):
     def best(c, o, oh, okey):
         n = str(c); pK = T["pK" + n]; Bk = T["Bk" + n]; kk = "key" + n
         j, other = (0, OP.max) if o == OP.min else (1, OP.min)
-        scan(Bk[0:64, 0, :], T.keepT[0:64, 0:128], pK[0:64, 0:128], OP.mult, o, [kk, "keepT"], ["Bk" + n], 128, 1.0, "K" + n)
+        scan(Bk[0:64, :], T.keepT[0:64, 0:128], pK[0:64, 0:128], OP.mult, o, [kk, "keepT"], ["Bk" + n], 128, 1.0, "K" + n)
         scan(pK[0:64, 255:127:-1], T.edge[0:64, j, :], pK[0:64, 127::-1], other, o, [kk, "edge%d" % j], ["Bs" + n], 128, 1.0, "K" + n)
-        tt(oh[0:64, :], pK[0:64, 128:256], Bk[0:64, 0, :], OP.is_equal, ["Bs" + n, "Bk" + n], [okey], 128, "K" + n)
+        tt(oh[0:64, :], pK[0:64, 128:256], Bk[0:64, :], OP.is_equal, ["Bs" + n, "Bk" + n], [okey], 128, "K" + n)
 
     def begin(t, c):
         n = str(c); tl, tk = tile_of(t, c); pU = T["pU" + n]
@@ -339,6 +373,14 @@ def build_ops(g, core, T, topo, rank):
             group(bh, "aj" + n, [[(pH[:, 1:128:2], mats["PS%d" % s], an[:, :], ["PS%d" % s, "an" + n], 64)]])
             scan(hi2[:, :], T.rs2[:, :], pH[:, 0:128], OP.add, OP.max, ["ak" + n, "aj" + n, "rs2"], ["hi" + n], 128, 1.0, bh)
         tt(eq[:, :], pH[:, 1:128:2], a_ap, OP.is_equal, ["aj" + n, ak], ["eq" + n], CW, bh)
+        if s == 2:
+            Cs = pH[:, 320:384]
+            group(bh, "Cn" + n, [[const(Cs, 128, -8, 64), (Cs, mats["I"], tl(128, 192), ["I", tk], 64)]
+                                 + [(Cs, mats["I"], y[:, r, 128:192], ["I", "yC%d" % r + n], 64) for r in range(2)]
+                                 + [(Cs, mats["nSx%d" % r], y[:, r, 64 * h:64 * h + 64], ["nSx%d" % r, ("yh%d", "y%d")[h] % r + n], 64)
+                                    for r in range(2) for h in range(2)]])
+            act(T["Cs" + n][:, 64:128], Cs, AF.Relu, 0.0, -1.0, ["Cn" + n], ["Es" + n], CW, bh)
+            act(T["Cs" + n][:, 0:64], Cs, AF.Identity, 0.0, 1.0, ["Cn" + n], ["Cs" + n], CW, bh)
         cyc = 16 if s < 2 else 8
         w_ = 16 // cyc
         for a, b in CFG["CP"]:
@@ -347,10 +389,10 @@ def build_ops(g, core, T, topo, rank):
             rk = units("rec" + n, a, b)
             scan(mn[:, 16 * a:16 * b - 1], rec[:, 16 * a:16 * b - 1], rec[:, 16 * a + 1:16 * b], OP.max, OP.min, rk, units("mn" + n, a, b), 16 * (b - a), 0.5)
         key = pK[0:64, 0:128]
-        runs = [[const(key, 64, 128 * s, 128 * s + 128, ["cK%d" % s, "cK%db" % s])]]
-        for r in range(s):
-            nm = "PN%d%d" % (r, s)
-            runs.append([(key, y[:, r, 64 * h:64 * h + 64], mats[nm], ["y%d" % r + n, nm], 128) for h in range(2)])
+        if s == 1:
+            runs = [[const2(key, 64, 128, 256, "fg")], [(key, y[:, 0, 64 * h:64 * h + 64], mats["PN"], [("yh0", "y0")[h] + n, "PN"], 128) for h in range(2)]]
+        else:
+            runs = [[const2(key, 64, 0, 128, "ab")]]
         sums = []
         for a, b in PH:
             rk = units("rec" + n, a, b); mk = units("mn" + n, a, b); ck = units("cl" + n, a, b)
@@ -364,88 +406,117 @@ def build_ops(g, core, T, topo, rank):
                 else:
                     two.append((pK[a:b, k:128:16], mn[:, 16 * a + p:16 * b:16], T.gs[:, 16:24], mk + ["Gm64"], b - a))
             sums.append((one, two))
-        runs += [sums[0][0], sums[0][1], [(key, eq[:, :], mats["BI"], ["eq" + n, "BI"], 128)], sums[1][0], sums[1][1],
-                 [(key, T.thx[0:8, 64 * c:64 * c + 64], T.thR[0:8, :], ["thx", "thR"], 128)]]
+        k = row_of(s, 0)
+        both = (pK[0:64, k:128:16], mn[:, 0:1024:16], T.gs[:, 16:24], units("mn" + n, 0, 64) + ["Gm64"], 64)
+        out = [(key, eq[:, :], mats["BI"], ["eq" + n, "BI"], 128)]
+        if s == 2:
+            out.append((key, T["Cs" + n][:, 64:128], mats["PE"], ["Es" + n, "PE"], 128))
+        lim = [(key, T.thx[0:8, 64 * c:64 * c + 64], T.thR[0:8, :], ["thx", "thR"], 128)]
+        if CFG["SM"]:
+            whole = [(pK[0:64, j:128:16], rec[:, p:1024:16], T.gs[:, 0:8], units("rec" + n, 0, 64) + ["G32"], 64)
+                     for p in range(16) for j in (row_of(s, p), (row_of(s, p) - SH[s]) & 15)]
+            runs += [sums[0][1][1:], out, lim, whole, sums[1][1][1:] + [both]]
+        else:
+            runs += [sums[0][0], sums[0][1][1:], out, sums[1][0], lim, sums[1][1][1:] + [both]]
         group("K" + n, "key" + n, runs)
         best(c, OP.min, ohT, "ohT" + n)
         cs_ = [(tl(128, 192), tk)] + [(y[:, r, 128:192], "yC%d" % r + n) for r in range(s)]
         group(bo, "yP" + n, [
-            [const(pO[:, 0:192], 128, 576, 768, ["cOa", "cOb", "cOc", "cOd"])],
+            [const2(pO[:, 0:192], 128, 512, 704, "cde")],
             [(pO[:, 128:192], mats["D%d" % s], d, ["D%d" % s, dk], 64) for d, dk in cs_],
             [(pO[:, 0:64], mats["I"], hi, ["I", "hi" + n], 64), (pO[:, 64:128], mats["I"], hi, ["I", "hi" + n], 64),
              (pO[:, 64:128], mats["nIS%d" % s], a_ap, ["nIS%d" % s, ak], 64)],
             [(pO[:, 0:192], ohT[0:64, :], T.IB[0:64, :], ["ohT" + n, "IB0", "IB1", "IB2"], 192)]])
         yk = "y%d" % s + n
-        late = [lambda: ts(y[:, s, 0:128], pO[:, 0:128], -2048.0, None, OP.max, None, ["yP" + n], [yk], 128, 1.0, bo),
-                lambda: ts(y[:, s, 128:192], pO[:, 128:192], 0.0, None, OP.min, None, ["yP" + n], ["yC%d" % s + n], 64, 1.0, bo)]
-        for fn in late:
-            fn()
+        yh = "yh%d" % s + n
+        ts(y[:, s, 0:64], pO[:, 0:64], -2048.0, None, OP.max, None, ["yP" + n], [yh], CW, 1.0, bo)
+        ts(y[:, s, 64:128], pO[:, 64:128], -2048.0, None, OP.max, None, ["yP" + n], [yk], CW, 1.0, bo)
+        ts(y[:, s, 128:192], pO[:, 128:192], 0.0, None, OP.min, None, ["yP" + n], ["yC%d" % s + n], CW, 1.0, bo)
         nb = (s + 1) % 3
         pn = "P%d" % nb; pk = pn if nb else "I"
         group(bu, "ua" + n, [[(pU[:, 1:192:3], mats[pn], a_ap, [pk, ak], 64)]])
         group(bu, "uw" + n, [[(pU[:, 2:192:3], mats["W%d" % nb], tl(64, 128), ["W%d" % nb, tk], 64)]])
         group(bh, "E" + n, [[(pH[:, 128:192], mats[pn], a_ap, [pk, ak], 64)],
-                            [(pH[:, 128:192], mats["nG"], y[:, s, 0:64], ["nG", yk], 64)]])
-        group(bu, "ud" + n, [[const(pU[:, 0:192:3], 128, 768, 832, ["c60"])],
-                             [(pU[:, 0:192:3], mats["nG"], y[:, s, 64 * h:64 * h + 64], ["nG", yk], 64) for h in range(2)]])
+                            [(pH[:, 128:192], mats["nG"], y[:, s, 0:64], ["nG", yh], 64)]])
+        group(bu, "ud" + n, [[const(pU[:, 0:192:3], 128, -60, 64)],
+                             [(pU[:, 0:192:3], mats["nG"], y[:, s, 64 * h:64 * h + 64], ["nG", yh, yk], 64) for h in range(2)]])
         ts(d3[:, 192 * s + 1:192 * s + 192:3], pH[:, 128:192], 30719.0, None, OP.is_equal, None, ["E" + n], ["e%d" % s + n], CW, 1.0, bh)
         scan(so[:, 0:192], d3[:, 192 * s:192 * s + 192], pU[:, 0:192], OP.mult, OP.add,
              ["e%d" % s + n, "d3z" + n, "d3l" + n, "ua" + n, "uw" + n, "ud" + n], ["so" + n], 192, 1.0, bu)
-        bits(ib[:, 1, :], so[:, 2:192:3], 5, 2047, ["so" + n], ["pl" + n], CW)
-        if s < 2:
-            cp(T["off" + n][:, :], ib[:, 1, :], ["pl" + n], ["off" + n], CW)
-        cp(an[:, :], so[:, 1:192:3], ["so" + n], ["an" + n], CW)
+        if s < 2 and CFG["U16"]:
+            bits(T["off" + n][:, :], so[:, 2:192:3], 5, 2047, ["so" + n], ["off" + n], CW)
+        else:
+            bits(ib[:, 1, :], so[:, 2:192:3], 5, 2047, ["so" + n], ["pl" + n], CW)
+            if s < 2:
+                cp(T["off" + n][:, :], ib[:, 1, :], ["pl" + n], ["off" + n], CW)
+        (gcopy if s < CFG["GA"] else cp)(an[:, :], so[:, 1:192:3], ["so" + n], ["an" + n], CW)
 
     def count():
         out = pA[0:8, 288:292:3]
         runs = [[(out, mats["Ib8"], T.a31[0:8, 3:5], ["Ib", "a31"], 8)]
                 + [(out, T["ohT%d" % c][0:64, k:128:16], T.keepT[0:64, 1:3], ["ohT%d" % c, "keepT"], 8) for c in range(NCH) for k in range(16)]]
-        group("K1", "Ac", runs)
-        scan(T.a31[0:8, 0:5], T.dc[0:8, 0:5], pA[0:8, 288:293], OP.mult, OP.add, ["Ac", "cA", "dc"], ["a31"], 5, 1.0, "K1")
+        group("O1", "Ac", runs)
+        scan(T.a31[0:8, 0:6], T.dc[0:8, 0:6], pA[0:8, 288:294], OP.mult, OP.add, ["Ac", "cA", "dc"], ["a31"], 5, 1.0, "O1")
         limit()
+
+    def spot(c, z, zcol, zk):
+        n = str(c); pK = T["pK" + n]; pO = T["pO" + n]; q = T["q" + n]; r5 = T["r5" + n]; ib = T["i" + n]
+        bk, bo = "K" + n, "O" + n
+        S = pK[:, 256:288:8]
+        group(bk, "uQ" + n, [[(S, T.selw[:, 15 - r:143 - r], zcol(r), ["selw", zk], 64) for r in range(16)]])
+        scan(r5[:, :], T.du[:, 0:32], pK[:, 256:288], OP.mult, OP.add, ["uQ" + n, "cu" + n, "du"], ["r5" + n], 32, 1.0, bk)
+        tt(q[:, 0, :], S, r5[:, 4:32:8], OP.add, ["uQ" + n, "r5" + n], ["q0" + n], 4, bk)
+        group(bo, "uP" + n, [[(pO[:, 128:192], mats["Wev"], z, ["Wev", zk], 64)]])
+        tt(q[:, 1, :], S, r5[:, 5:32:8], OP.add, ["uQ" + n, "r5" + n], ["q1" + n], 4, bk)
+        tt(q[:, 2, :], q[:, 0, :], q[:, 1, :], OP.mult, ["q0" + n, "q1" + n], ["q2" + n], 4)
+        bits(q[:, 3, :], q[:, 2, :], 5, 1023, ["q2" + n], ["q3" + n], 4)
+        cp(T["offq" + n][:, 4:8], q[:, 3, :], ["q3" + n], ["on" + n], 4)
+        cp(ib[:, 0, :], pO[:, 128:192], ["uP" + n], ["u0" + n], CW, 1.0, bo)
+        bits(ib[:, 3, :], ib[:, 0, :], 0, 4095, ["u0" + n], ["u" + n], CW)
 
     def refill(t, c):
         n = str(c); tl, tk = tile_of(t, c)
         pK = T["pK" + n]; pO = T["pO" + n]; pU = T["pU" + n]; pH = T["pH" + n]
         y = T["y" + n]; f = T["f" + n]; an = T["an" + n]; ib = T["i" + n]; so = T["so" + n]; d4 = T["d4" + n]
         Bk = T["Bk" + n]; oh2 = T["oh2" + n]; hT = T["hT" + n]; yq = T["yq" + n]; oq = T["offq" + n]
-        z = T["z" + n]; q = T["q" + n]; nw = T["nw" + n]; av = T["av" + n]; r5 = T["r5" + n]
+        z = T.z[:, 64 * c:64 * c + 64]; nw = T["nw" + n]; av = T.av[:, 64 * c:64 * c + 64]; r5 = T["r5" + n]
+
+        def zcol(r):
+            return T.z[:, 64 * c + r:64 * c + 64:16]
         bk, bh, bo, bu = "K" + n, "H" + n, "O" + n, "U" + n
         a_ap, ak = an[:, :], "an" + n
         cost = [(tl(128, 192), tk, "I")] + [(y[:, r, 128:192], "yC%d" % r + n, "I") for r in range(3)]
-        emp = [(y[:, r, 64 * h:64 * h + 64], "y%d" % r + n, "nSx%d" % r) for r in range(3) for h in range(2)]
-        early = cost[0:3] + emp[0:4]; late = emp[4:6] + cost[3:4]
+        emp = [(y[:, r, 64 * h:64 * h + 64], ("yh%d", "y%d")[h] % r + n, "nSx%d" % r) for r in range(3) for h in range(2)]
+        early = [(T["Cs" + n][:, 0:64], "Cs" + n, "Ib")]; late = emp[4:6] + cost[3:4]
         key = pK[0:64, 0:128]
-        group(bk, "key" + n, [[const(key, 64, 384, 512, ["cC", "c12"])] + [(key, d, mats[m], [dk, m], 128) for d, dk, m in early],
+        group(bk, "key" + n, [[const2(key, 64, 384, 512, "hi")] + [(key, d, mats[m], [dk, m], 128) for d, dk, m in early],
                               [(key, d, mats[m], [dk, m], 128) for d, dk, m in late]])
         best(c, OP.max, oh2, "oh2" + n)
-        tt(Bk[0:64, 1, :], pK[0:64, 128:256], Bk[0:64, 0, :], OP.max, ["Bs" + n, "Bk" + n], ["Bb" + n], 128, bk)
-        act(hT[0:64, :], Bk[0:64, 1, :], AF.Identity, 128.515625, 1.0 / 32, ["Bb" + n], ["hT" + n], 128)
-        group(bh, "emp" + n, [[const(pH[:, 256:320], 128, 512, 576, ["c12"])] + [(pH[:, 256:320], mats[m], d, [dk, m], 64) for d, dk, m in emp[0:4]],
+        act(hT[0:64, 0:8], Bk[0:64, 15:128:16], AF.Identity, 128.515625, 1.0 / 32, ["Bk" + n], ["hT" + n], 8)
+        group(bh, "emp" + n, [[const(pH[:, 256:320], 128, -12, 64)] + [(pH[:, 256:320], mats[m], d, [dk, m], 64) for d, dk, m in emp[0:4]],
                               [(pH[:, 256:320], mats[m], d, [dk, m], 64) for d, dk, m in emp[4:6]]])
         tt(f[:, 3, :], ib[:, 1, :], pH[:, 256:320], OP.subtract, ["pl" + n, "emp" + n], ["pl2" + n], CW, bh)
         ts(T["off" + n][:, :], f[:, 3, :], 2048.0, None, OP.min, None, ["pl2" + n], ["off" + n], CW)
         group(bo, "oN" + n, [[(pO[:, 0:64], oh2[0:64, :], mats["Ib64"], ["oh2" + n, "Ib"], 64)]])
         tt(yq[:, 0, :], pO[:, 0:64], ib[:, 1, :], OP.mult, ["oN" + n, "pl" + n], ["yq" + n], CW, bo)
         tt(yq[:, 1, :], pO[:, 0:64], a_ap, OP.mult, ["oN" + n, ak], ["ya" + n], CW, bo)
+        group(bo, "hP" + n, [[(pO[0:8, 192:256], hT[0:64, 0:8], mats["Ib64"], ["hT" + n, "Ib"], 64)]])
+        act(hT[0:8, 64:128], pO[0:8, 192:256], AF.Identity, -1.0, 1.0, ["hP" + n], ["hB" + n], CW, bo)
         group(bu, "Qp" + n, [[(pU[:, 448:512], mats["I"], T.mk[:, :], ["I", "mk"], 64)],
                              [(pU[:, 448:512], mats["G"], yq[:, 0, :], ["G", "yq" + n], 64)]])
         scan(f[:, 4, :], T.keepT[:, 0:64], pU[:, 448:512], OP.mult, OP.max, ["Qp" + n, "keepT"], ["Qs" + n], CW, 1.0, bu)
         cp(oq[:, 0:4], f[:, 4, 15:64:16], ["Qs" + n], ["oz" + n], 4)
-        gather(CFG["ZE"], z[:, :], XW, oq[:, 0:4], XK + ["oz" + n], ["z" + n], 64)
-        S = pK[:, 256:288:8]
-        group(bk, "uQ" + n, [[(S, T.selw[:, 15 - r:143 - r], z[:, r:64:16], ["selw", "z" + n], 64) for r in range(16)]])
-        group(bo, "uP" + n, [[(pO[:, 128:192], mats["Wev"], z[:, :], ["Wev", "z" + n], 64)]])
-        scan(r5[:, :], T.du[:, :], pK[:, 256:288], OP.mult, OP.add, ["uQ" + n, "cu" + n, "du"], ["r5" + n], 32, 1.0, bk)
-        tt(q[:, 0, :], S, r5[:, 4:32:8], OP.add, ["uQ" + n, "r5" + n], ["q0" + n], 4, bk)
-        tt(q[:, 1, :], S, r5[:, 5:32:8], OP.add, ["uQ" + n, "r5" + n], ["q1" + n], 4, bk)
-        tt(q[:, 2, :], q[:, 0, :], q[:, 1, :], OP.mult, ["q0" + n, "q1" + n], ["q2" + n], 4)
-        bits(q[:, 3, :], q[:, 2, :], 5, 1023, ["q2" + n], ["q3" + n], 4)
-        cp(oq[:, 4:8], q[:, 3, :], ["q3" + n], ["on" + n], 4)
-        cp(ib[:, 0, :], pO[:, 128:192], ["uP" + n], ["u0" + n], CW, 1.0, bo)
-        bits(ib[:, 3, :], ib[:, 0, :], 0, 4095, ["u0" + n], ["u" + n], CW)
+        gather(CFG["ZE"], z, XW, oq[:, 0:4], XK + ["oz" + n], ["z" + n], 64)
+        dg = 60 + GAM * 64
+        if t == 0 or not CFG["TAB"]:
+            spot(c, z, zcol, "z" + n)
+            body, bo_, bkeys, u, uk = T.rbf[:, 0:1024], oq[:, 4:8], ["rbf", "on" + n], ib[:, 3, :], "u" + n
+        else:
+            body, bo_, bkeys, u, uk = T.TB[:, 0:2048], oq[:, 0:4], ["TB0", "TB1", "oz" + n], f[:, 0, :], "f0" + n
+            gather(CFG["UE"], u, T.TU[:, 0:2048], bo_, ["TU0", "TU1", "oz" + n], [uk], 64)
         Cn = pH[:, 320:384]
-        group(bh, "Cn" + n, [[const(Cn, 128, 512, 576, ["c12"])] + [(Cn, mats[m], d, [dk, m], 64) for d, dk, m in early + late],
+        group(bh, "Cn" + n, [[const(Cn, 128, -4, 64)] + [(Cn, mats[m], d, [dk, m], 64) for d, dk, m in early],
+                             [(Cn, mats[m], d, [dk, m], 64) for d, dk, m in late],
                              [(Cn, oh2[0:64, :], mats["nI4k64"], ["oh2" + n, "nI4k"], 64)]])
         sx = 2 * t + c; sk = "snd%d" % sx
         sg = nw[:, 0, :]
@@ -453,25 +524,23 @@ def build_ops(g, core, T, topo, rank):
         act(nw[:, 1, :], Cn, AF.Relu, 0.0, 1.0, ["Cn" + n], ["cr" + n], CW, bh)
         ts(d4[:, 2:256:4], Cn, 0.0, None, OP.is_lt, None, ["Cn" + n], ["d4n" + n], CW, 1.0, bh)
         act(f[:, 1, :], sg, AF.Identity, -6144.0, -4096.0, ["nw" + n], ["mL" + n], CW)
-        group(bu, "ud" + n, [[const(pU[:, 0:256:4], 128, 960, 1024, ["c1"])]])
+        group(bu, "ud" + n, [[(pU[:, 0:256:4], T.c33[0:1, 0, :], T.c33[0:1, 0, 0:64], ["c1"], 64)]])
         group(bu, "ua" + n, [[(pU[:, 2:256:4], mats["I"], a_ap, ["I", ak], 64)]])
-        group(bu, "uw" + n, [[(pU[:, 1:256:4], T.cev[0:1, :], cR[0:1, 960:1024], ["cev", "c1"], 64),
+        group(bu, "uw" + n, [[(pU[:, 1:256:4], T.cev[0:1, :], T.c33[0:1, 0, 0:64], ["cev", "c1"], 64),
                               (pU[:, 1:256:4], mats["nI"], a_ap, ["nI", ak], 64),
                               (pU[:, 1:256:4], mats["Godd"], yq[:, 1, :], ["Godd", "ya" + n], 64)]])
-        group(bu, "Lp0" + n, [[const(pU[:, 256:320], 128, 832, 896, ["c4"]), (pU[:, 256:320], mats["I"], tl(64, 128), ["I", tk], 64),
+        group(bu, "Lp0" + n, [[const(pU[:, 256:320], 128, -4, 64), (pU[:, 256:320], mats["I"], tl(64, 128), ["I", tk], 64),
                                (pU[:, 256:320], mats["I4k"], sg, ["I4k", "nw" + n], 64)]])
-        group(bu, "Lp1" + n, [[const(pU[:, 320:384], 128, 896, 960, ["cEa", "cEb"]),
+        group(bu, "Lp1" + n, [[const(pU[:, 320:384], 128, -6, 64),
                                (pU[:, 320:384], mats["nI4k"], sg, ["nI4k", "nw" + n], 64),
-                               (pU[:, 320:384], hT[0:64, :], mats["I1664"], ["hT" + n, "I16"], 64)]])
+                               (pU[:, 320:384], T.G16[0:8, :], hT[0:8, 64:128], ["hB" + n, "G16"], 64)]])
         tt(T.snd[:, sx, 128:192], pU[:, 320:384], nw[:, 1, :], OP.max, ["Lp1" + n, "cr" + n], [sk + "c"], CW, bu)
-        dg = 60 + GAM * 64
-        body = T.rbt[:, 0:1024]
-        op("v", lambda: V.tensor_tensor(f[:, 2, :], body.indirect(oq[:, 4:8]), f[:, 1, :], OP.add), ["rbt", "on" + n, "mL" + n], ["vb" + n], dg)
-        op("v", lambda: V.tensor_tensor(ib[:, 2, :], body.indirect(oq[:, 4:8]), ib[:, 3, :], OP.mult), ["rbt", "on" + n, "u" + n], ["w" + n], dg)
+        op("v", lambda: V.tensor_tensor(f[:, 2, :], body.indirect(bo_), f[:, 1, :], OP.add), bkeys + ["mL" + n], ["vb" + n], dg)
+        op("v", lambda: V.tensor_tensor(ib[:, 2, :], body.indirect(bo_), u, OP.mult), bkeys + [uk], ["w" + n], dg)
         Ln = T.snd[:, sx, 64:128]
         tt(Ln, pU[:, 256:320], f[:, 2, :], OP.max, ["Lp0" + n, "vb" + n], [sk + "l"], CW, bu)
         if t > 0:
-            ts(ib[:, 2, :], ib[:, 2, :], T.t32[:, 3 + t:4 + t], None, OP.add, None, ["w" + n, "t32"], ["w" + n], CW)
+            ts(ib[:, 2, :], ib[:, 2, :], pf[:, 30:31], T.t32[:, 3 + t:4 + t], OP.mult, OP.add, ["w" + n, "t32", "evc"], ["w" + n], CW)
         bits(d4[:, 1:256:4], ib[:, 2, :], 5, 4095, ["w" + n], ["d4x" + n], CW)
         if t < VIS - 1:
             ts(d4[:, 3:256:4], Ln, 3232.0, None, OP.add, None, [sk + "l"], ["d4l" + n], CW)
@@ -491,61 +560,110 @@ def build_ops(g, core, T, topo, rank):
                                                          (T.ya, so[:, 2:256:4], 1.0, 2048.0, "so" + n))):
                 ts(T.fin[:, 3 * c + j, :], src, mul, add, OP.mult, OP.add, [k], ["fin%d" % (3 * c + j)], CW)
                 dma("s", dst[:, 64 * c:64 * c + 64], T.fin[:, 3 * c + j, :], ["fin%d" % (3 * c + j)], [], 2400)
-        pick(c, CFG["GF"], lambda a, b: T["off" + n][:, a:b], "off" + n)
+        pick(c, CFG["GF"][c], lambda a, b: T["off" + n][:, a:b], "off" + n)
         rec = T["rec" + n]; mn = T["mn" + n]
-        for a, b in PH:
-            scan(mn[:, 16 * a:16 * b], T.keepT[:, :], rec[:, 16 * a:16 * b], OP.mult, OP.max, units("rec" + n, a, b) + ["keepT"], units("mn" + n, a, b), 16 * (b - a), 0.5)
-        group(bh, "zt" + n, [[(pH[:, 192:256], mats["Ib"], z[:, :], ["Ib", "z" + n], 64),
-                              (pH[:, 192:256], mats["Ib"], mn[:, 15:1024:16], ["Ib"] + units("mn" + n, 0, 64), 64)]])
-        ts(av[:, :], pH[:, 192:256], 0.5, -0.25, OP.mult, OP.add, ["zt" + n], ["av" + n], CW, 1.0, bh)
-        a, b = 4 * c, 4 * c + 4
-        bits(T.qw[:, 0, a:b], q[:, 0, :], 0, 15, ["q0" + n], ["q4" + n], 4)
-        tt(T.qw[:, 1, a:b], T.qw[:, 0, a:b], T.qc[:, 8 + a:8 + b], OP.add, ["q4" + n, "qc"], ["q5" + n], 4)
-        cp(T.ow[:, a:b], T.qw[:, 1, a:b], ["q5" + n], ["ow" + n], 4)
-
-    def write(t, c):
-        n = str(c)
-        tab_, k = (T.X, "X" + n) if t < VIS - 1 else (T.Xo, "Xo" + n)
-        op("v", lambda: V.tensor_copy(tab_[:, 1024 * c:1024 * c + 1024].indirect(T.ow[:, 4 * c:4 * c + 4]), T["av" + n][:, :]),
-           ["ow" + n, "av" + n, k], [k], 60 + 3.8 * 64)
+        for a, b in CFG["TS"][c]:
+            scan(mn[:, 16 * a:16 * b], T.keepT[:, 0:16 * (b - a)], rec[:, 16 * a:16 * b], OP.mult, OP.max, units("rec" + n, a, b) + ["keepT", "keepW"], units("mn" + n, a, b), 16 * (b - a), 0.5)
+        group(bh, "zt" + n, [[(pH[:, 192:256], mats["Ib"], z, ["Ib", "z" + n], 64)],
+                             [(pH[:, 192:256], mats["Ib"], mn[:, 15:1024:16], ["Ib"] + units("mn" + n, 0, 64), 64)]])
+        avi = T.avi[:, 64 * c:64 * c + 64]
+        ts(avi, pH[:, 192:256], 0.5, -0.25, OP.mult, OP.add, ["zt" + n], ["avi" + n], CW, 1.0, bh)
         if t == VIS - 1:
+            S = pK[:, 288:320:8]; a, b = 4 * c, 4 * c + 4; k = "Xo" + n
+            group(bk, "uW" + n, [[(S, T.selw[:, 15 - r:143 - r], zcol(r), ["selw", "z" + n], 64) for r in range(16)]])
+            scan(r5[:, :], T.du[:, 64:96], pK[:, 288:320], OP.mult, OP.add, ["uW" + n, "cu" + n, "du"], ["r5" + n], 32, 1.0, bk)
+            tt(T.qw[:, a:b], S, r5[:, 4:32:8], OP.add, ["uW" + n, "r5" + n], ["q5" + n], 4, bk)
+            cp(T.ow[:, a:b], T.qw[:, a:b], ["q5" + n], ["ow" + n], 4)
+            op("v", lambda: V.tensor_copy(T.Xo[:, 1024 * c:1024 * c + 1024].indirect(T.ow[:, a:b]), avi), ["ow" + n, "avi" + n, k], [k], 60 + 3.8 * 64)
             dma("s" if c == 0 else "a", T.yx[:, 1024 * c:1024 * c + 1024], T.Xo[:, 1024 * c:1024 * c + 1024], [k], [], 3000)
+
+    def scatter(tab_, k, src, skeys):
+        op("v", lambda: V.tensor_copy(tab_[:, 0:2048].indirect(T.ow[:, 0:8]), src), ["ow0", "ow1"] + skeys, [k + "0", k + "1"], 60 + 3.8 * 128)
+
+    def write():
+        pK = T.pK1; S = pK[:, 384:448:8]
+        group("K1", "uW", [[(S, T.selw[:, 15 - r:143 - r], T.z[:, r:128:16], ["selw", "z0", "z1"], 64) for r in range(16)]])
+        scan(T.rw[:, :], T.du[:, 64:128], pK[:, 384:448], OP.mult, OP.add, ["uW", "cu1", "du"], ["rw"], 64, 1.0, "K1")
+        tt(T.qw[:, :], S, T.rw[:, 4:64:8], OP.add, ["uW", "rw"], ["q50", "q51"], 8, "K1")
+        cp(T.ow[:, :], T.qw[:, :], ["q50", "q51"], ["ow0", "ow1"], 8)
+        for c in range(NCH):
+            op("v", lambda c=c: V.tensor_copy(T.X[:, 0:2048].indirect(T.ow[:, 4 * c:4 * c + 4]), T.avi[:, 64 * c:64 * c + 64]),
+               ["ow0", "avi%d" % c], ["X0", "X1"], 60 + 3.8 * 64)
+
+    def renew():
+        pK = T.pK1; S = pK[:, 320:384:8]; q = T.qn
+        gcopy(T.av[:, :], T.avi[:, :], ["avi0", "avi1"], ["av0", "av1"], 128)
+        group("K1", "uN", [[(S, T.selw[:, 15 - r:143 - r], T.av[:, r:128:16], ["selw", "av0", "av1"], 64) for r in range(16)]])
+        scan(T.rw[:, :], T.du[:, 0:64], pK[:, 320:384], OP.mult, OP.add, ["uN", "cu1", "du"], ["rw"], 64, 1.0, "K1")
+        tt(q[:, 0, :], S, T.rw[:, 4:64:8], OP.add, ["uN", "rw"], ["qn0"], 8, "K1")
+        tt(q[:, 1, :], S, T.rw[:, 5:64:8], OP.add, ["uN", "rw"], ["qn1"], 8, "K1")
+        ts(T.on[:, 0:8], q[:, 0, :], 2048.0, None, OP.add, None, ["qn0"], ["onu"], 8)
+        tt(q[:, 2, :], q[:, 0, :], q[:, 1, :], OP.mult, ["qn0", "qn1"], ["qn2"], 8)
+        bits(q[:, 3, :], q[:, 2, :], 5, 1023, ["qn2"], ["qn3"], 8)
+        cp(T.on[:, 8:16], q[:, 3, :], ["qn3"], ["onb"], 8)
+        gather("a", T.nv[:, 0, :], T.IU[:, 0:4096], T.on[:, 0:8], ["IU0", "IU1", "IU2", "IU3", "onu"], ["nv0"], 128)
+        gather("a", T.nv[:, 1, :], T.rbf[:, 0:1024], T.on[:, 8:16], ["rbf", "onb"], ["nv1"], 128)
+        scatter(T.TU, "TU", T.nv[:, 0, :], ["nv0"])
+        scatter(T.TB, "TB", T.nv[:, 1, :], ["nv1"])
+
+    def tables():
+        pO = T.pO0; w = T.tw
+        group("O0", "uT", [[(pO[:, 256:384], T.selw[:, 15 - r:143 - r], T.X[:, r:2048:16], ["selw", "X0", "X1"], 128) for r in range(16)]])
+        cp(w[:, 0, :], pO[:, 256:384], ["uT"], ["tw0"], 128, 1.0, "O0")
+        bits(w[:, 1, :], w[:, 0, :], 0, 4095, ["tw0"], ["tw1"], 128)
+        cp(T.to[:, 0, :], w[:, 1, :], ["tw1"], ["to0"], 128)
+        ts(w[:, 0, :], w[:, 1, :], -2048.0, None, OP.add, None, ["tw1"], ["tw0"], 128)
+        ts(w[:, 2, :], w[:, 1, :], 3232.0, None, OP.add, None, ["tw1"], ["tw2"], 128)
+        tt(w[:, 1, :], w[:, 0, :], w[:, 2, :], OP.mult, ["tw0", "tw2"], ["tw1"], 128)
+        bits(w[:, 0, :], w[:, 1, :], 5, 1023, ["tw1"], ["tw0"], 128)
+        cp(T.to[:, 1, :], w[:, 0, :], ["tw0"], ["to1"], 128)
+        m = CFG["TP"]
+        for j in range(0, 128, m):
+            k = "%d" % (j // 64)
+            gather("a", T.TU[:, 16 * j:16 * (j + m)], T.IU[:, 0:4096], T.to[:, 0, j:j + m], ["IU0", "IU1", "IU2", "IU3", "to0"], ["TU" + k], 16 * m)
+            gather("a", T.TB[:, 16 * j:16 * (j + m)], T.rbf[:, 0:1024], T.to[:, 1, j:j + m], ["rbf", "to1"], ["TB" + k], 16 * m)
 
     limit()
     for c in range(NCH):
         n = str(c); tl, tk = tile_of(0, c); f = T["f" + n]; ib = T["i" + n]; cs_ = slice(64 * c, 64 * c + 64)
-        ts(tl(0, 64), T.agi[:, cs_], -2048.0, None, OP.add, None, ["agi"], [tk + "a"], CW)
-        ts(f[:, 0, :], T.lti[:, cs_], 1184.0, None, OP.add, None, ["lti"], ["f0" + n], CW)
-        ts(f[:, 1, :], T.lti[:, cs_], -2048.0, 2080.0, OP.add, OP.mult, ["lti"], ["mL" + n], CW)
-        tt(f[:, 2, :], f[:, 0, :], tl(0, 64), OP.mult, ["f0" + n, tk + "a"], ["vb" + n], CW)
-        tt(ib[:, 0, :], f[:, 2, :], f[:, 1, :], OP.add, ["vb" + n, "mL" + n], ["u0" + n], CW)
-        bits(ib[:, 1, :], ib[:, 0, :], 5, 2047, ["u0" + n], ["pl" + n], CW)
+        d4 = T["d4" + n]; so = T["so" + n]
+        ts(so[:, 0:128:2], T.agi[:, cs_], -2048.0, None, OP.add, None, ["agi"], ["so" + n], CW)
+        ts(d4[:, 1:128:2], T.lti[:, cs_], 1184.0, None, OP.add, None, ["lti"], ["d4x" + n, "d4l" + n], CW)
+        ts(so[:, 1:128:2], T.lti[:, cs_], -2048.0, 2080.0, OP.add, OP.mult, ["lti"], ["sw" + n], CW)
+        scan(T.tw[:, c, :], d4[:, 0:128], so[:, 0:128], OP.mult, OP.add, ["so" + n, "sw" + n, "d4x" + n, "d4z" + n], ["tw" + n], 128)
+        bits(ib[:, 1, :], T.tw[:, c, 1:128:2], 5, 2047, ["tw" + n], ["pl" + n], CW)
         cp(T["off" + n][:, :], ib[:, 1, :], ["pl" + n], ["off" + n], CW)
+        ts(tl(0, 64), T.agi[:, cs_], -2048.0, None, OP.add, None, ["agi"], [tk + "a"], CW)
         ts(tl(64, 128), T.lti[:, cs_], -2048.0, None, OP.add, None, ["lti"], [tk + "l"], CW)
         ts(tl(128, 192), T.csi[:, cs_], 16.0, None, OP.mult, None, ["csi", tk + "l", tk + "a"], [tk], CW)
     for t in range(VIS):
         for c in range(NCH):
-            begin(t, c)
+            phase(begin, "b%d" % c, t, c)
         if t == VIS - 1:
+            at[0] = "copy"
             for c in range(NCH):
                 dma("s", T.Xo[:, 1024 * c:1024 * c + 1024], T.X[:, 1024 * c:1024 * c + 1024], ["X%d" % c], ["Xo%d" % c], 3000)
         for s in range(3):
             for c in range(NCH):
-                step(t, s, c)
+                phase(step, "s%d%d" % (s, c), t, s, c)
             if not (t == VIS - 1 and s == 2):
-                count()
+                phase(count, "c%d" % s)
             if t == 0 and s == 0:
-                late_constants()
+                phase(late_constants, "late")
+                if CFG["TAB"]:
+                    phase(tables, "tab")
+            if t > 0 and s == CFG["RS"] and CFG["TAB"]:
+                phase(renew, "new")
         for c in range(NCH):
-            refill(t, c)
-        for c in range(NCH):
-            write(t, c)
+            phase(refill, "r%d%d" % (c, t == 0 and CFG["TAB"]), t, c)
+        if t < VIS - 1:
+            phase(write, "w")
     return ops
 
 
 def schedule(ops):
     n = len(ops)
-    LAT, FAC, SLACK, FRAC = CFG["LAT"], CFG["FAC"], CFG["SLACK"], CFG["FRAC"]
+    LAT, FAC = CFG["LAT"], CFG["FAC"]
     lastw = {}; readers = {}; lastb = {}
     deps = []
     for i, o in enumerate(ops):
@@ -578,40 +696,94 @@ def schedule(ops):
             succ[j].append(i)
     dur = [o["d"] * (FAC if o["kind"] in ("c", "mm") else 1.0) for o in ops]
     occ = [{"dma": 80.0, "rem": 500.0}.get(o["kind"], dur[i]) for i, o in enumerate(ops)]
+
+    def gap(i, j):
+        if not waits(i, j):
+            return occ[j]
+        return dur[j] + (CFG["LATS"] if ops[i]["e"] == ops[j]["e"] else LAT)
+
+    fwd = [[(j, gap(i, j)) for j in deps[i]] for i in range(n)]
+    bwd = [[(k, occ[k] - occ[j] + gap(k, j)) for k in succ[j]] for j in range(n)]
+
+    def place(seq, edges, first):
+        st = [0.0] * n
+        line = {e: [] for e in "vapgs"}
+        for i in seq:
+            t = max([first[i]] + [st[j] + w for j, w in edges[i]])
+            lst = line[ops[i]["e"]]
+            lo, hi = 0, len(lst)
+            while lo < hi:
+                mid = (lo + hi) // 2
+                if lst[mid][1] <= t:
+                    lo = mid + 1
+                else:
+                    hi = mid
+            while lo < len(lst) and lst[lo][0] < t + occ[i]:
+                t = max(t, lst[lo][1]); lo += 1
+            lst.insert(lo, (t, t + occ[i]))
+            st[i] = t
+        return st
+
+    tail = [dur[i] + (CFG["LAG"] if o["kind"] == "dma" and o["r"] and o["r"][0] in ("fin0", "fin1", "fin2", "Xo0") else 0.0)
+            for i, o in enumerate(ops)]
     pr = [0.0] * n
     for i in range(n - 1, -1, -1):
-        pr[i] = max([dur[i]] + [pr[k] + (dur[i] + LAT if waits(k, i) else occ[i]) for k in succ[i]])
-    left = [len(d) for d in deps]
-    rdy = [0.0] * n
-    end = [0.0] * n
-    free = {e: 0.0 for e in "vapgs"}
-    cand = {e: [] for e in "vapgs"}
-    for i in range(n):
-        if left[i] == 0:
-            cand[ops[i]["e"]].append(i)
-    order = []
-    while len(order) < n:
-        best = None
-        for e, lst in cand.items():
-            if not lst:
-                continue
-            t0 = max(free[e], min(rdy[i] for i in lst))
-            if best is None or t0 < best[0]:
-                best = (t0, e)
-        t0, e = best
-        lst = cand[e]
-        i = max((k for k in lst if rdy[k] <= t0 + SLACK), key=lambda k: (pr[k], -k))
-        i = max((k for k in lst if rdy[k] <= t0 + max(SLACK, FRAC * occ[i])), key=lambda k: (pr[k], -k))
-        st = max(t0, rdy[i])
-        lst.remove(i)
-        free[e] = st + occ[i]
-        end[i] = st + dur[i]
-        order.append(i)
-        for k in succ[i]:
-            rdy[k] = max(rdy[k], end[i] + LAT if waits(k, i) else st)
-            left[k] -= 1
-            if left[k] == 0:
-                cand[ops[k]["e"]].append(k)
+        pr[i] = max([tail[i]] + [pr[k] + gap(k, i) for k in succ[i]])
+    seq = sorted(range(n), key=lambda i: (-pr[i], i))
+    found = None
+    x = 1
+    for _ in range(CFG["PASSES"]):
+        st = place(seq, fwd, [0.0] * n)
+        total = max(st[i] + tail[i] for i in range(n))
+        if found is None or total < found[0]:
+            found = (total, st)
+        st = found[1]
+        back = place(sorted(range(n), key=lambda i: (-st[i] - occ[i], -i)), bwd, [tail[i] - occ[i] for i in range(n)])
+        key = [0.0] * n
+        for i in range(n):
+            x = (x * 1103515245 + 12345) & 0x7FFFFFFF
+            key[i] = max([CFG["JIT"] * x / 2.0 ** 31 - back[i] - occ[i]] + [key[j] for j in deps[i]])
+        seq = sorted(range(n), key=lambda i: (key[i], i))
+    slow = [o["d"] * (1.0 if o["kind"] in ("dma", "rem") else CFG["FAC2"] * (CFG["GX2"] if o["ext"] == "pick" else CFG["PX2"] if o["kind"] == "mm" else 1.0)) for o in ops]
+    eng = [o["e"] for o in ops]
+    hold = [occ[i] if o["kind"] in ("dma", "rem") else slow[i] for i, o in enumerate(ops)]
+    edge2 = [[(j, slow[j] + gap(i, j) - dur[j]) for j in deps[i] if waits(i, j)] for i in range(n)]
+
+    def cost(st):
+        s2 = [0.0] * n; free = {e: 0.0 for e in "vapgs"}; last = 0.0
+        for i in sorted(range(n), key=lambda i: (st[i], i)):
+            t = free[eng[i]]
+            for j, w in edge2[i]:
+                if s2[j] + w > t:
+                    t = s2[j] + w
+            s2[i] = t; free[eng[i]] = t + hold[i]
+            last = max(last, t + slow[i])
+        return max(st[i] + dur[i] for i in range(n)) + CFG["W2"] * last
+
+    st = found[1]
+    kinds = {}
+    for i, o in enumerate(ops):
+        kinds.setdefault(o["cls"], []).append(i)
+    names = [k for k in kinds if k[0] not in ("start", "late")]
+    low = cost(st)
+    zero = [0.0] * n
+    for _ in range(CFG["MOVES"]):
+        key = list(st)
+        for _k in range(CFG["MK"]):
+            x = (x * 1103515245 + 12345) & 0x7FFFFFFF
+            by = ((x >> 4 & 1023) - 512) * CFG["BY"]
+            for i in kinds[names[(x >> 14) % len(names)]]:
+                key[i] += by
+        for i in range(n):
+            for j in deps[i]:
+                if key[j] > key[i]:
+                    key[i] = key[j]
+        new = place(sorted(range(n), key=lambda i: (key[i], i)), fwd, zero)
+        c = cost(new)
+        if c <= low:
+            low, st = c, new
+    end = [st[i] + dur[i] for i in range(n)]
+    order = sorted(range(n), key=lambda i: (st[i], i))
     pos = {}; cnt = {e: 0 for e in "vapgs"}
     know = {e: ({x: -1 for x in "vapg"}, set()) for e in "vapgs"}
     snap = {}; wait = {}

from concourse.mybir import dt, AluOpType as OP, AxisListType, ActivationFunctionType as AF

CW = 64
NCH = 2
SH = (1, 3, 6)
VIS = 5
H = "float16"
B = "bfloat16"
F = "float32"
I = "int32"
U = "uint16"
RND = 12582912.0

CFG = {
    "GP": (("a", 0, 32), ("v", 32, 40), ("a", 40, 64)),
    "G0": (("a", 0, 32), ("v", 32, 48), ("a", 48, 64)),
    "GF": ((("a", 0, 32), ("a", 32, 64)),) * 2,
    "TS": (((0, 32), (32, 64)),) * 2,
    "SP": ((0, 32), (32, 64)),
    "CP": ((0, 32), (32, 64)),
    "ZE": "a", "UE": "v", "U16": False,
    "GA": 0, "SM": False, "PX2": 1.5, "TAB": True, "AFX": 100, "TP": 16, "RS": 0, "RUN": 4, "LAT": 280.0, "LATS": 320.0, "FAC": 1.0, "GAM": 1.4, "PEC": 0.35,
    "PASSES": 10, "JIT": 100.0, "LAG": 2000.0, "MOVES": 800, "MK": 1, "BY": 1.5,
    "FAC2": 1.35, "GX2": 1.1, "W2": 0.6, "REM": 2400.0,
}
PH = ((0, 32), (32, 64))


def row_of(s, p):
    return ((6 * (p & 7) + 3 * (p >> 3)) if s == 2 else SH[s] * p) & 15


def _scratch():
    s = {}

    def sb(n, sh, d):
        s[n] = ("sbuf", [128] + list(sh), d)
    sb("X", [2064], B); sb("Xo", [2048], B); sb("rbt", [1024], I); sb("rbf", [1024], F)
    sb("IU", [4096], F); sb("TU", [2048], F); sb("TB", [2048], F); sb("tw", [3, 128], I); sb("to", [2, 128], U)
    sb("lti", [128], I); sb("agi", [128], I); sb("csi", [128], I); sb("thi", [128], I)
    sb("Fi", [2, 128], I); sb("Fh", [2, 128], H); sb("pi", [28], I); sb("pf", [36], F)
    sb("mh", [30, 128], H); sb("mb", [7, 128], B); sb("IB", [192], B)
    sb("tab", [5, 128], B); sb("gF2", [16], B); sb("gs", [24], B)
    sb("selw", [144], B); sb("keepT", [512], B); sb("edge", [2, 128], B); sb("rs2", [128], B)
    sb("c33", [2, 128], B); sb("cR", [320], B); sb("c2", [704], B); sb("w2", [128], B); sb("cn", [4], B); sb("cev", [128], B); sb("mk", [64], H); sb("G16", [128], B)
    sb("thR", [128], H); sb("thf", [128], H); sb("thx", [128], H)
    sb("t32", [8], F); sb("cu", [192], F); sb("a31", [8], B); sb("dc", [8], F); sb("du", [128], F)
    sb("z", [128], B); sb("av", [128], B); sb("avi", [128], I); sb("rw", [64], F); sb("qn", [4, 8], I); sb("on", [16], U); sb("nv", [2, 128], F)
    sb("tile0", [2, 192], H); sb("lnd", [8, 192], H); sb("snd", [10, 192], H)
    sb("lno", [8, 64], U); sb("sno", [8, 64], U)
    sb("fin", [6, 64], F); sb("qw", [8], F); sb("ow", [8], U)
    for c in range(NCH):
        n = str(c)
        sb("rec" + n, [1024], B); sb("mn" + n, [1024], B); sb("cl" + n, [128], B)
        sb("Bk" + n, [128], F); sb("Cs" + n, [128], B); sb("ohT" + n, [128], B); sb("oh2" + n, [128], B); sb("hT" + n, [128], B)
        sb("hi" + n, [128], H); sb("y" + n, [3, 192], H); sb("eq" + n, [64], B)
        sb("d3" + n, [576], F); sb("d4" + n, [256], I); sb("so" + n, [256], I); sb("an" + n, [64], H)
        sb("f" + n, [5, 64], F); sb("i" + n, [4, 64], I); sb("off" + n, [64], U)
        sb("yq" + n, [2, 64], H); sb("offq" + n, [8], U)
        sb("q" + n, [4, 4], I); sb("r5" + n, [32], F); sb("nw" + n, [2, 64], B)
        s["pK" + n] = ("psum", [128, 512], F)
        s["pO" + n] = ("psum", [128, 512], F)
        s["pU" + n] = ("psum", [128, 512], F)
        s["pH" + n] = ("psum", [128, 512], F)
    return s


SCRATCH = _scratch()
NDMA = 24
SEMAPHORES = (["sv", "sa", "sp", "sg", "loc"] + ["d%d" % k for k in range(NDMA)]
              + ["aro%d" % k for k in range(8)] + ["art%d" % k for k in range(8)])


def build_ops(g, core, T, topo, rank):
    ops = []
    V, A, PE = g.vector, g.scalar, g.tensor
    GAM = CFG["GAM"]
    at = ["start", 0]

    def op(e, fn, r, w, d, bank=None, kind="c", ext=None):
        at[1] += 1
        ops.append({"e": e, "fn": fn, "r": list(r), "w": list(w), "d": float(d), "bank": bank, "kind": kind, "ext": ext, "cls": tuple(at)})

    def phase(fn, name, *args):
        at[0], at[1] = name, 0
        fn(*args)

    def vt(n, rate=1.0):
        return max(64.0, n * rate)

    def ts(out, in0, s1, s2, o0, o1, r, w, n, rate=1.0, bank=None):
        if o1 is None:
            op("v", lambda: V.tensor_scalar(out, in0, s1, None, o0), r, w, vt(n, rate), bank)
        else:
            op("v", lambda: V.tensor_scalar(out, in0, s1, s2, o0, o1), r, w, vt(n, rate), bank)

    def tt(out, a, b, o, r, w, n, bank=None, d=None):
        op("v", lambda: V.tensor_tensor(out, a, b, o), r, w, d or vt(n, 1.0 if bank else 2.0), bank)

    def cp(out, a, r, w, n, rate=1.0, bank=None):
        op("v", lambda: V.tensor_copy(out, a), r, w, vt(n, rate), bank)

    def ms(out, c, w, n, bank=None, r=()):
        op("v", lambda: V.memset(out, c), r, w, vt(n, 1.0), bank)

    def scan(out, a, b, o0, o1, r, w, n, rate=1.0, bank=None):
        op("v", lambda: V.tensor_tensor_scan(out, a, b, 0.0, o0, o1), r, w, vt(n, rate), bank)

    def bits(out, in0, sh, mask, r, w, n):
        if sh:
            ts(out, in0, sh, mask, OP.arith_shift_right, OP.bitwise_and, r, w, n)
        else:
            ts(out, in0, mask, None, OP.bitwise_and, None, r, w, n)

    def act(out, in_, fn, bias, scale, r, w, n, bank=None):
        op("a", lambda: A.activation(out, in_, fn, bias=bias, scale=scale), r, w, CFG["AFX"] + n, bank)

    def iota(out, pat, base, cm, w, n, fl=False):
        if fl:
            op("g", lambda: g.iota(out, pat, base, cm, allow_small_or_imprecise_dtypes=True), [], w, 160 + 2 * n)
        else:
            op("g", lambda: g.iota(out, pat, base, cm), [], w, 160 + 2 * n)

    def gcopy(out, in_, r, w, n):
        op("g", lambda: g.affine_select(out, in_, [[0, n]], OP.is_ge, 0.0, 0, 0), r, w, 205 + 2 * n)

    def group(bank, key, runs):
        runs = [x[k:k + CFG["RUN"]] for x in runs for k in range(0, len(x), CFG["RUN"])]
        for j, run in enumerate(runs):
            def fn(run=run, a=(j == 0), b=(j == len(runs) - 1)):
                ins = None
                for k, (o, l, r_, rd, cyc) in enumerate(run):
                    ins = PE.matmul(o, l, r_, a and k == 0, b and k == len(run) - 1)
                return ins
            rd = []
            for x in run:
                rd += [k for k in x[3] if k not in rd]
            op("p", fn, rd, [key], sum(x[4] for x in run) * CFG["PEC"], bank, "mm")

    def dma(e, out, in_, r, w, d):
        q = {"s": g.sync, "a": g.scalar}[e]
        op(e, lambda: q.dma_start(out, in_), r, w, d, None, "dma")

    def gather(e, out, win, off, r, w, n):
        if e == "a":
            op("a", lambda: A.activation(out, win.indirect(off), AF.Copy), r, w, 80 + GAM * n, None, "c", "pick")
        else:
            op("v", lambda: V.tensor_copy(out, win.indirect(off)), r, w, 60 + GAM * n, None, "c", "pick")

    dma("s", T.lti[:], T.lt[:], [], ["lti"], 2400)
    dma("a", T.agi[:], T.ag[:], [], ["agi"], 2400)
    dma("s", T.X[:, 0:1024], T.xs[:, 0:1024], [], ["X0"], 3200)
    dma("a", T.X[:, 1024:2048], T.xs[:, 1024:2048], [], ["X1"], 3200)
    dma("s", T.csi[:], T.cs[:], [], ["csi"], 3200)
    dma("s", T.thi[0:8, :], T.th[:], [], ["thi"], 3200)
    dma("s", T.rbt[:], T.rb[:], [], ["rbt"], 5000)
    ms(T.X[:, 2048:2064], 0.0, ["Xz"], 16)

    P = T.pi; pf = T.pf; tab = T.tab
    iota(P[:, 0:16], [[1, 16]], 0, 1, ["pa"], 16)
    iota(tab[:, 0, :], [[1, 128]], 0, 0, ["h0"], 128, True)
    iota(tab[:, 1, :], [[1, 8], [0, 16]], 0, 0, ["gF0"], 128, True)
    iota(T.gF2[:, :], [[1, 8], [0, 2]], 0, 0, ["gF2b"], 16, True)
    iota(tab[:, 2, :], [[0, 8], [1, 16]], 0, 0, ["kk"], 128, True)
    iota(P[:, 16:18], [[-3, 2]], 48, 3, ["pb"], 2)
    iota(P[:, 18:20], [[-6, 2]], 48, 6, ["pc"], 2)
    for o, pat in ((1, [[256, 8], [3, 16]]), (2, [[256, 8], [3, 2], [6, 8]])):
        iota(T.Fi[:, o - 1, :], pat, 0, 0, ["Fi%d" % o], 128)
        bits(T.Fi[:, o - 1, :], T.Fi[:, o - 1, :], 0, 0x70F, ["Fi%d" % o], ["Fi%d" % o], 128)
        cp(T.Fh[:, o - 1, :], T.Fi[:, o - 1, :], ["Fi%d" % o], ["Fh%d" % o], 128)
    iota(tab[:, 3, :], [[1, 8], [0, 8], [-100, 2]], 100, 0, ["gF1"], 128, True)
    iota(tab[:, 4, :], [[1, 8], [0, 8], [100, 2]], 0, 0, ["gF2"], 128, True)
    iota(T.t32[:, 0:4], [[32, 4]], 32, 0, ["t32a"], 4, True)
    cp(pf[:, 20:21], P[:, 0:1], ["pa"], ["pcol"], 1)
    bits(P[:, 21:22], P[:, 0:1], 4, 7, ["pa"], ["p21"], 1)
    bits(P[:, 22:23], P[:, 0:1], 3, 1, ["pa"], ["p22"], 1)
    bits(P[:, 23:24], P[:, 0:1], 0, 1, ["pa"], ["p23"], 1)
    bits(P[:, 24:25], P[:, 0:1], 0, 0x70, ["pa"], ["p24"], 1)
    bits(P[:, 25:26], P[:, 0:1], 0, 15, ["pa"], ["p25"], 1)
    cp(pf[:, 21:26], P[:, 21:26], ["p21", "p22", "p23", "p24", "p25"], ["pfa"], 5)
    pcol, gcol, g16, kcol = pf[:, 20:21], pf[:, 21:22], pf[:, 24:25], pf[:, 25:26]
    bits(P[:, 0:16], P[:, 0:16], 0, 15, ["pa"], ["pa", "pa2"], 16)
    ts(pf[:, 0:16], P[:, 0:16], g16, None, OP.add, None, ["pa2", "pfa"], ["shf"], 16)
    ts(pf[:, 26:27], pf[:, 22:23], 3.0, None, OP.mult, None, ["pfa"], ["h3"], 1)
    ts(P[:, 18:20], P[:, 18:20], pf[:, 26:27], None, OP.add, None, ["pc", "h3"], ["pc"], 2)
    bits(P[:, 16:20], P[:, 16:20], 0, 15, ["pb", "pc"], ["pb2"], 4)
    ts(pf[:, 16:20], P[:, 16:20], g16, None, OP.add, None, ["pb2", "pfa"], ["shr"], 4)
    ts(pf[:, 27:28], gcol, 256.0, kcol, OP.mult, OP.add, ["pfa"], ["p256"], 1)
    ts(pf[:, 28:29], kcol, 2.0, 1.0, OP.mult, OP.add, ["pfa"], ["wcol"], 1)
    ts(pf[:, 29:30], kcol, 16.0, None, OP.mult, None, ["pfa"], ["k16"], 1)
    ts(pf[:, 30:31], pf[:, 23:24], -1.0, 1.0, OP.mult, OP.add, ["pfa"], ["evc"], 1)
    ts(T.t32[:, 4:8], T.t32[:, 0:4], pf[:, 30:31], None, OP.mult, None, ["t32a", "evc"], ["t32"], 4)

    slots = {"h": [0], "b": [0]}
    mats = {}

    def slot(name, kind):
        j = slots[kind][0]; slots[kind][0] += 1
        mats[name] = (T.mh if kind == "h" else T.mb)[:, j, :]
        mats[name + "64"] = (T.mh if kind == "h" else T.mb)[0:64, j, 0:64]
        mats[name + "8"] = (T.mh if kind == "h" else T.mb)[0:8, j, 0:8]
        return mats[name]

    def pick1(name, kind, table, tkey, col, ckey, scale):
        ts(slot(name, kind), table, col, scale, OP.is_equal, OP.mult, [tkey, ckey], [name], 128, 0.5)

    def diagonal(name, src, skey, v):
        op("g", lambda: g.affine_select(mats[name], src, [[-1, 128]], OP.not_equal, v, 0, 1), [skey], [name], 461)

    def shift(name, j, scale):
        pick1(name, "h", tab[:, 0, :], "h0", pf[:, j & 15:(j & 15) + 1], "shf", scale)

    pick1("I", "h", tab[:, 0, :], "h0", pcol, "pcol", 1.0)
    pick1("nI", "h", tab[:, 0, :], "h0", pcol, "pcol", -1.0)
    pick1("W0", "h", tab[:, 0, :], "h0", pcol, "pcol", 2080.0)
    mats["P0"] = mats["I"]
    for o in (1, 2):
        pick1("P%d" % o, "h", T.Fh[:, o - 1, :], "Fh%d" % o, pf[:, 27:28], "p256", 1.0)
        pick1("W%d" % o, "h", T.Fh[:, o - 1, :], "Fh%d" % o, pf[:, 27:28], "p256", 2080.0)
        pick1("PT%d" % o, "h", tab[:, 0, :], "h0", pf[:, 14 + 2 * o:15 + 2 * o], "shr", 1.0)
        pick1("PS%d" % o, "h", tab[:, 0, :], "h0", pf[:, 15 + 2 * o:16 + 2 * o], "shr", 1.0)
    for s in range(3):
        shift("Sh%d" % s, -SH[s], 1.0)
        shift("nIS%d" % s, -SH[s], -1.0)
        diagonal("nIS%d" % s, mats["nIS%d" % s], "nIS%d" % s, -1.0)
        slot("D%d" % s, "h")
        diagonal("D%d" % s, mats["Sh%d" % s], "Sh%d" % s, -1.0)
        shift("nSx%d" % s, SH[s], -1.0)
    shift("PN", SH[0], 64.0)
    shift("PNb", SH[0] - SH[1], 64.0)
    tt(mats["PN"], mats["PN"], mats["PNb"], OP.add, ["PN", "PNb"], ["PN"], 128)
    j = -SH[2] & 15
    pick1("PE", "b", tab[:, 0, :], "h0", pf[:, j:j + 1], "shf", 8192.0)
    diagonal("PE", mats["PE"], "PE", 8192.0)
    pick1("G", "h", tab[:, 1, :], "gF0", gcol, "pfa", 1.0)
    pick1("nG", "h", tab[:, 1, :], "gF0", gcol, "pfa", -1.0)
    pick1("Godd", "h", tab[:, 3, :], "gF1", gcol, "pfa", 1.0)
    for nm, v in (("Ib", 1.0), ("BI", 262144.0), ("I4k", 4096.0), ("nI4k", -4096.0)):
        pick1(nm, "b", tab[:, 0, :], "h0", pcol, "pcol", v)
    ts(slot("Wev", "b"), tab[:, 4, :], gcol, pf[:, 28:29], OP.is_equal, OP.mult, ["gF2", "pfa", "wcol"], ["Wev"], 128, 0.5)
    for j, v in enumerate((4096.0, 4096.0, -8192.0)):
        ts(T.IB[0:64, 64 * j:64 * j + 64], tab[0:64, 0, 0:64], pf[0:64, 20:21], v, OP.is_equal, OP.mult, ["h0", "pcol"], ["IB%d" % j], 64)
    ts(T.gs[:, 0:8], T.gF2[:, 0:16:2], gcol, 32.0, OP.is_equal, OP.mult, ["gF2b", "pfa"], ["G32"], 16)
    ts(T.gs[:, 16:24], T.gF2[:, 0:16:2], gcol, -64.0, OP.is_equal, OP.mult, ["gF2b", "pfa"], ["Gm64"], 8)
    ms(T.selw[:], 0.0, ["selw"], 72)
    ts(T.selw[:, 15:143:16], T.gF2[:, 0:16:2], gcol, pf[:, 28:29], OP.is_equal, OP.mult, ["gF2b", "pfa", "wcol", "selw"], ["selw"], 8)
    ts(T.mk[:, :], tab[:, 2, 0:64], kcol, -4096.0, OP.not_equal, OP.mult, ["kk", "pfa"], ["mk"], 64)
    ts(T.thR[0:8, :], tab[0:8, 1, :], pf[0:8, 20:21], -32.0, OP.is_equal, OP.mult, ["gF0", "pcol"], ["thR"], 128, 0.5)
    ts(T.G16[0:8, :], tab[0:8, 1, :], pf[0:8, 20:21], 16.0, OP.is_equal, OP.mult, ["gF0", "pcol"], ["G16"], 128, 0.5)
    ms(T.keepT[:, 0:128], 1.0, ["keepT"], 64)
    ms(T.keepT[:, 0:128:16], 0.0, ["keepT"], 8)
    iota(T.keepT[:, 128:512], [[0, 384]], 1, 0, ["keepW"], 384, True)
    iota(T.keepT[:, 128:512:16], [[0, 24]], 0, 0, ["keepW"], 24, True)
    for j, v in enumerate((1.0e9, -1.0e9)):
        ms(T.edge[:, j, :], -v, ["edge%d" % j], 64)
        ms(T.edge[:, j, 0:128:16], v, ["edge%d" % j], 8)
    iota(T.rs2[:, :], [[0, 64], [30000, 2]], -30000, 0, ["rs2"], 128, True)
    iota(T.cev[0:1, :], [[0, 64], [2048, 2]], -2048, 0, ["cev"], 128, True)
    cR = T.cR; rows = {}
    ms(T.c33[0:1, 0, :], 1.0, ["c1"], 64)
    ms(T.c33[0:1, 1, :], 1024.0, ["c1k"], 64)
    for j, v in enumerate((-60, -4, -12, -8, -6)):
        rows[v] = 64 * j
        iota(cR[0:1, 64 * j:64 * j + 64], [[0, 64]], v, 0, ["row%d" % v], 64, True)

    def const(out, m, v, n_):
        return (out, T.c33[0:1, 1, 0:m], cR[0:1, rows[v]:rows[v] + n_], ["c1k", "row%d" % v], 64)

    c2 = T.c2
    ms(T.w2[0:33, :], 1.0, ["w2"], 64)
    ms(T.w2[32:33, :], 1024.0, ["w2"], 64)
    ms(c2[0:33, :], 0.0, ["c2"], 352)
    for a, b, pat, base, k in ((0, 128, [[0, 8], [2, 16]], 1, "a"), (512, 640, [[-2, 2], [0, 64]], 1, "c"),
                               (128, 256, [[0, 8], [2, 16]], 1, "f"), (384, 512, [[0, 8], [-1, 16]], 15, "h")):
        op("g", lambda a=a, b=b, pat=pat, base=base: g.iota(c2[0:1, a:b], pat, base, 0, allow_small_or_imprecise_dtypes=True),
           ["c2"], ["c2" + k], 160 + 2 * (b - a))
    for a, b, v, k in ((0, 128, -64.0, ["c2b"]), (384, 640, -4.0, ["c2d", "c2i"]), (640, 704, 8.0, ["c2e"]), (128, 256, 448.0, ["c2g"])):
        ms(c2[32:33, a:b], v, k, (b - a) // 2, None, ["c2"])

    def const2(out, m, a, b, keys):
        return (out, T.w2[0:33, 0:m], c2[0:33, a:b], ["w2"] + ["c2" + k for k in keys], b - a)

    ms(T.dc[0:8, 0:6], 1.0, ["dc"], 8)
    for j, v in ((0, 0.0), (1, 1.0 / 32), (3, -32.0)):
        ms(T.dc[0:8, j:j + 1], v, ["dc"], 1)
    for c in range(NCH):
        n = str(c)
        iota(T["d3" + n][:, 0:576:3], [[0, 192]], 0, 0, ["d3z" + n], 192, True)
        ms(T["d4" + n][:, 0:256:2], 0, ["d4z" + n, "d4n" + n], 128)
    pA = T.pO1
    for j, v in ((1, RND), (2, -RND), (4, 0.0), (5, 15.5)):
        ms(pA[0:8, 288 + j:289 + j], v, ["cA"], 1, "O1")
    ms(T.a31[0:8, 0:5], -15.5, ["a31"], 8)
    ms(T.a31[0:8, 5:6], 0.0, ["a31"], 1)
    ts(T.thf[0:8, :], T.thi[0:8, :], -2048.0, None, OP.add, None, ["thi"], ["thf"], 128)

    def late_constants():
        for a, b, st_, pat, base in ((0, 128, 1, [[0, 128]], 1), (0, 128, 8, [[0, 16]], 0), (1, 128, 8, [[0, 16]], 2), (4, 128, 8, [[4080, 2], [0, 8]], -4096)):
            iota(T.du[:, a:b:st_], pat, base, 0, ["du"], (b - a) // st_, True)
        for a, m in ((0, 4096.0), (64, 16.0)):
            ms(T.du[:, a + 2:a + 64:8], 0.5 / m, ["du"], 8)
        for a, b, st_, pat, base in ((0, 192, 1, [[0, 192]], 0), (1, 64, 8, [[4080, 2], [0, 4]], -4095), (65, 192, 8, [[4080, 2], [0, 8]], -4095),
                                     (2, 192, 8, [[0, 24]], int(RND)), (3, 192, 8, [[0, 24]], -int(RND)), (4, 32, 8, [[0, 4]], -2048),
                                     (68, 128, 8, [[0, 8]], -2048), (5, 32, 8, [[0, 4]], 5280), (69, 128, 8, [[0, 8]], 5280),
                                     (36, 64, 8, [[256, 4]], 0), (132, 192, 8, [[256, 8]], 0)):
            iota(T.cu[:, a:b:st_], pat, base, 0, ["cu"], (b - a) // st_, True)
        for a, b in ((36, 64), (132, 192)):
            ts(T.cu[:, a:b:8], T.cu[:, a:b:8], pf[:, 29:30], None, OP.add, None, ["cu", "k16"], ["cu"], 8)
        cp(T.pK0[:, 256:320], T.cu[:, 0:64], ["cu"], ["cu0"], 64, 1.0, "K0")
        cp(T.pK1[:, 256:448], T.cu[:, :], ["cu"], ["cu1"], 192, 1.0, "K1")
        for j in range(4):
            gcopy(T.rbf[:, 256 * j:256 * j + 256], T.rbt[:, 256 * j:256 * j + 256], ["rbt"], ["rbf"], 256)
        for j in range(4):
            iota(T.IU[:, 1024 * j:1024 * j + 1024], [[1, 1024]], 1024 * j, 0, ["IU%d" % j], 1024, True)

    def limit():
        ts(T.thx[0:8, :], T.thf[0:8, :], T.a31[0:8, 5:6], 2047.0, OP.add, OP.min, ["thf", "a31"], ["thx"], 128, 0.5)

    nxt = T.cores[(rank + 1) % len(T.cores)]
    rid, pid = topo.addr(nxt, core)
    mask = topo.mask(core, nxt)
    pcore = T.cores[(rank - 1) % len(T.cores)]
    n_in = len(topo.engines(pcore, core))
    n_out = len(topo.engines(core, nxt))
    XW = T.X[:, 0:2064]
    XK = ["X0", "X1", "Xz"]

    def units(name, a, b):
        return ["%s_%d" % (name, j) for j in range(a // 8, b // 8)]

    def pick(c, pieces, off, okey):
        n = str(c)
        for e, a, b in pieces:
            gather(e, T["rec" + n][:, 16 * a:16 * b], XW, off(a, b), XK + [okey], units("rec" + n, a, b) + (["turnA"] if e == "a" else []), 16 * (b - a))

    def tile_of(t, c):
        if t == 0:
            return (lambda a, b: T.tile0[:, c, a:b]), "tile0_%d" % c
        return (lambda a, b: T.lnd[:, 2 * (t - 1) + c, a:b]), "lnd%d_%d" % (t, c)

    def best(c, o, oh, okey):
        n = str(c); pK = T["pK" + n]; Bk = T["Bk" + n]; kk = "key" + n
        j, other = (0, OP.max) if o == OP.min else (1, OP.min)
        scan(Bk[0:64, :], T.keepT[0:64, 0:128], pK[0:64, 0:128], OP.mult, o, [kk, "keepT"], ["Bk" + n], 128, 1.0, "K" + n)
        scan(pK[0:64, 255:127:-1], T.edge[0:64, j, :], pK[0:64, 127::-1], other, o, [kk, "edge%d" % j], ["Bs" + n], 128, 1.0, "K" + n)
        tt(oh[0:64, :], pK[0:64, 128:256], Bk[0:64, :], OP.is_equal, ["Bs" + n, "Bk" + n], [okey], 128, "K" + n)

    def begin(t, c):
        n = str(c); tl, tk = tile_of(t, c); pU = T["pU" + n]
        for s in range(3):
            nb = "P%d" % ((s + 1) % 3)
            group("U" + n, "Lp%d" % s + n, [[(pU[:, 256 + 64 * s:320 + 64 * s], mats[nb], tl(64, 128), [nb if nb != "P0" else "I", tk], 64)]])
        act(T["d3" + n][:, 2:576:3], pU[:, 256:448], AF.Identity, 3232.0, 1.0, ["Lp%d" % s + n for s in range(3)], ["d3l" + n], 192, "U" + n)

    def step(t, s, c):
        n = str(c); tl, tk = tile_of(t, c)
        pK = T["pK" + n]; pO = T["pO" + n]; pU = T["pU" + n]; pH = T["pH" + n]
        rec = T["rec" + n]; mn = T["mn" + n]; cl = T["cl" + n]; y = T["y" + n]; hi2 = T["hi" + n]
        an = T["an" + n]; eq = T["eq" + n]; so = T["so" + n]; d3 = T["d3" + n]; ib = T["i" + n]; ohT = T["ohT" + n]
        bh, bo, bu = "H" + n, "O" + n, "U" + n
        if s == 0 and t > 0:
            pick(c, CFG["G0"], lambda a, b: T.lno[:, 2 * (t - 1) + c, a:b], "lno%d_%d" % (t, c))
        else:
            pick(c, CFG["G0"] if s == 0 else CFG["GP"], lambda a, b: T["off" + n][:, a:b], "off" + n)
        hi = hi2[:, 1:128:2]
        if s == 0:
            a_ap, ak = tl(0, 64), tk
            group(bh, "aj" + n, [[(pH[:, 1:128:2], mats["Sh0"], a_ap, ["Sh0", ak], 64)]])
            tt(hi, pH[:, 1:128:2], a_ap, OP.max, ["aj" + n, ak], ["hi" + n], CW, bh)
        else:
            a_ap, ak = hi2[:, 0:128:2], "hi" + n
            group(bh, "ak" + n, [[(pH[:, 0:128:2], mats["PT%d" % s], an[:, :], ["PT%d" % s, "an" + n], 64)]])
            group(bh, "aj" + n, [[(pH[:, 1:128:2], mats["PS%d" % s], an[:, :], ["PS%d" % s, "an" + n], 64)]])
            scan(hi2[:, :], T.rs2[:, :], pH[:, 0:128], OP.add, OP.max, ["ak" + n, "aj" + n, "rs2"], ["hi" + n], 128, 1.0, bh)
        tt(eq[:, :], pH[:, 1:128:2], a_ap, OP.is_equal, ["aj" + n, ak], ["eq" + n], CW, bh)
        if s == 2:
            Cs = pH[:, 320:384]
            group(bh, "Cn" + n, [[const(Cs, 128, -8, 64), (Cs, mats["I"], tl(128, 192), ["I", tk], 64)]
                                 + [(Cs, mats["I"], y[:, r, 128:192], ["I", "yC%d" % r + n], 64) for r in range(2)]
                                 + [(Cs, mats["nSx%d" % r], y[:, r, 64 * h:64 * h + 64], ["nSx%d" % r, ("yh%d", "y%d")[h] % r + n], 64)
                                    for r in range(2) for h in range(2)]])
            act(T["Cs" + n][:, 64:128], Cs, AF.Relu, 0.0, -1.0, ["Cn" + n], ["Es" + n], CW, bh)
            act(T["Cs" + n][:, 0:64], Cs, AF.Identity, 0.0, 1.0, ["Cn" + n], ["Cs" + n], CW, bh)
        cyc = 16 if s < 2 else 8
        w_ = 16 // cyc
        for a, b in CFG["CP"]:
            tt(cl[:, w_ * a:w_ * b], rec[:, 16 * a + cyc - 1:16 * b:cyc], rec[:, 16 * a:16 * b:cyc], OP.min, units("rec" + n, a, b), units("cl" + n, a, b), w_ * (b - a))
        for a, b in CFG["SP"]:
            rk = units("rec" + n, a, b)
            scan(mn[:, 16 * a:16 * b - 1], rec[:, 16 * a:16 * b - 1], rec[:, 16 * a + 1:16 * b], OP.max, OP.min, rk, units("mn" + n, a, b), 16 * (b - a), 0.5)
        key = pK[0:64, 0:128]
        if s == 1:
            runs = [[const2(key, 64, 128, 256, "fg")], [(key, y[:, 0, 64 * h:64 * h + 64], mats["PN"], [("yh0", "y0")[h] + n, "PN"], 128) for h in range(2)]]
        else:
            runs = [[const2(key, 64, 0, 128, "ab")]]
        sums = []
        for a, b in PH:
            rk = units("rec" + n, a, b); mk = units("mn" + n, a, b); ck = units("cl" + n, a, b)
            one = []; two = []
            for p in range(16):
                k = row_of(s, p)
                for j in (k, (k - SH[s]) & 15):
                    one.append((pK[a:b, j:128:16], rec[:, 16 * a + p:16 * b:16], T.gs[:, 0:8], rk + ["G32"], b - a))
                if p % cyc == cyc - 1:
                    two.append((pK[a:b, k:128:16], cl[:, w_ * a + p // cyc:w_ * b:w_], T.gs[:, 16:24], ck + ["Gm64"], b - a))
                else:
                    two.append((pK[a:b, k:128:16], mn[:, 16 * a + p:16 * b:16], T.gs[:, 16:24], mk + ["Gm64"], b - a))
            sums.append((one, two))
        k = row_of(s, 0)
        both = (pK[0:64, k:128:16], mn[:, 0:1024:16], T.gs[:, 16:24], units("mn" + n, 0, 64) + ["Gm64"], 64)
        out = [(key, eq[:, :], mats["BI"], ["eq" + n, "BI"], 128)]
        if s == 2:
            out.append((key, T["Cs" + n][:, 64:128], mats["PE"], ["Es" + n, "PE"], 128))
        lim = [(key, T.thx[0:8, 64 * c:64 * c + 64], T.thR[0:8, :], ["thx", "thR"], 128)]
        if CFG["SM"]:
            whole = [(pK[0:64, j:128:16], rec[:, p:1024:16], T.gs[:, 0:8], units("rec" + n, 0, 64) + ["G32"], 64)
                     for p in range(16) for j in (row_of(s, p), (row_of(s, p) - SH[s]) & 15)]
            runs += [sums[0][1][1:], out, lim, whole, sums[1][1][1:] + [both]]
        else:
            runs += [sums[0][0], sums[0][1][1:], out, sums[1][0], lim, sums[1][1][1:] + [both]]
        group("K" + n, "key" + n, runs)
        best(c, OP.min, ohT, "ohT" + n)
        cs_ = [(tl(128, 192), tk)] + [(y[:, r, 128:192], "yC%d" % r + n) for r in range(s)]
        group(bo, "yP" + n, [
            [const2(pO[:, 0:192], 128, 512, 704, "cde")],
            [(pO[:, 128:192], mats["D%d" % s], d, ["D%d" % s, dk], 64) for d, dk in cs_],
            [(pO[:, 0:64], mats["I"], hi, ["I", "hi" + n], 64), (pO[:, 64:128], mats["I"], hi, ["I", "hi" + n], 64),
             (pO[:, 64:128], mats["nIS%d" % s], a_ap, ["nIS%d" % s, ak], 64)],
            [(pO[:, 0:192], ohT[0:64, :], T.IB[0:64, :], ["ohT" + n, "IB0", "IB1", "IB2"], 192)]])
        yk = "y%d" % s + n
        yh = "yh%d" % s + n
        ts(y[:, s, 0:64], pO[:, 0:64], -2048.0, None, OP.max, None, ["yP" + n], [yh], CW, 1.0, bo)
        ts(y[:, s, 64:128], pO[:, 64:128], -2048.0, None, OP.max, None, ["yP" + n], [yk], CW, 1.0, bo)
        ts(y[:, s, 128:192], pO[:, 128:192], 0.0, None, OP.min, None, ["yP" + n], ["yC%d" % s + n], CW, 1.0, bo)
        nb = (s + 1) % 3
        pn = "P%d" % nb; pk = pn if nb else "I"
        group(bu, "ua" + n, [[(pU[:, 1:192:3], mats[pn], a_ap, [pk, ak], 64)]])
        group(bu, "uw" + n, [[(pU[:, 2:192:3], mats["W%d" % nb], tl(64, 128), ["W%d" % nb, tk], 64)]])
        group(bh, "E" + n, [[(pH[:, 128:192], mats[pn], a_ap, [pk, ak], 64)],
                            [(pH[:, 128:192], mats["nG"], y[:, s, 0:64], ["nG", yh], 64)]])
        group(bu, "ud" + n, [[const(pU[:, 0:192:3], 128, -60, 64)],
                             [(pU[:, 0:192:3], mats["nG"], y[:, s, 64 * h:64 * h + 64], ["nG", yh, yk], 64) for h in range(2)]])
        ts(d3[:, 192 * s + 1:192 * s + 192:3], pH[:, 128:192], 30719.0, None, OP.is_equal, None, ["E" + n], ["e%d" % s + n], CW, 1.0, bh)
        scan(so[:, 0:192], d3[:, 192 * s:192 * s + 192], pU[:, 0:192], OP.mult, OP.add,
             ["e%d" % s + n, "d3z" + n, "d3l" + n, "ua" + n, "uw" + n, "ud" + n], ["so" + n], 192, 1.0, bu)
        if s < 2 and CFG["U16"]:
            bits(T["off" + n][:, :], so[:, 2:192:3], 5, 2047, ["so" + n], ["off" + n], CW)
        else:
            bits(ib[:, 1, :], so[:, 2:192:3], 5, 2047, ["so" + n], ["pl" + n], CW)
            if s < 2:
                cp(T["off" + n][:, :], ib[:, 1, :], ["pl" + n], ["off" + n], CW)
        (gcopy if s < CFG["GA"] else cp)(an[:, :], so[:, 1:192:3], ["so" + n], ["an" + n], CW)

    def count():
        out = pA[0:8, 288:292:3]
        runs = [[(out, mats["Ib8"], T.a31[0:8, 3:5], ["Ib", "a31"], 8)]
                + [(out, T["ohT%d" % c][0:64, k:128:16], T.keepT[0:64, 1:3], ["ohT%d" % c, "keepT"], 8) for c in range(NCH) for k in range(16)]]
        group("O1", "Ac", runs)
        scan(T.a31[0:8, 0:6], T.dc[0:8, 0:6], pA[0:8, 288:294], OP.mult, OP.add, ["Ac", "cA", "dc"], ["a31"], 5, 1.0, "O1")
        limit()

    def spot(c, z, zcol, zk):
        n = str(c); pK = T["pK" + n]; pO = T["pO" + n]; q = T["q" + n]; r5 = T["r5" + n]; ib = T["i" + n]
        bk, bo = "K" + n, "O" + n
        S = pK[:, 256:288:8]
        group(bk, "uQ" + n, [[(S, T.selw[:, 15 - r:143 - r], zcol(r), ["selw", zk], 64) for r in range(16)]])
        scan(r5[:, :], T.du[:, 0:32], pK[:, 256:288], OP.mult, OP.add, ["uQ" + n, "cu" + n, "du"], ["r5" + n], 32, 1.0, bk)
        tt(q[:, 0, :], S, r5[:, 4:32:8], OP.add, ["uQ" + n, "r5" + n], ["q0" + n], 4, bk)
        group(bo, "uP" + n, [[(pO[:, 128:192], mats["Wev"], z, ["Wev", zk], 64)]])
        tt(q[:, 1, :], S, r5[:, 5:32:8], OP.add, ["uQ" + n, "r5" + n], ["q1" + n], 4, bk)
        tt(q[:, 2, :], q[:, 0, :], q[:, 1, :], OP.mult, ["q0" + n, "q1" + n], ["q2" + n], 4)
        bits(q[:, 3, :], q[:, 2, :], 5, 1023, ["q2" + n], ["q3" + n], 4)
        cp(T["offq" + n][:, 4:8], q[:, 3, :], ["q3" + n], ["on" + n], 4)
        cp(ib[:, 0, :], pO[:, 128:192], ["uP" + n], ["u0" + n], CW, 1.0, bo)
        bits(ib[:, 3, :], ib[:, 0, :], 0, 4095, ["u0" + n], ["u" + n], CW)

    def refill(t, c):
        n = str(c); tl, tk = tile_of(t, c)
        pK = T["pK" + n]; pO = T["pO" + n]; pU = T["pU" + n]; pH = T["pH" + n]
        y = T["y" + n]; f = T["f" + n]; an = T["an" + n]; ib = T["i" + n]; so = T["so" + n]; d4 = T["d4" + n]
        Bk = T["Bk" + n]; oh2 = T["oh2" + n]; hT = T["hT" + n]; yq = T["yq" + n]; oq = T["offq" + n]
        z = T.z[:, 64 * c:64 * c + 64]; nw = T["nw" + n]; av = T.av[:, 64 * c:64 * c + 64]; r5 = T["r5" + n]

        def zcol(r):
            return T.z[:, 64 * c + r:64 * c + 64:16]
        bk, bh, bo, bu = "K" + n, "H" + n, "O" + n, "U" + n
        a_ap, ak = an[:, :], "an" + n
        cost = [(tl(128, 192), tk, "I")] + [(y[:, r, 128:192], "yC%d" % r + n, "I") for r in range(3)]
        emp = [(y[:, r, 64 * h:64 * h + 64], ("yh%d", "y%d")[h] % r + n, "nSx%d" % r) for r in range(3) for h in range(2)]
        early = [(T["Cs" + n][:, 0:64], "Cs" + n, "Ib")]; late = emp[4:6] + cost[3:4]
        key = pK[0:64, 0:128]
        group(bk, "key" + n, [[const2(key, 64, 384, 512, "hi")] + [(key, d, mats[m], [dk, m], 128) for d, dk, m in early],
                              [(key, d, mats[m], [dk, m], 128) for d, dk, m in late]])
        best(c, OP.max, oh2, "oh2" + n)
        act(hT[0:64, 0:8], Bk[0:64, 15:128:16], AF.Identity, 128.515625, 1.0 / 32, ["Bk" + n], ["hT" + n], 8)
        group(bh, "emp" + n, [[const(pH[:, 256:320], 128, -12, 64)] + [(pH[:, 256:320], mats[m], d, [dk, m], 64) for d, dk, m in emp[0:4]],
                              [(pH[:, 256:320], mats[m], d, [dk, m], 64) for d, dk, m in emp[4:6]]])
        tt(f[:, 3, :], ib[:, 1, :], pH[:, 256:320], OP.subtract, ["pl" + n, "emp" + n], ["pl2" + n], CW, bh)
        ts(T["off" + n][:, :], f[:, 3, :], 2048.0, None, OP.min, None, ["pl2" + n], ["off" + n], CW)
        group(bo, "oN" + n, [[(pO[:, 0:64], oh2[0:64, :], mats["Ib64"], ["oh2" + n, "Ib"], 64)]])
        tt(yq[:, 0, :], pO[:, 0:64], ib[:, 1, :], OP.mult, ["oN" + n, "pl" + n], ["yq" + n], CW, bo)
        tt(yq[:, 1, :], pO[:, 0:64], a_ap, OP.mult, ["oN" + n, ak], ["ya" + n], CW, bo)
        group(bo, "hP" + n, [[(pO[0:8, 192:256], hT[0:64, 0:8], mats["Ib64"], ["hT" + n, "Ib"], 64)]])
        act(hT[0:8, 64:128], pO[0:8, 192:256], AF.Identity, -1.0, 1.0, ["hP" + n], ["hB" + n], CW, bo)
        group(bu, "Qp" + n, [[(pU[:, 448:512], mats["I"], T.mk[:, :], ["I", "mk"], 64)],
                             [(pU[:, 448:512], mats["G"], yq[:, 0, :], ["G", "yq" + n], 64)]])
        scan(f[:, 4, :], T.keepT[:, 0:64], pU[:, 448:512], OP.mult, OP.max, ["Qp" + n, "keepT"], ["Qs" + n], CW, 1.0, bu)
        cp(oq[:, 0:4], f[:, 4, 15:64:16], ["Qs" + n], ["oz" + n], 4)
        gather(CFG["ZE"], z, XW, oq[:, 0:4], XK + ["oz" + n], ["z" + n], 64)
        dg = 60 + GAM * 64
        if t == 0 or not CFG["TAB"]:
            spot(c, z, zcol, "z" + n)
            body, bo_, bkeys, u, uk = T.rbf[:, 0:1024], oq[:, 4:8], ["rbf", "on" + n], ib[:, 3, :], "u" + n
        else:
            body, bo_, bkeys, u, uk = T.TB[:, 0:2048], oq[:, 0:4], ["TB0", "TB1", "oz" + n], f[:, 0, :], "f0" + n
            gather(CFG["UE"], u, T.TU[:, 0:2048], bo_, ["TU0", "TU1", "oz" + n], [uk], 64)
        Cn = pH[:, 320:384]
        group(bh, "Cn" + n, [[const(Cn, 128, -4, 64)] + [(Cn, mats[m], d, [dk, m], 64) for d, dk, m in early],
                             [(Cn, mats[m], d, [dk, m], 64) for d, dk, m in late],
                             [(Cn, oh2[0:64, :], mats["nI4k64"], ["oh2" + n, "nI4k"], 64)]])
        sx = 2 * t + c; sk = "snd%d" % sx
        sg = nw[:, 0, :]
        act(sg, Cn, AF.Sign, 8.0, 1.0, ["Cn" + n], ["nw" + n], CW, bh)
        act(nw[:, 1, :], Cn, AF.Relu, 0.0, 1.0, ["Cn" + n], ["cr" + n], CW, bh)
        ts(d4[:, 2:256:4], Cn, 0.0, None, OP.is_lt, None, ["Cn" + n], ["d4n" + n], CW, 1.0, bh)
        act(f[:, 1, :], sg, AF.Identity, -6144.0, -4096.0, ["nw" + n], ["mL" + n], CW)
        group(bu, "ud" + n, [[(pU[:, 0:256:4], T.c33[0:1, 0, :], T.c33[0:1, 0, 0:64], ["c1"], 64)]])
        group(bu, "ua" + n, [[(pU[:, 2:256:4], mats["I"], a_ap, ["I", ak], 64)]])
        group(bu, "uw" + n, [[(pU[:, 1:256:4], T.cev[0:1, :], T.c33[0:1, 0, 0:64], ["cev", "c1"], 64),
                              (pU[:, 1:256:4], mats["nI"], a_ap, ["nI", ak], 64),
                              (pU[:, 1:256:4], mats["Godd"], yq[:, 1, :], ["Godd", "ya" + n], 64)]])
        group(bu, "Lp0" + n, [[const(pU[:, 256:320], 128, -4, 64), (pU[:, 256:320], mats["I"], tl(64, 128), ["I", tk], 64),
                               (pU[:, 256:320], mats["I4k"], sg, ["I4k", "nw" + n], 64)]])
        group(bu, "Lp1" + n, [[const(pU[:, 320:384], 128, -6, 64),
                               (pU[:, 320:384], mats["nI4k"], sg, ["nI4k", "nw" + n], 64),
                               (pU[:, 320:384], T.G16[0:8, :], hT[0:8, 64:128], ["hB" + n, "G16"], 64)]])
        tt(T.snd[:, sx, 128:192], pU[:, 320:384], nw[:, 1, :], OP.max, ["Lp1" + n, "cr" + n], [sk + "c"], CW, bu)
        op("v", lambda: V.tensor_tensor(f[:, 2, :], body.indirect(bo_), f[:, 1, :], OP.add), bkeys + ["mL" + n], ["vb" + n], dg)
        op("v", lambda: V.tensor_tensor(ib[:, 2, :], body.indirect(bo_), u, OP.mult), bkeys + [uk], ["w" + n], dg)
        Ln = T.snd[:, sx, 64:128]
        tt(Ln, pU[:, 256:320], f[:, 2, :], OP.max, ["Lp0" + n, "vb" + n], [sk + "l"], CW, bu)
        if t > 0:
            ts(ib[:, 2, :], ib[:, 2, :], pf[:, 30:31], T.t32[:, 3 + t:4 + t], OP.mult, OP.add, ["w" + n, "t32", "evc"], ["w" + n], CW)
        bits(d4[:, 1:256:4], ib[:, 2, :], 5, 4095, ["w" + n], ["d4x" + n], CW)
        if t < VIS - 1:
            ts(d4[:, 3:256:4], Ln, 3232.0, None, OP.add, None, [sk + "l"], ["d4l" + n], CW)
            group(bu, "u4" + n, [[(pU[:, 3:256:4], mats["W0"], Ln, ["W0", sk + "l"], 64)]])
        scan(so[:, :], d4[:, :], pU[:, 0:256], OP.mult, OP.add,
             ["d4z" + n, "d4x" + n, "d4n" + n, "d4l" + n, "ua" + n, "uw" + n, "ud" + n, "u4" + n], ["so" + n], 256, 1.0, bu)
        if t < VIS - 1:
            bits(ib[:, 2, :], so[:, 3:256:4], 5, 2047, ["so" + n], ["w" + n], CW)
            cp(T.sno[:, sx, :], ib[:, 2, :], ["w" + n], ["sno%d" % sx], CW)
            cp(T.snd[:, sx, 0:64], so[:, 2:256:4], ["so" + n], [sk + "a"], CW)
            op("g", lambda: g.remote_dma(T.lno[:, sx, :], T.sno[:, sx, :], T.sem["aro%d" % sx], T.sem.loc, pid, rid, mask),
               ["sno%d" % sx], ["lno%d_%d" % (t + 1, c), "turn"], CFG["REM"], None, "rem", ("aro%d" % sx, n_in, n_out))
            op("g", lambda: g.remote_dma(T.lnd[:, sx, :], T.snd[:, sx, :], T.sem["art%d" % sx], T.sem.loc, pid, rid, mask),
               [sk + "a", sk + "l", sk + "c"], ["lnd%d_%d" % (t + 1, c), "turn"], CFG["REM"], None, "rem", ("art%d" % sx, n_in, n_out))
        else:
            for j, (dst, src, mul, add, k) in enumerate(((T.yc, T.snd[:, sx, 128:192], 1.0 / 16, 0.0, sk + "c"), (T.yl, Ln, 1.0, 2048.0, sk + "l"),
                                                         (T.ya, so[:, 2:256:4], 1.0, 2048.0, "so" + n))):
                ts(T.fin[:, 3 * c + j, :], src, mul, add, OP.mult, OP.add, [k], ["fin%d" % (3 * c + j)], CW)
                dma("s", dst[:, 64 * c:64 * c + 64], T.fin[:, 3 * c + j, :], ["fin%d" % (3 * c + j)], [], 2400)
        pick(c, CFG["GF"][c], lambda a, b: T["off" + n][:, a:b], "off" + n)
        rec = T["rec" + n]; mn = T["mn" + n]
        for a, b in CFG["TS"][c]:
            scan(mn[:, 16 * a:16 * b], T.keepT[:, 0:16 * (b - a)], rec[:, 16 * a:16 * b], OP.mult, OP.max, units("rec" + n, a, b) + ["keepT", "keepW"], units("mn" + n, a, b), 16 * (b - a), 0.5)
        group(bh, "zt" + n, [[(pH[:, 192:256], mats["Ib"], z, ["Ib", "z" + n], 64)],
                             [(pH[:, 192:256], mats["Ib"], mn[:, 15:1024:16], ["Ib"] + units("mn" + n, 0, 64), 64)]])
        avi = T.avi[:, 64 * c:64 * c + 64]
        ts(avi, pH[:, 192:256], 0.5, -0.25, OP.mult, OP.add, ["zt" + n], ["avi" + n], CW, 1.0, bh)
        if t == VIS - 1:
            S = pK[:, 288:320:8]; a, b = 4 * c, 4 * c + 4; k = "Xo" + n
            group(bk, "uW" + n, [[(S, T.selw[:, 15 - r:143 - r], zcol(r), ["selw", "z" + n], 64) for r in range(16)]])
            scan(r5[:, :], T.du[:, 64:96], pK[:, 288:320], OP.mult, OP.add, ["uW" + n, "cu" + n, "du"], ["r5" + n], 32, 1.0, bk)
            tt(T.qw[:, a:b], S, r5[:, 4:32:8], OP.add, ["uW" + n, "r5" + n], ["q5" + n], 4, bk)
            cp(T.ow[:, a:b], T.qw[:, a:b], ["q5" + n], ["ow" + n], 4)
            op("v", lambda: V.tensor_copy(T.Xo[:, 1024 * c:1024 * c + 1024].indirect(T.ow[:, a:b]), avi), ["ow" + n, "avi" + n, k], [k], 60 + 3.8 * 64)
            dma("s" if c == 0 else "a", T.yx[:, 1024 * c:1024 * c + 1024], T.Xo[:, 1024 * c:1024 * c + 1024], [k], [], 3000)

    def scatter(tab_, k, src, skeys):
        op("v", lambda: V.tensor_copy(tab_[:, 0:2048].indirect(T.ow[:, 0:8]), src), ["ow0", "ow1"] + skeys, [k + "0", k + "1"], 60 + 3.8 * 128)

    def write():
        pK = T.pK1; S = pK[:, 384:448:8]
        group("K1", "uW", [[(S, T.selw[:, 15 - r:143 - r], T.z[:, r:128:16], ["selw", "z0", "z1"], 64) for r in range(16)]])
        scan(T.rw[:, :], T.du[:, 64:128], pK[:, 384:448], OP.mult, OP.add, ["uW", "cu1", "du"], ["rw"], 64, 1.0, "K1")
        tt(T.qw[:, :], S, T.rw[:, 4:64:8], OP.add, ["uW", "rw"], ["q50", "q51"], 8, "K1")
        cp(T.ow[:, :], T.qw[:, :], ["q50", "q51"], ["ow0", "ow1"], 8)
        for c in range(NCH):
            op("v", lambda c=c: V.tensor_copy(T.X[:, 0:2048].indirect(T.ow[:, 4 * c:4 * c + 4]), T.avi[:, 64 * c:64 * c + 64]),
               ["ow0", "avi%d" % c], ["X0", "X1"], 60 + 3.8 * 64)

    def renew():
        pK = T.pK1; S = pK[:, 320:384:8]; q = T.qn
        gcopy(T.av[:, :], T.avi[:, :], ["avi0", "avi1"], ["av0", "av1"], 128)
        group("K1", "uN", [[(S, T.selw[:, 15 - r:143 - r], T.av[:, r:128:16], ["selw", "av0", "av1"], 64) for r in range(16)]])
        scan(T.rw[:, :], T.du[:, 0:64], pK[:, 320:384], OP.mult, OP.add, ["uN", "cu1", "du"], ["rw"], 64, 1.0, "K1")
        tt(q[:, 0, :], S, T.rw[:, 4:64:8], OP.add, ["uN", "rw"], ["qn0"], 8, "K1")
        tt(q[:, 1, :], S, T.rw[:, 5:64:8], OP.add, ["uN", "rw"], ["qn1"], 8, "K1")
        ts(T.on[:, 0:8], q[:, 0, :], 2048.0, None, OP.add, None, ["qn0"], ["onu"], 8)
        tt(q[:, 2, :], q[:, 0, :], q[:, 1, :], OP.mult, ["qn0", "qn1"], ["qn2"], 8)
        bits(q[:, 3, :], q[:, 2, :], 5, 1023, ["qn2"], ["qn3"], 8)
        cp(T.on[:, 8:16], q[:, 3, :], ["qn3"], ["onb"], 8)
        gather("a", T.nv[:, 0, :], T.IU[:, 0:4096], T.on[:, 0:8], ["IU0", "IU1", "IU2", "IU3", "onu"], ["nv0"], 128)
        gather("a", T.nv[:, 1, :], T.rbf[:, 0:1024], T.on[:, 8:16], ["rbf", "onb"], ["nv1"], 128)
        scatter(T.TU, "TU", T.nv[:, 0, :], ["nv0"])
        scatter(T.TB, "TB", T.nv[:, 1, :], ["nv1"])

    def tables():
        pO = T.pO0; w = T.tw
        group("O0", "uT", [[(pO[:, 256:384], T.selw[:, 15 - r:143 - r], T.X[:, r:2048:16], ["selw", "X0", "X1"], 128) for r in range(16)]])
        cp(w[:, 0, :], pO[:, 256:384], ["uT"], ["tw0"], 128, 1.0, "O0")
        bits(w[:, 1, :], w[:, 0, :], 0, 4095, ["tw0"], ["tw1"], 128)
        cp(T.to[:, 0, :], w[:, 1, :], ["tw1"], ["to0"], 128)
        ts(w[:, 0, :], w[:, 1, :], -2048.0, None, OP.add, None, ["tw1"], ["tw0"], 128)
        ts(w[:, 2, :], w[:, 1, :], 3232.0, None, OP.add, None, ["tw1"], ["tw2"], 128)
        tt(w[:, 1, :], w[:, 0, :], w[:, 2, :], OP.mult, ["tw0", "tw2"], ["tw1"], 128)
        bits(w[:, 0, :], w[:, 1, :], 5, 1023, ["tw1"], ["tw0"], 128)
        cp(T.to[:, 1, :], w[:, 0, :], ["tw0"], ["to1"], 128)
        m = CFG["TP"]
        for j in range(0, 128, m):
            k = "%d" % (j // 64)
            gather("a", T.TU[:, 16 * j:16 * (j + m)], T.IU[:, 0:4096], T.to[:, 0, j:j + m], ["IU0", "IU1", "IU2", "IU3", "to0"], ["TU" + k], 16 * m)
            gather("a", T.TB[:, 16 * j:16 * (j + m)], T.rbf[:, 0:1024], T.to[:, 1, j:j + m], ["rbf", "to1"], ["TB" + k], 16 * m)

    limit()
    for c in range(NCH):
        n = str(c); tl, tk = tile_of(0, c); f = T["f" + n]; ib = T["i" + n]; cs_ = slice(64 * c, 64 * c + 64)
        d4 = T["d4" + n]; so = T["so" + n]
        ts(so[:, 0:128:2], T.agi[:, cs_], -2048.0, None, OP.add, None, ["agi"], ["so" + n], CW)
        ts(d4[:, 1:128:2], T.lti[:, cs_], 1184.0, None, OP.add, None, ["lti"], ["d4x" + n, "d4l" + n], CW)
        ts(so[:, 1:128:2], T.lti[:, cs_], -2048.0, 2080.0, OP.add, OP.mult, ["lti"], ["sw" + n], CW)
        scan(T.tw[:, c, :], d4[:, 0:128], so[:, 0:128], OP.mult, OP.add, ["so" + n, "sw" + n, "d4x" + n, "d4z" + n], ["tw" + n], 128)
        bits(ib[:, 1, :], T.tw[:, c, 1:128:2], 5, 2047, ["tw" + n], ["pl" + n], CW)
        cp(T["off" + n][:, :], ib[:, 1, :], ["pl" + n], ["off" + n], CW)
        ts(tl(0, 64), T.agi[:, cs_], -2048.0, None, OP.add, None, ["agi"], [tk + "a"], CW)
        ts(tl(64, 128), T.lti[:, cs_], -2048.0, None, OP.add, None, ["lti"], [tk + "l"], CW)
        ts(tl(128, 192), T.csi[:, cs_], 16.0, None, OP.mult, None, ["csi", tk + "l", tk + "a"], [tk], CW)
    for t in range(VIS):
        for c in range(NCH):
            phase(begin, "b%d" % c, t, c)
        if t == VIS - 1:
            at[0] = "copy"
            for c in range(NCH):
                dma("s", T.Xo[:, 1024 * c:1024 * c + 1024], T.X[:, 1024 * c:1024 * c + 1024], ["X%d" % c], ["Xo%d" % c], 3000)
        for s in range(3):
            for c in range(NCH):
                phase(step, "s%d%d" % (s, c), t, s, c)
            if not (t == VIS - 1 and s == 2):
                phase(count, "c%d" % s)
            if t == 0 and s == 0:
                phase(late_constants, "late")
                if CFG["TAB"]:
                    phase(tables, "tab")
            if t > 0 and s == CFG["RS"] and CFG["TAB"]:
                phase(renew, "new")
        for c in range(NCH):
            phase(refill, "r%d%d" % (c, t == 0 and CFG["TAB"]), t, c)
        if t < VIS - 1:
            phase(write, "w")
    return ops


def schedule(ops):
    n = len(ops)
    LAT, FAC = CFG["LAT"], CFG["FAC"]
    lastw = {}; readers = {}; lastb = {}
    deps = []
    for i, o in enumerate(ops):
        dep = {}
        for k in o["r"]:
            if k in lastw:
                dep[lastw[k]] = "raw"
        for k in o["w"]:
            if k in lastw:
                dep.setdefault(lastw[k], "ord" if o["kind"] == "mm" or k.startswith("turn") else "raw")
            for j in readers.get(k, ()):
                if j != i:
                    dep.setdefault(j, "raw")
        if o["bank"]:
            for e, j in lastb.get(o["bank"], {}).items():
                dep.setdefault(j, "ord")
            lastb.setdefault(o["bank"], {})[o["e"]] = i
        for k in o["r"]:
            readers.setdefault(k, []).append(i)
        for k in o["w"]:
            lastw[k] = i; readers[k] = []
        deps.append(dep)

    def waits(i, j):
        return ops[j]["e"] != ops[i]["e"] or deps[i][j] == "raw"

    succ = [[] for _ in range(n)]
    for i in range(n):
        for j in deps[i]:
            succ[j].append(i)
    dur = [o["d"] * (FAC if o["kind"] in ("c", "mm") else 1.0) for o in ops]
    occ = [{"dma": 80.0, "rem": 500.0}.get(o["kind"], dur[i]) for i, o in enumerate(ops)]

    def gap(i, j):
        if not waits(i, j):
            return occ[j]
        return dur[j] + (CFG["LATS"] if ops[i]["e"] == ops[j]["e"] else LAT)

    fwd = [[(j, gap(i, j)) for j in deps[i]] for i in range(n)]
    bwd = [[(k, occ[k] - occ[j] + gap(k, j)) for k in succ[j]] for j in range(n)]

    def place(seq, edges, first):
        st = [0.0] * n
        line = {e: [] for e in "vapgs"}
        for i in seq:
            t = max([first[i]] + [st[j] + w for j, w in edges[i]])
            lst = line[ops[i]["e"]]
            lo, hi = 0, len(lst)
            while lo < hi:
                mid = (lo + hi) // 2
                if lst[mid][1] <= t:
                    lo = mid + 1
                else:
                    hi = mid
            while lo < len(lst) and lst[lo][0] < t + occ[i]:
                t = max(t, lst[lo][1]); lo += 1
            lst.insert(lo, (t, t + occ[i]))
            st[i] = t
        return st

    tail = [dur[i] + (CFG["LAG"] if o["kind"] == "dma" and o["r"] and o["r"][0] in ("fin0", "fin1", "fin2", "Xo0") else 0.0)
            for i, o in enumerate(ops)]
    pr = [0.0] * n
    for i in range(n - 1, -1, -1):
        pr[i] = max([tail[i]] + [pr[k] + gap(k, i) for k in succ[i]])
    seq = sorted(range(n), key=lambda i: (-pr[i], i))
    found = None
    x = 1
    for _ in range(CFG["PASSES"]):
        st = place(seq, fwd, [0.0] * n)
        total = max(st[i] + tail[i] for i in range(n))
        if found is None or total < found[0]:
            found = (total, st)
        st = found[1]
        back = place(sorted(range(n), key=lambda i: (-st[i] - occ[i], -i)), bwd, [tail[i] - occ[i] for i in range(n)])
        key = [0.0] * n
        for i in range(n):
            x = (x * 1103515245 + 12345) & 0x7FFFFFFF
            key[i] = max([CFG["JIT"] * x / 2.0 ** 31 - back[i] - occ[i]] + [key[j] for j in deps[i]])
        seq = sorted(range(n), key=lambda i: (key[i], i))
    slow = [o["d"] * (1.0 if o["kind"] in ("dma", "rem") else CFG["FAC2"] * (CFG["GX2"] if o["ext"] == "pick" else CFG["PX2"] if o["kind"] == "mm" else 1.0)) for o in ops]
    eng = [o["e"] for o in ops]
    hold = [occ[i] if o["kind"] in ("dma", "rem") else slow[i] for i, o in enumerate(ops)]
    edge2 = [[(j, slow[j] + gap(i, j) - dur[j]) for j in deps[i] if waits(i, j)] for i in range(n)]

    def cost(st):
        s2 = [0.0] * n; free = {e: 0.0 for e in "vapgs"}; last = 0.0
        for i in sorted(range(n), key=lambda i: (st[i], i)):
            t = free[eng[i]]
            for j, w in edge2[i]:
                if s2[j] + w > t:
                    t = s2[j] + w
            s2[i] = t; free[eng[i]] = t + hold[i]
            last = max(last, t + slow[i])
        return max(st[i] + dur[i] for i in range(n)) + CFG["W2"] * last

    st = found[1]
    kinds = {}
    for i, o in enumerate(ops):
        kinds.setdefault(o["cls"], []).append(i)
    names = [k for k in kinds if k[0] not in ("start", "late")]
    low = cost(st)
    zero = [0.0] * n
    for _ in range(CFG["MOVES"]):
        key = list(st)
        for _k in range(CFG["MK"]):
            x = (x * 1103515245 + 12345) & 0x7FFFFFFF
            by = ((x >> 4 & 1023) - 512) * CFG["BY"]
            for i in kinds[names[(x >> 14) % len(names)]]:
                key[i] += by
        for i in range(n):
            for j in deps[i]:
                if key[j] > key[i]:
                    key[i] = key[j]
        new = place(sorted(range(n), key=lambda i: (key[i], i)), fwd, zero)
        c = cost(new)
        if c <= low:
            low, st = c, new
    end = [st[i] + dur[i] for i in range(n)]
    order = sorted(range(n), key=lambda i: (st[i], i))
    pos = {}; cnt = {e: 0 for e in "vapgs"}
    know = {e: ({x: -1 for x in "vapg"}, set()) for e in "vapgs"}
    snap = {}; wait = {}
    for i in order:
        o = ops[i]; e = o["e"]
        kc, kd = know[e]
        need = []
        for j in sorted((j for j in deps[i] if waits(i, j)), key=lambda j: -end[j]):
            a = ops[j]
            if a["kind"] in ("dma", "rem"):
                if j in kd:
                    continue
                kd.add(j)
            else:
                if kc[a["e"]] >= pos[j]:
                    continue
                kc[a["e"]] = pos[j]
            need.append(j)
            if a["kind"] != "rem":
                sc, sd = snap[j]
                for x in sc:
                    kc[x] = max(kc[x], sc[x])
                kd.update(sd)
        wait[i] = need
        if o["kind"] not in ("dma", "rem"):
            pos[i] = cnt[e]; cnt[e] += 1
        snap[i] = (dict(kc), set(kd))
    return order, wait, max(end)


PLAN = {}


def rank_program(g, core, T, topo):
    rank = T.rank_of(core)
    if rank is None:
        return
    ops = build_ops(g, core, T, topo, rank)
    if "plan" not in PLAN:
        PLAN["plan"] = schedule(ops)
    order, wait, _ = PLAN["plan"]
    Q = {"v": g.vector, "a": g.scalar, "p": g.tensor, "g": g, "s": g.sync}
    wanted = set()
    for i in order:
        wanted.update(wait[i])
    sig = {}; cnt = {e: 0 for e in "vapg"}; nd = [0]; open_d = []; sent = 0
    for i in order:
        o = ops[i]; q = Q[o["e"]]
        for j in wait[i]:
            q.wait_ge(sig[j][0], sig[j][1])
        ins = o["fn"]()
        if o["kind"] == "dma":
            s = T.sem["d%d" % nd[0]]; nd[0] += 1
            ins.then_inc(s, 16)
            sig[i] = (s, 16)
            if i not in wanted:
                open_d.append((o["e"], s))
        elif o["kind"] == "rem":
            name, n_in, n_out = o["ext"]
            sig[i] = (T.sem[name], n_in)
            sent += n_out
        elif i in wanted:
            cnt[o["e"]] += 1
            s = T.sem["s" + o["e"]]
            ins.then_inc(s, 1)
            sig[i] = (s, cnt[o["e"]])
    g.wait_ge(T.sem.loc, sent)
    for e, s in open_d:
        Q[e].wait_ge(s, 16)
